import numpy as np
import ml_dtypes


def mxq(x, axis, fmt="e4m3"):
    dtype, down = {"e4m3": (ml_dtypes.float8_e4m3fn, 7), "e5m2": (ml_dtypes.float8_e5m2, 14)}[fmt]
    v = np.moveaxis(np.asarray(x, np.float32).astype(ml_dtypes.bfloat16).astype(np.float64), axis, -1)
    blocks = v.reshape(v.shape[:-1] + (-1, 32))
    amax = np.abs(blocks).max(-1, keepdims=True)
    byte = np.maximum(np.where(amax > 0, np.frexp(amax)[1] - 1 + 127, 0) - down, 1)
    scale = np.exp2(byte - 127.0)
    codes = (blocks / scale).astype(np.float32).astype(dtype).astype(np.float64)
    return np.moveaxis((codes * scale).reshape(v.shape), -1, axis)


WIDE = False


def mx_kscale(k):
    if not WIDE:
        return np.ones(k)
    levels = np.array([10, -10, 5, -5, 0])
    if k % 512:
        return np.exp2(np.random.permutation(np.resize(levels, k // 32))).repeat(32)
    a = np.empty((k // 512, 16))
    for p in range(k // 512):
        a[p, :8] = np.random.permutation(np.resize(levels, 8))
        for g in range(8):
            far = levels[np.abs(levels - a[p, g]) >= 10]
            a[p, g + 8] = far[np.random.randint(len(far))]
    return np.exp2(a.ravel()).repeat(32)


def f64(x):
    return np.asarray(x).astype(np.float64)


def striped(idx):
    return np.tile(idx.reshape(-1, 16).T, (8, 1)).astype(np.uint16)


def unstriped(offs):
    return offs[:16].T.reshape(-1).astype(np.int64)


E2M1 = np.array([0.0, 0.5, 1.0, 1.5, 2.0, 3.0, 4.0, 6.0, -0.0, -0.5, -1.0, -1.5, -2.0, -3.0, -4.0, -6.0])


def pack_weight(w, fmt):
    k, n = w.shape
    w = f64(np.asarray(w, np.float32).astype(ml_dtypes.bfloat16)).reshape(k // 32, 32, n)
    amax = np.abs(w).max(1)
    if fmt == "e4m3":
        byte = np.frexp(amax)[1] - 1 + 127 - 7
    else:
        mant, ex = np.frexp(amax / 6.0)
        byte = np.where(mant > 0.5, ex, ex - 1) + 127
    byte = np.clip(np.where(amax > 0, byte, 1), 1, 254)
    scaled = (w * np.exp2(127.0 - byte)[:, None, :]).reshape(k, n).astype(np.float32)
    by_word = np.ascontiguousarray(scaled.reshape(k // 512, 128, 4, n).transpose(0, 1, 3, 2))
    if fmt == "e4m3":
        words = by_word.astype(ml_dtypes.float8_e4m3fn).view(np.uint8)
    else:
        c = by_word.astype(ml_dtypes.float4_e2m1fn).view(np.uint8) & 0xF
        words = (c[..., 0::2] | (c[..., 1::2] << 4)).reshape(k // 512, 128, 2 * n)
    return np.ascontiguousarray(words), np.ascontiguousarray(byte.astype(np.uint8).reshape(k // 512, 16, n))


def unpack_weight(words, scales, fmt):
    g, _, n = scales.shape
    words = np.ascontiguousarray(words).reshape(g, 128, n, -1)
    if fmt == "e4m3":
        vals = words.view(ml_dtypes.float8_e4m3fn).astype(np.float64)
    else:
        nib = np.empty((g, 128, n, 4), np.uint8)
        nib[..., 0::2] = words & 0xF
        nib[..., 1::2] = words >> 4
        vals = E2M1[nib]
    vals = vals * np.repeat(np.exp2(scales.astype(np.float64) - 127.0), 8, axis=1)[..., None]
    return vals.transpose(0, 1, 3, 2).reshape(g * 512, n)


def gelu(v):
    return 0.5 * v * (1.0 + np.tanh(np.sqrt(2.0 / np.pi) * (v + 0.044715 * v**3)))


K, T, S, P, H, N = 1024, 4096, 1024, 512, 1024, 512

def setup_inputs():
    n = np.random.standard_normal
    s = mx_kscale(K)[:, None]
    u = mx_kscale(H)[:, None]
    tab_words, tab_scales = pack_weight(n((K, T)) * np.exp(0.4 * n((1, T))) * s, "e4m3")
    w4_words, w4_scales = pack_weight(n((K, H)) / np.sqrt(K) / s * u.T, "e2m1")
    w2 = n((H, N)) / np.sqrt(H) / u
    eps = 0.5 * np.exp(0.3 * n(H)) * u[:, 0] * u[:, 0]
    return {
        "tab_words": tab_words, "tab_scales": tab_scales,
        "offs": striped(np.random.permutation(T)[:S]),
        "w4_words": w4_words, "w4_scales": w4_scales,
        "pos1": striped(np.random.permutation(S)[:P]),
        "pos2": striped(np.random.permutation(S)[:P]),
        "pos3": striped(np.random.permutation(S)[:P]),
        "eps": eps.astype(np.float32),
        "w2": w2.astype(np.float32),
    }

def reference(tab_words, tab_scales, offs, w4_words, w4_scales, pos1, pos2, pos3, eps, w2):
    v = unpack_weight(tab_words, tab_scales, "e4m3")[:, unstriped(offs)]
    w4 = unpack_weight(w4_words, w4_scales, "e2m1")
    h = w4.T @ v
    e = h * h
    e3 = e[:, unstriped(pos1)] + e[:, unstriped(pos2)] + e[:, unstriped(pos3)]
    z = np.sqrt(e3 + f64(eps)[:, None])
    y = mxq(f64(w2), 0, "e4m3").T @ mxq(z, 0, "e4m3")
    return y / (1.0 + np.exp(-y))

@@ -1,0 +1,212 @@
+from contextlib import ExitStack
+
+import concourse.mybir as mybir
+
+K, T, S, M, H, N = 1024, 4096, 1024, 512, 1024, 512
+FLOPS = 2 * K * H * S + 2 * H * N * M
+
+F32 = mybir.dt.float32
+BF16 = mybir.dt.bfloat16
+I32 = mybir.dt.int32
+U32 = mybir.dt.uint32
+U16 = mybir.dt.uint16
+U8 = mybir.dt.uint8
+FP8X4 = mybir.dt.float8_e4m3fn_x4
+FP4X4 = mybir.dt.float4_e2m1fn_x4
+ACT = mybir.ActivationFunctionType
+ADD = mybir.AluOpType.add
+
+P = 128
+PACK = 4
+HALF = 512
+
+
+def tile_list_choir_blend_features_kernel(
+    tc, tab_words, tab_scales, offs, w4_words, w4_scales, pos1, pos2, pos3, eps, w2, out
+):
+    nc = tc.nc
+    with ExitStack() as ctx:
+        lists = ctx.enter_context(tc.tile_pool(name="lists", bufs=1))
+        keep = ctx.enter_context(tc.tile_pool(name="keep", bufs=1))
+        big = ctx.enter_context(tc.tile_pool(name="big", bufs=2))
+        ring = ctx.enter_context(tc.tile_pool(name="ring", bufs=4))
+        psum = ctx.enter_context(tc.psum_pool(name="psum", bufs=1))
+
+        offs_sb = lists.tile([P, S // 16], U16, name="offs_sb")
+        pos_sb = [lists.tile([P, M // 16], U16, name="pos%d_sb" % i) for i in range(3)]
+
+        tsc = keep.tile([P, T], U8, name="tsc", align_bytes=64)
+        nc.vector.memset(tsc[:].bitcast(I32), 0)
+        wsc_raw = keep.tile([P, 2, H], U8, name="wsc_raw", align_bytes=64)
+        nc.gpsimd.memset(wsc_raw[:].bitcast(I32), 0)
+        vsc = keep.tile([P, 2, S], U8, name="vsc", align_bytes=64)
+        nc.vector.memset(vsc[:].bitcast(I32), 0)
+
+        nc.sync.dma_start(offs_sb[:], offs)
+        nc.scalar.dma_start(tsc[0:P:4, :].bitcast(I32), tab_scales.rearrange("a q t -> (a q) t").bitcast(I32))
+        for q in range(4):
+            nc.gpsimd.dma_start(
+                wsc_raw[32 * q : 32 * q + 4, :, :].bitcast(I32),
+                w4_scales[:, 4 * q : 4 * q + 4, :].rearrange("a r c -> r a c").bitcast(I32),
+            )
+        w4_raw = keep.tile([P, 2, 2 * H], U8, name="w4_raw", align_bytes=64)
+        nc.sync.dma_start(w4_raw[:].bitcast(I32), w4_words.rearrange("a p c -> p a c").bitcast(I32))
+        words = [big.tile([P, T], I32, name="words%d" % a, tag="big", align_bytes=64) for a in range(2)]
+        nc.sync.dma_start(words[0][:], tab_words[0].rearrange("p t i -> p (t i)").bitcast(I32))
+        for sb, src in zip(pos_sb, (pos1, pos2, pos3)):
+            nc.sync.dma_start(sb[:], src)
+        nc.sync.dma_start(words[1][:], tab_words[1].rearrange("p t i -> p (t i)").bitcast(I32))
+        eps_sb = keep.tile([P, 2, PACK], F32, name="eps_sb")
+        nc.gpsimd.dma_start(eps_sb[:], eps.rearrange("(b p t) -> p b t", p=P, t=PACK))
+
+        gsc = keep.tile([P, S], U8, name="gsc", align_bytes=64)
+        nc.vector.tensor_copy(gsc[:], tsc[:].indirect(offs_sb[:]))
+        for a in range(2):
+            for q in range(4):
+                eng = nc.scalar if 4 * a + q < 6 else nc.gpsimd
+                first = 4 * (16 * a + 4 * q)
+                eng.dma_start(vsc[32 * q : 32 * q + 4, a, :].bitcast(I32), gsc[first : first + 16 : 4, :].bitcast(I32))
+
+        w4 = keep.tile([P, 2, 2 * H], U8, name="w4", align_bytes=64)
+        wsc = keep.tile([P, 2, H], U8, name="wsc", align_bytes=64)
+        for a in range(2):
+            nc.vector.tensor_copy(
+                w4[:, a, :].bitcast(U16).rearrange("p (b t m) -> p b t m", b=2, t=PACK),
+                w4_raw[:, a, :].bitcast(U16).rearrange("p (b m t) -> p b t m", b=2, t=PACK),
+            )
+            nc.vector.tensor_copy(
+                wsc[:, a, :].rearrange("p (b t m) -> p b t m", b=2, t=PACK),
+                wsc_raw[:, a, :].rearrange("p (b m t) -> p b t m", b=2, t=PACK),
+            )
+
+        eps_wide = keep.tile([P, 2 * PACK, M], F32, name="eps_wide")
+        for b in range(2):
+            nc.scalar.copy(
+                eps_wide[:, PACK * b : PACK * (b + 1), :],
+                eps_sb[:, b, :].unsqueeze(2).to_broadcast([P, PACK, M]),
+            )
+
+        v = {}
+        for a in range(2):
+            for h in range(2):
+                v[a, h] = keep.tile([P, HALF], U32, name="v%d%d" % (a, h), align_bytes=64)
+                nc.vector.tensor_copy(
+                    v[a, h][:], words[a][:].bitcast(U32).indirect(offs_sb[:, 32 * h : 32 * (h + 1)])
+                )
+
+        sq = [keep.tile([P, S], F32, name="sq%d" % j) for j in range(8)]
+        acc = {}
+
+        def mm1(j, h, a):
+            if a == 0:
+                acc[j, h] = psum.tile([P, HALF], F32, name="acc%d%d" % (j, h), tag="bank%d" % (2 * (j % 4) + h))
+            nc.tensor.matmul_mx(
+                out=acc[j, h][:],
+                lhsT=w4[:, a, 2 * P * j : 2 * P * (j + 1)].bitcast(FP4X4),
+                lhsT_scale=wsc[:, a, P * j : P * (j + 1)],
+                rhs=v[a, h][:].bitcast(FP8X4),
+                rhs_scale=vsc[:, a, HALF * h : HALF * (h + 1)],
+                start=(a == 0),
+                stop=(a == 1),
+            )
+
+        def square(j, h):
+            nc.scalar.activation(sq[j][:, HALF * h : HALF * (h + 1)], acc[j, h][:], ACT.Square)
+
+        for h in range(2):
+            for j in range(4):
+                mm1(j, h, 0)
+        for pair in (0, 2):
+            for h in range(2):
+                for j in (pair, pair + 1):
+                    mm1(j, h, 1)
+                    square(j, h)
+        for j in range(4, 8):
+            for h in range(2):
+                mm1(j, h, 0)
+                mm1(j, h, 1)
+                square(j, h)
+
+        w2_codes, w2_sc = [], []
+        w2_bf = []
+        for b in range(2):
+            raw = big.tile([P, PACK, N], F32, name="w2raw%d" % b, tag="big", align_bytes=64)
+            nc.sync.dma_start(raw[:], w2[HALF * b : HALF * (b + 1), :].rearrange("(p t) n -> p t n", t=PACK))
+            bf = keep.tile([P, N, PACK], BF16, name="w2bf%d" % b, align_bytes=64)
+            for n in range(4):
+                cols = slice(P * n, P * (n + 1))
+                nc.scalar.copy(bf[:, cols, :], raw[:, :, cols].rearrange("p t n -> p n t"))
+            w2_bf.append(bf)
+            w2_codes.append(keep.tile([P, N], U32, name="w2c%d" % b, align_bytes=64))
+            w2_sc.append(keep.tile([P, N], U8, name="w2s%d" % b, align_bytes=64))
+
+        def quant_w2(b):
+            nc.vector.quantize_mx(
+                out=w2_codes[b][:].bitcast(FP8X4), scales=w2_sc[b][:], in_=w2_bf[b][:].rearrange("p n t -> p (n t)")
+            )
+
+        def gathers(b, m0, width):
+            total = keep.tile([P, PACK, width], F32, name="total%d_%d" % (b, m0))
+            cols = slice(m0 // 16, (m0 + width) // 16)
+            for pair in (0, 2):
+                prev = [eps_wide[:, PACK * b + t, 0:width] for t in (pair, pair + 1)]
+                for i in range(3):
+                    for u, t in enumerate((pair, pair + 1)):
+                        if i < 2:
+                            part = ring.tile([P, width], F32, name="part", tag="part")
+                            dst = part[:]
+                        else:
+                            dst = total[:, t, :]
+                        nc.vector.tensor_tensor(dst, sq[PACK * b + t][:].indirect(pos_sb[i][:, cols]), prev[u], ADD)
+                        prev[u] = dst
+            return total
+
+        def root(b, m0, width, total):
+            zb = keep.tile([P, width, PACK], BF16, name="zb%d_%d" % (b, m0), align_bytes=64)
+            nc.scalar.activation(zb[:], total[:].rearrange("p t m -> p m t"), ACT.Sqrt)
+            return zb
+
+        def quant_z(b, m0, width, zb):
+            codes = keep.tile([P, width], U32, name="zc%d_%d" % (b, m0), align_bytes=64)
+            sc = keep.tile([P, width], U8, name="zs%d_%d" % (b, m0), align_bytes=64)
+            nc.vector.quantize_mx(out=codes[:].bitcast(FP8X4), scales=sc[:], in_=zb[:].rearrange("p m t -> p (m t)"))
+            return codes, sc
+
+        W = M // 2
+        y = {}
+
+        def mm2(n, c, b, codes, sc):
+            if b == 0:
+                y[n, c] = psum.tile([P, W], F32, name="y%d%d" % (n, c), tag="bank%d" % (4 * c + n))
+            nc.tensor.matmul_mx(
+                out=y[n, c][:],
+                lhsT=w2_codes[b][:, P * n : P * (n + 1)].bitcast(FP8X4),
+                lhsT_scale=w2_sc[b][:, P * n : P * (n + 1)],
+                rhs=codes.bitcast(FP8X4),
+                rhs_scale=sc,
+                start=(b == 0),
+                stop=(b == 1),
+            )
+
+        def finish(c, zb):
+            codes, sc = quant_z(1, W * c, W, zb)
+            for n in range(4):
+                mm2(n, c, 1, codes[:], sc[:])
+                res = keep.tile([P, W], F32, name="res%d%d" % (n, c))
+                nc.scalar.activation(res[:], y[n, c][:], ACT.Silu)
+                nc.sync.dma_start(out[P * n : P * (n + 1), W * c : W * (c + 1)], res[:])
+
+        total0 = gathers(0, 0, M)
+        zb0 = root(0, 0, M, total0)
+        total_a = gathers(1, 0, W)
+        quant_w2(0)
+        quant_w2(1)
+        codes0, sc0 = quant_z(0, 0, M, zb0)
+        for c in range(2):
+            for n in range(4):
+                mm2(n, c, 0, codes0[:, W * c : W * (c + 1)], sc0[:, W * c : W * (c + 1)])
+        zb_a = root(1, 0, W, total_a)
+        finish(0, zb_a)
+        total_b = gathers(1, W, W)
+        zb_b = root(1, W, W, total_b)
+        finish(1, zb_b)

@@ -35,9 +35,9 @@ def tile_list_choir_blend_features_kernel(
         offs_sb = lists.tile([P, S // 16], U16, name="offs_sb")
         pos_sb = [lists.tile([P, M // 16], U16, name="pos%d_sb" % i) for i in range(3)]
 
-        tsc = keep.tile([P, T], U8, name="tsc", align_bytes=64)
+        tsc = keep.tile([P, T], U8, name="tsc", tag="tsc", align_bytes=64)
         nc.vector.memset(tsc[:].bitcast(I32), 0)
-        wsc_raw = keep.tile([P, 2, H], U8, name="wsc_raw", align_bytes=64)
+        wsc_raw = keep.tile([P, 2, H], U8, name="wsc_raw", tag="wsc_raw", align_bytes=64)
         nc.gpsimd.memset(wsc_raw[:].bitcast(I32), 0)
         vsc = keep.tile([P, 2, S], U8, name="vsc", align_bytes=64)
         nc.vector.memset(vsc[:].bitcast(I32), 0)
@@ -51,14 +51,21 @@ def tile_list_choir_blend_features_kernel(
             )
         w4_raw = keep.tile([P, 2, 2 * H], U8, name="w4_raw", align_bytes=64)
         nc.sync.dma_start(w4_raw[:].bitcast(I32), w4_words.rearrange("a p c -> p a c").bitcast(I32))
-        words = [big.tile([P, T], I32, name="words%d" % a, tag="big", align_bytes=64) for a in range(2)]
+        words = [big.tile([P, T], I32, name="words0", tag="big", align_bytes=64)]
         nc.sync.dma_start(words[0][:], tab_words[0].rearrange("p t i -> p (t i)").bitcast(I32))
         for sb, src in zip(pos_sb, (pos1, pos2, pos3)):
             nc.sync.dma_start(sb[:], src)
+        words.append(big.tile([P, T], I32, name="words1", tag="big", align_bytes=64))
         nc.sync.dma_start(words[1][:], tab_words[1].rearrange("p t i -> p (t i)").bitcast(I32))
         eps_sb = keep.tile([P, 2, PACK], F32, name="eps_sb")
         nc.gpsimd.dma_start(eps_sb[:], eps.rearrange("(b p t) -> p b t", p=P, t=PACK))
 
+        w4 = keep.tile([P, 2, 2 * H], U8, name="w4", align_bytes=64)
+        for a in range(2):
+            nc.vector.tensor_copy(
+                w4[:, a, :].bitcast(U16).rearrange("p (b t m) -> p b t m", b=2, t=PACK),
+                w4_raw[:, a, :].bitcast(U16).rearrange("p (b m t) -> p b t m", b=2, t=PACK),
+            )
         gsc = keep.tile([P, S], U8, name="gsc", align_bytes=64)
         nc.vector.tensor_copy(gsc[:], tsc[:].indirect(offs_sb[:]))
         for a in range(2):
@@ -67,13 +74,8 @@ def tile_list_choir_blend_features_kernel(
                 first = 4 * (16 * a + 4 * q)
                 eng.dma_start(vsc[32 * q : 32 * q + 4, a, :].bitcast(I32), gsc[first : first + 16 : 4, :].bitcast(I32))
 
-        w4 = keep.tile([P, 2, 2 * H], U8, name="w4", align_bytes=64)
-        wsc = keep.tile([P, 2, H], U8, name="wsc", align_bytes=64)
+        wsc = keep.tile([P, 2, H], U8, name="wsc", tag="tsc", align_bytes=64)
         for a in range(2):
-            nc.vector.tensor_copy(
-                w4[:, a, :].bitcast(U16).rearrange("p (b t m) -> p b t m", b=2, t=PACK),
-                w4_raw[:, a, :].bitcast(U16).rearrange("p (b m t) -> p b t m", b=2, t=PACK),
-            )
             nc.vector.tensor_copy(
                 wsc[:, a, :].rearrange("p (b t m) -> p b t m", b=2, t=PACK),
                 wsc_raw[:, a, :].rearrange("p (b m t) -> p b t m", b=2, t=PACK),
@@ -86,13 +88,13 @@ def tile_list_choir_blend_features_kernel(
                 eps_sb[:, b, :].unsqueeze(2).to_broadcast([P, PACK, M]),
             )
 
-        v = {}
-        for a in range(2):
-            for h in range(2):
-                v[a, h] = keep.tile([P, HALF], U32, name="v%d%d" % (a, h), align_bytes=64)
-                nc.vector.tensor_copy(
-                    v[a, h][:], words[a][:].bitcast(U32).indirect(offs_sb[:, 32 * h : 32 * (h + 1)])
-                )
+        v0 = keep.tile([P, S], U32, name="v0", tag="wsc_raw", align_bytes=64)
+        nc.vector.tensor_copy(v0[:], words[0][:].bitcast(U32).indirect(offs_sb[:]))
+        v = {(0, h): v0[:, HALF * h : HALF * (h + 1)] for h in range(2)}
+        for h in range(2):
+            v1 = keep.tile([P, HALF], U32, name="v1%d" % h, align_bytes=64)
+            nc.vector.tensor_copy(v1[:], words[1][:].bitcast(U32).indirect(offs_sb[:, 32 * h : 32 * (h + 1)]))
+            v[1, h] = v1[:]
 
         sq = [keep.tile([P, S], F32, name="sq%d" % j) for j in range(8)]
         acc = {}
@@ -104,7 +106,7 @@ def tile_list_choir_blend_features_kernel(
                 out=acc[j, h][:],
                 lhsT=w4[:, a, 2 * P * j : 2 * P * (j + 1)].bitcast(FP4X4),
                 lhsT_scale=wsc[:, a, P * j : P * (j + 1)],
-                rhs=v[a, h][:].bitcast(FP8X4),
+                rhs=v[a, h].bitcast(FP8X4),
                 rhs_scale=vsc[:, a, HALF * h : HALF * (h + 1)],
                 start=(a == 0),
                 stop=(a == 1),
@@ -114,14 +116,13 @@ def tile_list_choir_blend_features_kernel(
             nc.scalar.activation(sq[j][:, HALF * h : HALF * (h + 1)], acc[j, h][:], ACT.Square)
 
         for h in range(2):
-            for j in range(4):
+            for j in range(2):
                 mm1(j, h, 0)
-        for pair in (0, 2):
-            for h in range(2):
-                for j in (pair, pair + 1):
-                    mm1(j, h, 1)
-                    square(j, h)
-        for j in range(4, 8):
+        for h in range(2):
+            for j in range(2):
+                mm1(j, h, 1)
+                square(j, h)
+        for j in range(2, 8):
             for h in range(2):
                 mm1(j, h, 0)
                 mm1(j, h, 1)
@@ -146,7 +147,7 @@ def tile_list_choir_blend_features_kernel(
             )
 
         def gathers(b, m0, width):
-            total = keep.tile([P, PACK, width], F32, name="total%d_%d" % (b, m0))
+            total = keep.tile([P, PACK, width], F32, name="total%d_%d" % (b, m0), align_bytes=64)
             cols = slice(m0 // 16, (m0 + width) // 16)
             for pair in (0, 2):
                 prev = [eps_wide[:, PACK * b + t, 0:width] for t in (pair, pair + 1)]
@@ -162,7 +163,7 @@ def tile_list_choir_blend_features_kernel(
             return total
 
         def root(b, m0, width, total):
-            zb = keep.tile([P, width, PACK], BF16, name="zb%d_%d" % (b, m0), align_bytes=64)
+            zb = keep.tile([P, width, PACK], BF16, name="zb%d_%d" % (b, m0), tag="held" if (b, m0) == (1, 0) else "zb%d_%d" % (b, m0), align_bytes=64)
             nc.scalar.activation(zb[:], total[:].rearrange("p t m -> p m t"), ACT.Sqrt)
             return zb
 
@@ -207,6 +208,19 @@ def tile_list_choir_blend_features_kernel(
                 mm2(n, c, 0, codes0[:, W * c : W * (c + 1)], sc0[:, W * c : W * (c + 1)])
         zb_a = root(1, 0, W, total_a)
         finish(0, zb_a)
-        total_b = gathers(1, W, W)
-        zb_b = root(1, W, W, total_b)
+        prev = [eps_wide[:, PACK + t, 0:W] for t in range(PACK)]
+        first_sum = keep.tile([P, PACK, W], F32, name="first_sum")
+        second_sum = keep.tile([P, PACK, W], F32, name="second_sum", tag="held", align_bytes=64)
+        for i, sums in enumerate((first_sum, second_sum)):
+            for t in range(PACK):
+                nc.vector.tensor_tensor(sums[:, t, :], sq[PACK + t][:].indirect(pos_sb[i][:, W // 16 : M // 16]), prev[t], ADD)
+                prev[t] = sums[:, t, :]
+        zb_b = keep.tile([P, W, PACK], BF16, name="zb_b", align_bytes=64)
+        Q = W // 2
+        for u in range(2):
+            total = keep.tile([P, PACK, Q], F32, name="total_q%d" % u)
+            cols = slice((W + Q * u) // 16, (W + Q * (u + 1)) // 16)
+            for t in range(PACK):
+                nc.vector.tensor_tensor(total[:, t, :], sq[PACK + t][:].indirect(pos_sb[2][:, cols]), prev[t][:, Q * u : Q * (u + 1)], ADD)
+            nc.scalar.activation(zb_b[:, Q * u : Q * (u + 1), :], total[:].rearrange("p t m -> p m t"), ACT.Sqrt)
         finish(1, zb_b)

@@ -49,37 +49,51 @@ def tile_list_choir_blend_features_kernel(
                 wsc_raw[32 * q : 32 * q + 4, :, :].bitcast(I32),
                 w4_scales[:, 4 * q : 4 * q + 4, :].rearrange("a r c -> r a c").bitcast(I32),
             )
-        w4_raw = keep.tile([P, 2, 2 * H], U8, name="w4_raw", align_bytes=64)
-        nc.sync.dma_start(w4_raw[:].bitcast(I32), w4_words.rearrange("a p c -> p a c").bitcast(I32))
+        w4, wsc = [], []
+
+        def load_w4(b):
+            pool, tag = ((big, "big"), (keep, "gsc"))[b]
+            raw = pool.tile([P, 2, 2 * HALF], U8, name="w4_raw%d" % b, tag=tag, align_bytes=64)
+            src = w4_words[:, :, 2 * HALF * b : 2 * HALF * (b + 1)].rearrange("a p c -> p a c")
+            nc.sync.dma_start(raw[:].bitcast(I32), src.bitcast(I32))
+            return raw
+
+        def order_words(b, raw):
+            w4.append(keep.tile([P, 2, 2 * HALF], U8, name="w4_%d" % b, align_bytes=64))
+            nc.vector.tensor_copy(
+                w4[b][:].bitcast(U16).rearrange("p a (t m) -> p a t m", t=PACK),
+                raw[:].bitcast(U16).rearrange("p a (m t) -> p a t m", t=PACK),
+            )
+
+        def order_scales(b):
+            wsc.append(keep.tile([P, 2, HALF], U8, name="wsc%d" % b, align_bytes=64))
+            nc.vector.tensor_copy(
+                wsc[b][:].rearrange("p a (t m) -> p a t m", t=PACK),
+                wsc_raw[:, :, HALF * b : HALF * (b + 1)].rearrange("p a (m t) -> p a t m", t=PACK),
+            )
+
+        w4_raw0 = load_w4(0)
         words = [big.tile([P, T], I32, name="words0", tag="big", align_bytes=64)]
         nc.sync.dma_start(words[0][:], tab_words[0].rearrange("p t i -> p (t i)").bitcast(I32))
         for sb, src in zip(pos_sb, (pos1, pos2, pos3)):
             nc.sync.dma_start(sb[:], src)
+        eps_sb = keep.tile([P, 2, PACK], F32, name="eps_sb")
+        nc.sync.dma_start(eps_sb[:], eps.rearrange("(b p t) -> p b t", p=P, t=PACK))
+
+        order_words(0, w4_raw0)
         words.append(big.tile([P, T], I32, name="words1", tag="big", align_bytes=64))
         nc.sync.dma_start(words[1][:], tab_words[1].rearrange("p t i -> p (t i)").bitcast(I32))
-        eps_sb = keep.tile([P, 2, PACK], F32, name="eps_sb")
-        nc.gpsimd.dma_start(eps_sb[:], eps.rearrange("(b p t) -> p b t", p=P, t=PACK))
-
-        w4 = keep.tile([P, 2, 2 * H], U8, name="w4", align_bytes=64)
-        for a in range(2):
-            nc.vector.tensor_copy(
-                w4[:, a, :].bitcast(U16).rearrange("p (b t m) -> p b t m", b=2, t=PACK),
-                w4_raw[:, a, :].bitcast(U16).rearrange("p (b m t) -> p b t m", b=2, t=PACK),
-            )
-        gsc = keep.tile([P, S], U8, name="gsc", align_bytes=64)
+        gsc = keep.tile([P, S], U8, name="gsc", tag="gsc", align_bytes=64)
         nc.vector.tensor_copy(gsc[:], tsc[:].indirect(offs_sb[:]))
         for a in range(2):
             for q in range(4):
-                eng = nc.scalar if 4 * a + q < 6 else nc.gpsimd
+                eng = nc.scalar if 4 * a + q < 7 else nc.gpsimd
                 first = 4 * (16 * a + 4 * q)
                 eng.dma_start(vsc[32 * q : 32 * q + 4, a, :].bitcast(I32), gsc[first : first + 16 : 4, :].bitcast(I32))
 
-        wsc = keep.tile([P, 2, H], U8, name="wsc", tag="tsc", align_bytes=64)
-        for a in range(2):
-            nc.vector.tensor_copy(
-                wsc[:, a, :].rearrange("p (b t m) -> p b t m", b=2, t=PACK),
-                wsc_raw[:, a, :].rearrange("p (b m t) -> p b t m", b=2, t=PACK),
-            )
+        w4_raw1 = load_w4(1)
+        order_scales(0)
+        order_scales(1)
 
         eps_wide = keep.tile([P, 2 * PACK, M], F32, name="eps_wide")
         for b in range(2):
@@ -88,13 +102,14 @@ def tile_list_choir_blend_features_kernel(
                 eps_sb[:, b, :].unsqueeze(2).to_broadcast([P, PACK, M]),
             )
 
-        v0 = keep.tile([P, S], U32, name="v0", tag="wsc_raw", align_bytes=64)
+        v0 = keep.tile([P, S], U32, name="v0", tag="tsc", align_bytes=64)
         nc.vector.tensor_copy(v0[:], words[0][:].bitcast(U32).indirect(offs_sb[:]))
         v = {(0, h): v0[:, HALF * h : HALF * (h + 1)] for h in range(2)}
         for h in range(2):
-            v1 = keep.tile([P, HALF], U32, name="v1%d" % h, align_bytes=64)
+            v1 = keep.tile([P, HALF], U32, name="v1%d" % h, tag=("wsc_raw", "v11")[h], align_bytes=64)
             nc.vector.tensor_copy(v1[:], words[1][:].bitcast(U32).indirect(offs_sb[:, 32 * h : 32 * (h + 1)]))
             v[1, h] = v1[:]
+        order_words(1, w4_raw1)
 
         sq = [keep.tile([P, S], F32, name="sq%d" % j) for j in range(8)]
         acc = {}
@@ -104,8 +119,8 @@ def tile_list_choir_blend_features_kernel(
                 acc[j, h] = psum.tile([P, HALF], F32, name="acc%d%d" % (j, h), tag="bank%d" % (2 * (j % 4) + h))
             nc.tensor.matmul_mx(
                 out=acc[j, h][:],
-                lhsT=w4[:, a, 2 * P * j : 2 * P * (j + 1)].bitcast(FP4X4),
-                lhsT_scale=wsc[:, a, P * j : P * (j + 1)],
+                lhsT=w4[j // 4][:, a, 2 * P * (j % 4) : 2 * P * (j % 4 + 1)].bitcast(FP4X4),
+                lhsT_scale=wsc[j // 4][:, a, P * (j % 4) : P * (j % 4 + 1)],
                 rhs=v[a, h].bitcast(FP8X4),
                 rhs_scale=vsc[:, a, HALF * h : HALF * (h + 1)],
                 start=(a == 0),

@@ -18,7 +18,14 @@ ADD = mybir.AluOpType.add
 
 P = 128
 PACK = 4
-HALF = 512
+PASS = P * PACK
+BANK = 512
+PER_COLUMN = 16
+QUADRANT = 32
+SPREAD = 4
+FIRST_PART = 3 * T // 8
+BEATS_HALF = M // 2
+BEATS_QUARTER = M // 4
 
 
 def tile_list_choir_blend_features_kernel(
@@ -28,214 +35,229 @@ def tile_list_choir_blend_features_kernel(
     with ExitStack() as ctx:
         lists = ctx.enter_context(tc.tile_pool(name="lists", bufs=1))
         keep = ctx.enter_context(tc.tile_pool(name="keep", bufs=1))
-        big = ctx.enter_context(tc.tile_pool(name="big", bufs=2))
-        ring = ctx.enter_context(tc.tile_pool(name="ring", bufs=4))
+        partial = ctx.enter_context(tc.tile_pool(name="partial", bufs=4))
         psum = ctx.enter_context(tc.psum_pool(name="psum", bufs=1))
 
-        offs_sb = lists.tile([P, S // 16], U16, name="offs_sb")
-        pos_sb = [lists.tile([P, M // 16], U16, name="pos%d_sb" % i) for i in range(3)]
+        offs_sb = lists.tile([P, S // PER_COLUMN], U16, name="offs_sb")
+        pos_sb = [lists.tile([P, M // PER_COLUMN], U16, name="pos%d_sb" % i) for i in range(3)]
 
-        tsc = keep.tile([P, T], U8, name="tsc", tag="tsc", align_bytes=64)
-        nc.vector.memset(tsc[:].bitcast(I32), 0)
-        wsc_raw = keep.tile([P, 2, H], U8, name="wsc_raw", tag="wsc_raw", align_bytes=64)
-        nc.gpsimd.memset(wsc_raw[:].bitcast(I32), 0)
-        vsc = keep.tile([P, 2, S], U8, name="vsc", align_bytes=64)
-        nc.vector.memset(vsc[:].bitcast(I32), 0)
+        tab_scale_rows = keep.tile([P, T], U8, name="tab_scale_rows", tag="scale_window", align_bytes=64)
+        w4_planes_raw = keep.tile([P, 2, H], U8, name="w4_planes_raw", align_bytes=64)
+        nc.vector.memset(tab_scale_rows[:].bitcast(I32), 0)
+        nc.vector.memset(w4_planes_raw[:].bitcast(I32), 0)
+        v_planes = keep.tile([P, 2, S], U8, name="v_planes", align_bytes=64)
+        nc.gpsimd.memset(v_planes[:].bitcast(I32), 0)
 
-        nc.sync.dma_start(offs_sb[:], offs)
-        nc.scalar.dma_start(tsc[0:P:4, :].bitcast(I32), tab_scales.rearrange("a q t -> (a q) t").bitcast(I32))
-        for q in range(4):
-            nc.gpsimd.dma_start(
-                wsc_raw[32 * q : 32 * q + 4, :, :].bitcast(I32),
-                w4_scales[:, 4 * q : 4 * q + 4, :].rearrange("a r c -> r a c").bitcast(I32),
-            )
-        w4, wsc = [], []
+        w4_codes, w4_planes = [], []
 
-        def load_w4(b):
-            pool, tag = ((big, "big"), (keep, "gsc"))[b]
-            raw = pool.tile([P, 2, 2 * HALF], U8, name="w4_raw%d" % b, tag=tag, align_bytes=64)
-            src = w4_words[:, :, 2 * HALF * b : 2 * HALF * (b + 1)].rearrange("a p c -> p a c")
+        def load_w4_words(b, tag):
+            raw = keep.tile([P, 2, 2 * PASS], U8, name="w4_raw%d" % b, tag=tag, align_bytes=64)
+            src = w4_words[:, :, 2 * PASS * b : 2 * PASS * (b + 1)].rearrange("a p c -> p a c")
             nc.sync.dma_start(raw[:].bitcast(I32), src.bitcast(I32))
             return raw
 
-        def order_words(b, raw):
-            w4.append(keep.tile([P, 2, 2 * HALF], U8, name="w4_%d" % b, align_bytes=64))
+        def permute_w4_words(b, raw, tag):
+            w4_codes.append(keep.tile([P, 2, 2 * PASS], U8, name="w4_codes%d" % b, tag=tag, align_bytes=64))
             nc.vector.tensor_copy(
-                w4[b][:].bitcast(U16).rearrange("p a (t m) -> p a t m", t=PACK),
+                w4_codes[b][:].bitcast(U16).rearrange("p a (t m) -> p a t m", t=PACK),
                 raw[:].bitcast(U16).rearrange("p a (m t) -> p a t m", t=PACK),
             )
 
-        def order_scales(b):
-            wsc.append(keep.tile([P, 2, HALF], U8, name="wsc%d" % b, align_bytes=64))
+        def permute_w4_planes(b):
+            w4_planes.append(keep.tile([P, 2, PASS], U8, name="w4_planes%d" % b, align_bytes=64))
             nc.vector.tensor_copy(
-                wsc[b][:].rearrange("p a (t m) -> p a t m", t=PACK),
-                wsc_raw[:, :, HALF * b : HALF * (b + 1)].rearrange("p a (m t) -> p a t m", t=PACK),
+                w4_planes[b][:].rearrange("p a (t m) -> p a t m", t=PACK),
+                w4_planes_raw[:, :, PASS * b : PASS * (b + 1)].rearrange("p a (m t) -> p a t m", t=PACK),
             )
 
-        w4_raw0 = load_w4(0)
-        words = [big.tile([P, T], I32, name="words0", tag="big", align_bytes=64)]
-        nc.sync.dma_start(words[0][:], tab_words[0].rearrange("p t i -> p (t i)").bitcast(I32))
-        for sb, src in zip(pos_sb, (pos1, pos2, pos3)):
-            nc.sync.dma_start(sb[:], src)
+        tab = [tab_words[a].rearrange("p t i -> p (t i)").bitcast(I32) for a in range(2)]
+        words0 = keep.tile([P, T], I32, name="words0", align_bytes=64)
+        nc.sync.dma_start(offs_sb[:], offs)
+        w4_raw0 = load_w4_words(0, "words1")
+        nc.sync.dma_start(words0[:, 0:FIRST_PART], tab[0][:, 0:FIRST_PART])
+        nc.scalar.dma_start(
+            tab_scale_rows[0:P:SPREAD, :].bitcast(I32), tab_scales.rearrange("a q t -> (a q) t").bitcast(I32)
+        )
         eps_sb = keep.tile([P, 2, PACK], F32, name="eps_sb")
-        nc.sync.dma_start(eps_sb[:], eps.rearrange("(b p t) -> p b t", p=P, t=PACK))
-
-        order_words(0, w4_raw0)
-        words.append(big.tile([P, T], I32, name="words1", tag="big", align_bytes=64))
-        nc.sync.dma_start(words[1][:], tab_words[1].rearrange("p t i -> p (t i)").bitcast(I32))
-        gsc = keep.tile([P, S], U8, name="gsc", tag="gsc", align_bytes=64)
-        nc.vector.tensor_copy(gsc[:], tsc[:].indirect(offs_sb[:]))
-        for a in range(2):
-            for q in range(4):
-                eng = nc.scalar if 4 * a + q < 7 else nc.gpsimd
-                first = 4 * (16 * a + 4 * q)
-                eng.dma_start(vsc[32 * q : 32 * q + 4, a, :].bitcast(I32), gsc[first : first + 16 : 4, :].bitcast(I32))
-
-        w4_raw1 = load_w4(1)
-        order_scales(0)
-        order_scales(1)
-
-        eps_wide = keep.tile([P, 2 * PACK, M], F32, name="eps_wide")
-        for b in range(2):
-            nc.scalar.copy(
-                eps_wide[:, PACK * b : PACK * (b + 1), :],
-                eps_sb[:, b, :].unsqueeze(2).to_broadcast([P, PACK, M]),
+        nc.gpsimd.dma_start(eps_sb[:], eps.rearrange("(b p t) -> p b t", p=P, t=PACK))
+        nc.sync.dma_start(pos_sb[0][:], pos1)
+        nc.sync.dma_start(pos_sb[1][:], pos2)
+        nc.sync.dma_start(words0[:, FIRST_PART:T], tab[0][:, FIRST_PART:T])
+        nc.sync.dma_start(pos_sb[2][:], pos3)
+        for quad in range(4):
+            nc.scalar.dma_start(
+                w4_planes_raw[QUADRANT * quad : QUADRANT * quad + 4, :, :].bitcast(I32),
+                w4_scales[:, 4 * quad : 4 * quad + 4, :].rearrange("a r c -> r a c").bitcast(I32),
             )
+        permute_w4_words(0, w4_raw0, "w4_codes0")
+        words1 = keep.tile([P, T], I32, name="words1", tag="words1", align_bytes=64)
+        nc.sync.dma_start(words1[:], tab[1])
 
-        v0 = keep.tile([P, S], U32, name="v0", tag="tsc", align_bytes=64)
-        nc.vector.tensor_copy(v0[:], words[0][:].bitcast(U32).indirect(offs_sb[:]))
-        v = {(0, h): v0[:, HALF * h : HALF * (h + 1)] for h in range(2)}
-        for h in range(2):
-            v1 = keep.tile([P, HALF], U32, name="v1%d" % h, tag=("wsc_raw", "v11")[h], align_bytes=64)
-            nc.vector.tensor_copy(v1[:], words[1][:].bitcast(U32).indirect(offs_sb[:, 32 * h : 32 * (h + 1)]))
-            v[1, h] = v1[:]
-        order_words(1, w4_raw1)
+        picked_scales = keep.tile([P, S], U8, name="picked_scales", tag="picked_scales", align_bytes=64)
+        nc.vector.tensor_copy(picked_scales[:], tab_scale_rows[:].indirect(offs_sb[:]))
+        move_queues = [[nc.sync] * 4, [nc.scalar] * 3 + [nc.gpsimd]]
+        for a in range(2):
+            for quad in range(4):
+                first = SPREAD * (16 * a + 4 * quad)
+                move_queues[a][quad].dma_start(
+                    v_planes[QUADRANT * quad : QUADRANT * quad + 4, a, :].bitcast(I32),
+                    picked_scales[first : first + 4 * SPREAD : SPREAD, :].bitcast(I32),
+                )
+        w4_raw1 = load_w4_words(1, "picked_scales")
 
-        sq = [keep.tile([P, S], F32, name="sq%d" % j) for j in range(8)]
-        acc = {}
+        eps_wide = []
 
-        def mm1(j, h, a):
+        def spread_eps(b, tag):
+            eps_wide.append(keep.tile([P, PACK, M], F32, name="eps_wide%d" % b, tag=tag, align_bytes=64))
+            nc.scalar.copy(eps_wide[b][:], eps_sb[:, b, :].unsqueeze(2).to_broadcast([P, PACK, M]))
+
+        spread_eps(0, "scale_window")
+
+        v_pass0 = keep.tile([P, S], U32, name="v_pass0", tag="v_pass0", align_bytes=64)
+        nc.vector.tensor_copy(v_pass0[:], words0[:].bitcast(U32).indirect(offs_sb[:]))
+        permute_w4_planes(0)
+        v_codes = {(0, half): v_pass0[:, BANK * half : BANK * (half + 1)] for half in range(2)}
+        for half in range(2):
+            v_pass1 = keep.tile([P, BANK], U32, name="v_pass1_%d" % half, tag="v_pass1_%d" % half, align_bytes=64)
+            entries = slice(BANK * half // PER_COLUMN, BANK * (half + 1) // PER_COLUMN)
+            nc.vector.tensor_copy(v_pass1[:], words1[:].bitcast(U32).indirect(offs_sb[:, entries]))
+            v_codes[1, half] = v_pass1[:]
+        permute_w4_words(1, w4_raw1, "words1")
+        permute_w4_planes(1)
+
+        squares = [keep.tile([P, S], F32, name="squares%d" % j) for j in range(2 * PACK)]
+        h_banks = {}
+
+        def first_product(j, half, a):
+            b, t = divmod(j, PACK)
             if a == 0:
-                acc[j, h] = psum.tile([P, HALF], F32, name="acc%d%d" % (j, h), tag="bank%d" % (2 * (j % 4) + h))
+                h_banks[j, half] = psum.tile([P, BANK], F32, name="h%d_%d" % (j, half), tag="bank%d" % (2 * t + half))
             nc.tensor.matmul_mx(
-                out=acc[j, h][:],
-                lhsT=w4[j // 4][:, a, 2 * P * (j % 4) : 2 * P * (j % 4 + 1)].bitcast(FP4X4),
-                lhsT_scale=wsc[j // 4][:, a, P * (j % 4) : P * (j % 4 + 1)],
-                rhs=v[a, h].bitcast(FP8X4),
-                rhs_scale=vsc[:, a, HALF * h : HALF * (h + 1)],
+                out=h_banks[j, half][:],
+                lhsT=w4_codes[b][:, a, 2 * P * t : 2 * P * (t + 1)].bitcast(FP4X4),
+                lhsT_scale=w4_planes[b][:, a, P * t : P * (t + 1)],
+                rhs=v_codes[a, half].bitcast(FP8X4),
+                rhs_scale=v_planes[:, a, BANK * half : BANK * (half + 1)],
                 start=(a == 0),
                 stop=(a == 1),
             )
+            if a == 1:
+                nc.scalar.activation(squares[j][:, BANK * half : BANK * (half + 1)], h_banks[j, half][:], ACT.Square)
 
-        def square(j, h):
-            nc.scalar.activation(sq[j][:, HALF * h : HALF * (h + 1)], acc[j, h][:], ACT.Square)
+        first_product(0, 0, 0)
+        first_product(0, 1, 0)
+        first_product(0, 0, 1)
+        first_product(1, 0, 0)
+        first_product(0, 1, 1)
+        first_product(1, 0, 1)
+        first_product(1, 1, 0)
+        first_product(1, 1, 1)
+        for j in range(2, 2 * PACK):
+            for half in range(2):
+                for a in range(2):
+                    first_product(j, half, a)
 
-        for h in range(2):
-            for j in range(2):
-                mm1(j, h, 0)
-        for h in range(2):
-            for j in range(2):
-                mm1(j, h, 1)
-                square(j, h)
-        for j in range(2, 8):
-            for h in range(2):
-                mm1(j, h, 0)
-                mm1(j, h, 1)
-                square(j, h)
+        spread_eps(1, "v_pass1_0")
 
-        w2_codes, w2_sc = [], []
-        w2_bf = []
-        for b in range(2):
-            raw = big.tile([P, PACK, N], F32, name="w2raw%d" % b, tag="big", align_bytes=64)
-            nc.sync.dma_start(raw[:], w2[HALF * b : HALF * (b + 1), :].rearrange("(p t) n -> p t n", t=PACK))
-            bf = keep.tile([P, N, PACK], BF16, name="w2bf%d" % b, align_bytes=64)
-            for n in range(4):
+        w2_raw = keep.tile([P, 2, PACK, N], F32, name="w2_raw", tag="picked_scales", align_bytes=64)
+        w2_rounded, w2_codes, w2_planes = [], [], []
+        for b, tag in enumerate(("v_pass0", "v_pass1_1")):
+            raw = w2_raw[:, b, :, :]
+            nc.sync.dma_start(raw, w2[PASS * b : PASS * (b + 1), :].rearrange("(p t) n -> p t n", t=PACK))
+            rounded = keep.tile([P, N, PACK], BF16, name="w2_rounded%d" % b, tag=tag, align_bytes=64)
+            for n in range(N // P):
                 cols = slice(P * n, P * (n + 1))
-                nc.scalar.copy(bf[:, cols, :], raw[:, :, cols].rearrange("p t n -> p n t"))
-            w2_bf.append(bf)
-            w2_codes.append(keep.tile([P, N], U32, name="w2c%d" % b, align_bytes=64))
-            w2_sc.append(keep.tile([P, N], U8, name="w2s%d" % b, align_bytes=64))
+                nc.scalar.copy(rounded[:, cols, :], raw[:, :, cols].rearrange("p t n -> p n t"))
+            w2_rounded.append(rounded)
+            w2_codes.append(keep.tile([P, N], U32, name="w2_codes%d" % b, align_bytes=64))
+            w2_planes.append(keep.tile([P, N], U8, name="w2_plane%d" % b, align_bytes=64))
 
-        def quant_w2(b):
-            nc.vector.quantize_mx(
-                out=w2_codes[b][:].bitcast(FP8X4), scales=w2_sc[b][:], in_=w2_bf[b][:].rearrange("p n t -> p (n t)")
-            )
+        def pick_and_add(dst, b, t, i, beats, so_far):
+            entries = slice(beats.start // PER_COLUMN, beats.stop // PER_COLUMN)
+            nc.vector.tensor_tensor(dst, squares[PACK * b + t][:].indirect(pos_sb[i][:, entries]), so_far, ADD)
 
-        def gathers(b, m0, width):
-            total = keep.tile([P, PACK, width], F32, name="total%d_%d" % (b, m0), align_bytes=64)
-            cols = slice(m0 // 16, (m0 + width) // 16)
-            for pair in (0, 2):
-                prev = [eps_wide[:, PACK * b + t, 0:width] for t in (pair, pair + 1)]
+        def sum_of_picks(b, width):
+            total = keep.tile([P, PACK, width], F32, name="total%d" % b, align_bytes=64)
+            for pair in ((0, 1), (2, 3)):
+                so_far = {t: eps_wide[b][:, t, 0:width] for t in pair}
                 for i in range(3):
-                    for u, t in enumerate((pair, pair + 1)):
+                    for t in pair:
                         if i < 2:
-                            part = ring.tile([P, width], F32, name="part", tag="part")
+                            part = partial.tile([P, width], F32, name="part", tag="part")
                             dst = part[:]
                         else:
                             dst = total[:, t, :]
-                        nc.vector.tensor_tensor(dst, sq[PACK * b + t][:].indirect(pos_sb[i][:, cols]), prev[u], ADD)
-                        prev[u] = dst
+                        pick_and_add(dst, b, t, i, slice(0, width), so_far[t])
+                        so_far[t] = dst
             return total
 
-        def root(b, m0, width, total):
-            zb = keep.tile([P, width, PACK], BF16, name="zb%d_%d" % (b, m0), tag="held" if (b, m0) == (1, 0) else "zb%d_%d" % (b, m0), align_bytes=64)
-            nc.scalar.activation(zb[:], total[:].rearrange("p t m -> p m t"), ACT.Sqrt)
-            return zb
+        def root(dst, total):
+            nc.scalar.activation(dst, total[:].rearrange("p t m -> p m t"), ACT.Sqrt)
 
-        def quant_z(b, m0, width, zb):
-            codes = keep.tile([P, width], U32, name="zc%d_%d" % (b, m0), align_bytes=64)
-            sc = keep.tile([P, width], U8, name="zs%d_%d" % (b, m0), align_bytes=64)
-            nc.vector.quantize_mx(out=codes[:].bitcast(FP8X4), scales=sc[:], in_=zb[:].rearrange("p m t -> p (m t)"))
-            return codes, sc
+        def quantise_z(name, z):
+            width = z.shape[1]
+            codes = keep.tile([P, width], U32, name="z_codes_" + name, align_bytes=64)
+            plane = keep.tile([P, width], U8, name="z_plane_" + name, align_bytes=64)
+            nc.vector.quantize_mx(out=codes[:].bitcast(FP8X4), scales=plane[:], in_=z[:].rearrange("p m t -> p (m t)"))
+            return codes, plane
 
-        W = M // 2
-        y = {}
+        y_banks = {}
 
-        def mm2(n, c, b, codes, sc):
+        def second_product(n, half, b, codes, plane):
             if b == 0:
-                y[n, c] = psum.tile([P, W], F32, name="y%d%d" % (n, c), tag="bank%d" % (4 * c + n))
+                y_banks[n, half] = psum.tile(
+                    [P, BEATS_HALF], F32, name="y%d_%d" % (n, half), tag="bank%d" % (4 * half + n)
+                )
             nc.tensor.matmul_mx(
-                out=y[n, c][:],
+                out=y_banks[n, half][:],
                 lhsT=w2_codes[b][:, P * n : P * (n + 1)].bitcast(FP8X4),
-                lhsT_scale=w2_sc[b][:, P * n : P * (n + 1)],
+                lhsT_scale=w2_planes[b][:, P * n : P * (n + 1)],
                 rhs=codes.bitcast(FP8X4),
-                rhs_scale=sc,
+                rhs_scale=plane,
                 start=(b == 0),
                 stop=(b == 1),
             )
 
-        def finish(c, zb):
-            codes, sc = quant_z(1, W * c, W, zb)
-            for n in range(4):
-                mm2(n, c, 1, codes[:], sc[:])
-                res = keep.tile([P, W], F32, name="res%d%d" % (n, c))
-                nc.scalar.activation(res[:], y[n, c][:], ACT.Silu)
-                nc.sync.dma_start(out[P * n : P * (n + 1), W * c : W * (c + 1)], res[:])
+        def finish(half, z):
+            codes, plane = quantise_z("pass1_%d" % half, z)
+            for n in range(N // P):
+                second_product(n, half, 1, codes[:], plane[:])
+                result = keep.tile([P, BEATS_HALF], F32, name="result%d_%d" % (n, half))
+                nc.scalar.activation(result[:], y_banks[n, half][:], ACT.Silu)
+                nc.sync.dma_start(out[P * n : P * (n + 1), BEATS_HALF * half : BEATS_HALF * (half + 1)], result[:])
 
-        total0 = gathers(0, 0, M)
-        zb0 = root(0, 0, M, total0)
-        total_a = gathers(1, 0, W)
-        quant_w2(0)
-        quant_w2(1)
-        codes0, sc0 = quant_z(0, 0, M, zb0)
-        for c in range(2):
-            for n in range(4):
-                mm2(n, c, 0, codes0[:, W * c : W * (c + 1)], sc0[:, W * c : W * (c + 1)])
-        zb_a = root(1, 0, W, total_a)
-        finish(0, zb_a)
-        prev = [eps_wide[:, PACK + t, 0:W] for t in range(PACK)]
-        first_sum = keep.tile([P, PACK, W], F32, name="first_sum")
-        second_sum = keep.tile([P, PACK, W], F32, name="second_sum", tag="held", align_bytes=64)
+        total_pass0 = sum_of_picks(0, M)
+        z_pass0 = keep.tile([P, M, PACK], BF16, name="z_pass0", align_bytes=64)
+        root(z_pass0[:], total_pass0)
+        total_first_half = sum_of_picks(1, BEATS_HALF)
+        for b in range(2):
+            nc.vector.quantize_mx(
+                out=w2_codes[b][:].bitcast(FP8X4),
+                scales=w2_planes[b][:],
+                in_=w2_rounded[b][:].rearrange("p n t -> p (n t)"),
+            )
+        codes_pass0, plane_pass0 = quantise_z("pass0", z_pass0)
+        for half in range(2):
+            beats = slice(BEATS_HALF * half, BEATS_HALF * (half + 1))
+            for n in range(N // P):
+                second_product(n, half, 0, codes_pass0[:, beats], plane_pass0[:, beats])
+        z_first_half = keep.tile([P, BEATS_HALF, PACK], BF16, name="z_first_half", tag="z_first_half", align_bytes=64)
+        root(z_first_half[:], total_first_half)
+        finish(0, z_first_half)
+
+        so_far = [eps_wide[1][:, t, 0:BEATS_HALF] for t in range(PACK)]
+        first_sum = keep.tile([P, PACK, BEATS_HALF], F32, name="first_sum")
+        second_sum = keep.tile([P, PACK, BEATS_HALF], F32, name="second_sum", tag="z_first_half", align_bytes=64)
         for i, sums in enumerate((first_sum, second_sum)):
             for t in range(PACK):
-                nc.vector.tensor_tensor(sums[:, t, :], sq[PACK + t][:].indirect(pos_sb[i][:, W // 16 : M // 16]), prev[t], ADD)
-                prev[t] = sums[:, t, :]
-        zb_b = keep.tile([P, W, PACK], BF16, name="zb_b", align_bytes=64)
-        Q = W // 2
-        for u in range(2):
-            total = keep.tile([P, PACK, Q], F32, name="total_q%d" % u)
-            cols = slice((W + Q * u) // 16, (W + Q * (u + 1)) // 16)
+                pick_and_add(sums[:, t, :], 1, t, i, slice(BEATS_HALF, M), so_far[t])
+                so_far[t] = sums[:, t, :]
+        z_second_half = keep.tile([P, BEATS_HALF, PACK], BF16, name="z_second_half", align_bytes=64)
+        for quarter in range(2):
+            within = slice(BEATS_QUARTER * quarter, BEATS_QUARTER * (quarter + 1))
+            beats = slice(BEATS_HALF + within.start, BEATS_HALF + within.stop)
+            total_quarter = keep.tile([P, PACK, BEATS_QUARTER], F32, name="total_quarter%d" % quarter)
             for t in range(PACK):
-                nc.vector.tensor_tensor(total[:, t, :], sq[PACK + t][:].indirect(pos_sb[2][:, cols]), prev[t][:, Q * u : Q * (u + 1)], ADD)
-            nc.scalar.activation(zb_b[:, Q * u : Q * (u + 1), :], total[:].rearrange("p t m -> p m t"), ACT.Sqrt)
-        finish(1, zb_b)
+                pick_and_add(total_quarter[:, t, :], 1, t, 2, beats, so_far[t][:, within])
+            root(z_second_half[:, within, :], total_quarter)
+        finish(1, z_second_half)

@@ -1,6 +1,7 @@
 from contextlib import ExitStack
 
 import concourse.mybir as mybir
+from concourse.masks import make_identity
 
 K, T, S, M, H, N = 1024, 4096, 1024, 512, 1024, 512
 FLOPS = 2 * K * H * S + 2 * H * N * M
@@ -19,13 +20,11 @@ ADD = mybir.AluOpType.add
 P = 128
 PACK = 4
 PASS = P * PACK
+RUN = 4
 BANK = 512
 PER_COLUMN = 16
 QUADRANT = 32
-SPREAD = 4
-FIRST_PART = 3 * T // 8
-BEATS_HALF = M // 2
-BEATS_QUARTER = M // 4
+LINE = 4
 
 
 def tile_list_choir_blend_features_kernel(
@@ -38,94 +37,100 @@ def tile_list_choir_blend_features_kernel(
         partial = ctx.enter_context(tc.tile_pool(name="partial", bufs=4))
         psum = ctx.enter_context(tc.psum_pool(name="psum", bufs=1))
 
+        def tile(shape, dtype, name, tag=None):
+            return keep.tile(shape, dtype, name=name, tag=tag or name, align_bytes=64)
+
         offs_sb = lists.tile([P, S // PER_COLUMN], U16, name="offs_sb")
         pos_sb = [lists.tile([P, M // PER_COLUMN], U16, name="pos%d_sb" % i) for i in range(3)]
 
-        tab_scale_rows = keep.tile([P, T], U8, name="tab_scale_rows", tag="scale_window", align_bytes=64)
-        w4_planes_raw = keep.tile([P, 2, H], U8, name="w4_planes_raw", align_bytes=64)
-        nc.vector.memset(tab_scale_rows[:].bitcast(I32), 0)
-        nc.vector.memset(w4_planes_raw[:].bitcast(I32), 0)
-        v_planes = keep.tile([P, 2, S], U8, name="v_planes", align_bytes=64)
-        nc.gpsimd.memset(v_planes[:].bitcast(I32), 0)
-
-        w4_codes, w4_planes = [], []
+        tab = [tab_words[a].rearrange("p t i -> p (t i)").bitcast(I32) for a in range(2)]
 
         def load_w4_words(b, tag):
-            raw = keep.tile([P, 2, 2 * PASS], U8, name="w4_raw%d" % b, tag=tag, align_bytes=64)
+            raw = tile([P, 2, 2 * PASS], U8, "w4_raw%d" % b, tag)
             src = w4_words[:, :, 2 * PASS * b : 2 * PASS * (b + 1)].rearrange("a p c -> p a c")
             nc.sync.dma_start(raw[:].bitcast(I32), src.bitcast(I32))
             return raw
 
-        def permute_w4_words(b, raw, tag):
-            w4_codes.append(keep.tile([P, 2, 2 * PASS], U8, name="w4_codes%d" % b, tag=tag, align_bytes=64))
-            nc.vector.tensor_copy(
-                w4_codes[b][:].bitcast(U16).rearrange("p a (t m) -> p a t m", t=PACK),
-                raw[:].bitcast(U16).rearrange("p a (m t) -> p a t m", t=PACK),
-            )
-
-        def permute_w4_planes(b):
-            w4_planes.append(keep.tile([P, 2, PASS], U8, name="w4_planes%d" % b, align_bytes=64))
-            nc.vector.tensor_copy(
-                w4_planes[b][:].rearrange("p a (t m) -> p a t m", t=PACK),
-                w4_planes_raw[:, :, PASS * b : PASS * (b + 1)].rearrange("p a (m t) -> p a t m", t=PACK),
-            )
-
-        tab = [tab_words[a].rearrange("p t i -> p (t i)").bitcast(I32) for a in range(2)]
-        words0 = keep.tile([P, T], I32, name="words0", align_bytes=64)
+        w4_planes_raw = tile([P, 2, H], U8, "w4_planes_raw")
+        nc.vector.memset(w4_planes_raw[:].bitcast(I32), 0)
         nc.sync.dma_start(offs_sb[:], offs)
-        w4_raw0 = load_w4_words(0, "words1")
-        nc.sync.dma_start(words0[:, 0:FIRST_PART], tab[0][:, 0:FIRST_PART])
-        nc.scalar.dma_start(
-            tab_scale_rows[0:P:SPREAD, :].bitcast(I32), tab_scales.rearrange("a q t -> (a q) t").bitcast(I32)
+        scale_rows = tile([P, T], U8, "scale_rows")
+        nc.sync.dma_start(
+            scale_rows[0:QUADRANT, :].bitcast(I32), tab_scales.rearrange("a q t -> q a t").bitcast(I32)
         )
-        eps_sb = keep.tile([P, 2, PACK], F32, name="eps_sb")
-        nc.gpsimd.dma_start(eps_sb[:], eps.rearrange("(b p t) -> p b t", p=P, t=PACK))
-        nc.sync.dma_start(pos_sb[0][:], pos1)
-        nc.sync.dma_start(pos_sb[1][:], pos2)
-        nc.sync.dma_start(words0[:, FIRST_PART:T], tab[0][:, FIRST_PART:T])
-        nc.sync.dma_start(pos_sb[2][:], pos3)
+        eps_rows = tile([2, PASS], F32, "eps_rows")
+        nc.sync.dma_start(eps_rows[:], eps.rearrange("(b r) -> b r", b=2))
+        words = [tile([P, T], I32, "words%d" % a) for a in range(2)]
+        nc.sync.dma_start(words[0][:], tab[0])
+        w4_raw0 = load_w4_words(0, None)
         for quad in range(4):
-            nc.scalar.dma_start(
+            nc.sync.dma_start(
                 w4_planes_raw[QUADRANT * quad : QUADRANT * quad + 4, :, :].bitcast(I32),
                 w4_scales[:, 4 * quad : 4 * quad + 4, :].rearrange("a r c -> r a c").bitcast(I32),
             )
-        permute_w4_words(0, w4_raw0, "w4_codes0")
-        words1 = keep.tile([P, T], I32, name="words1", tag="words1", align_bytes=64)
-        nc.sync.dma_start(words1[:], tab[1])
+        nc.sync.dma_start(words[1][:], tab[1])
+        for i, pos in enumerate((pos1, pos2, pos3)):
+            nc.sync.dma_start(pos_sb[i][:], pos)
 
-        picked_scales = keep.tile([P, S], U8, name="picked_scales", tag="picked_scales", align_bytes=64)
-        nc.vector.tensor_copy(picked_scales[:], tab_scale_rows[:].indirect(offs_sb[:]))
-        move_queues = [[nc.sync] * 4, [nc.scalar] * 3 + [nc.gpsimd]]
-        for a in range(2):
-            for quad in range(4):
-                first = SPREAD * (16 * a + 4 * quad)
-                move_queues[a][quad].dma_start(
-                    v_planes[QUADRANT * quad : QUADRANT * quad + 4, a, :].bitcast(I32),
-                    picked_scales[first : first + 4 * SPREAD : SPREAD, :].bitcast(I32),
-                )
-        w4_raw1 = load_w4_words(1, "picked_scales")
+        eps_dealt = tile([P, PACK, P], F32, "eps_dealt")
+        nc.gpsimd.memset(eps_dealt[:], 0.0)
+        identity = tile([P, P], F32, "identity")
+        make_identity(nc, identity[:])
+        nc.gpsimd.tensor_copy(
+            eps_dealt[0:2, :, :].rearrange("b t (i u) -> b t i u", u=RUN),
+            eps_rows[:].rearrange("b (i t u) -> b t i u", t=PACK, u=RUN),
+        )
+        eps_turned = psum.tile([P, PACK, P], F32, name="eps_turned", tag="bank7")
+        for t in range(PACK):
+            nc.tensor.transpose(eps_turned[:, t, :], eps_dealt[:, t, :], identity[:])
+
+        nc.vector.memset(scale_rows[QUADRANT : 2 * QUADRANT, :].bitcast(I32), 0)
+        nc.vector.memset(scale_rows[2 * QUADRANT : P, :].bitcast(I32), 0)
+        v_planes = tile([P, 2, S], U8, "v_planes")
+        nc.vector.memset(v_planes[:].bitcast(I32), 0)
+
+        w4_codes = []
+
+        def permute_w4_words(b, raw, tag):
+            w4_codes.append(tile([P, 2, 2 * PASS], U8, "w4_codes%d" % b, tag))
+            nc.vector.tensor_copy(
+                w4_codes[b][:].bitcast(I32).rearrange("p a (t i v) -> p a t i v", t=PACK, v=2),
+                raw[:].bitcast(I32).rearrange("p a (i t v) -> p a t i v", t=PACK, v=2),
+            )
+
+        picked_scales = tile([P, S], U8, "picked_scales", "picked")
+        nc.vector.tensor_copy(picked_scales[:], scale_rows[:].indirect(offs_sb[:]))
+        for quad in range(4):
+            nc.sync.dma_start(
+                v_planes[QUADRANT * quad : QUADRANT * quad + 4, :, :].bitcast(I32),
+                picked_scales[8 * quad : 8 * quad + 8, :].bitcast(I32),
+            )
+        w4_raw1 = load_w4_words(1, "picked")
+        eps_sb = tile([P, 2, PACK], F32, "eps_sb")
+        nc.scalar.copy(eps_sb[:], eps_turned[:, :, 0:2].rearrange("p t b -> p b t"))
 
         eps_wide = []
-
-        def spread_eps(b, tag):
-            eps_wide.append(keep.tile([P, PACK, M], F32, name="eps_wide%d" % b, tag=tag, align_bytes=64))
+        for b in range(2):
+            eps_wide.append(tile([P, PACK, M], F32, "eps_wide%d" % b))
             nc.scalar.copy(eps_wide[b][:], eps_sb[:, b, :].unsqueeze(2).to_broadcast([P, PACK, M]))
 
-        spread_eps(0, "scale_window")
-
-        v_pass0 = keep.tile([P, S], U32, name="v_pass0", tag="v_pass0", align_bytes=64)
-        nc.vector.tensor_copy(v_pass0[:], words0[:].bitcast(U32).indirect(offs_sb[:]))
-        permute_w4_planes(0)
+        v_pass0 = tile([P, S], U32, "v_pass0")
+        nc.vector.tensor_copy(v_pass0[:], words[0][:].bitcast(U32).indirect(offs_sb[:]))
+        permute_w4_words(0, w4_raw0, None)
+        w4_planes = tile([P, 2, H], U8, "w4_planes", "words0")
+        nc.vector.tensor_copy(
+            w4_planes[:].bitcast(I32).rearrange("p a (b t i) -> p a b t i", b=2, t=PACK),
+            w4_planes_raw[:].bitcast(I32).rearrange("p a (b i t) -> p a b t i", b=2, t=PACK),
+        )
         v_codes = {(0, half): v_pass0[:, BANK * half : BANK * (half + 1)] for half in range(2)}
         for half in range(2):
-            v_pass1 = keep.tile([P, BANK], U32, name="v_pass1_%d" % half, tag="v_pass1_%d" % half, align_bytes=64)
+            v_pass1 = tile([P, BANK], U32, "v_pass1_%d" % half)
             entries = slice(BANK * half // PER_COLUMN, BANK * (half + 1) // PER_COLUMN)
-            nc.vector.tensor_copy(v_pass1[:], words1[:].bitcast(U32).indirect(offs_sb[:, entries]))
+            nc.vector.tensor_copy(v_pass1[:], words[1][:].bitcast(U32).indirect(offs_sb[:, entries]))
             v_codes[1, half] = v_pass1[:]
         permute_w4_words(1, w4_raw1, "words1")
-        permute_w4_planes(1)
 
-        squares = [keep.tile([P, S], F32, name="squares%d" % j) for j in range(2 * PACK)]
+        squares = [tile([P, S], F32, "squares%d" % j) for j in range(2 * PACK)]
         h_banks = {}
 
         def first_product(j, half, a):
@@ -135,7 +140,7 @@ def tile_list_choir_blend_features_kernel(
             nc.tensor.matmul_mx(
                 out=h_banks[j, half][:],
                 lhsT=w4_codes[b][:, a, 2 * P * t : 2 * P * (t + 1)].bitcast(FP4X4),
-                lhsT_scale=w4_planes[b][:, a, P * t : P * (t + 1)],
+                lhsT_scale=w4_planes[:, a, P * j : P * (j + 1)],
                 rhs=v_codes[a, half].bitcast(FP8X4),
                 rhs_scale=v_planes[:, a, BANK * half : BANK * (half + 1)],
                 start=(a == 0),
@@ -144,120 +149,119 @@ def tile_list_choir_blend_features_kernel(
             if a == 1:
                 nc.scalar.activation(squares[j][:, BANK * half : BANK * (half + 1)], h_banks[j, half][:], ACT.Square)
 
-        first_product(0, 0, 0)
-        first_product(0, 1, 0)
-        first_product(0, 0, 1)
-        first_product(1, 0, 0)
-        first_product(0, 1, 1)
-        first_product(1, 0, 1)
-        first_product(1, 1, 0)
-        first_product(1, 1, 1)
-        for j in range(2, 2 * PACK):
-            for half in range(2):
-                for a in range(2):
+        for j in range(2 * PACK):
+            for a in range(2):
+                for half in range(2):
                     first_product(j, half, a)
 
-        spread_eps(1, "v_pass1_0")
+        def by_lines(dst, src):
+            return (
+                dst.rearrange("p (c i) t -> p c t i", i=LINE),
+                src.rearrange("p t (c i) -> p c t i", i=LINE),
+            )
 
-        w2_raw = keep.tile([P, 2, PACK, N], F32, name="w2_raw", tag="picked_scales", align_bytes=64)
-        w2_rounded, w2_codes, w2_planes = [], [], []
+        w2_raw = tile([P, 2, PACK, N], F32, "w2_raw", "picked")
+        w2_rounded = []
         for b, tag in enumerate(("v_pass0", "v_pass1_1")):
-            raw = w2_raw[:, b, :, :]
-            nc.sync.dma_start(raw, w2[PASS * b : PASS * (b + 1), :].rearrange("(p t) n -> p t n", t=PACK))
-            rounded = keep.tile([P, N, PACK], BF16, name="w2_rounded%d" % b, tag=tag, align_bytes=64)
-            for n in range(N // P):
-                cols = slice(P * n, P * (n + 1))
-                nc.scalar.copy(rounded[:, cols, :], raw[:, :, cols].rearrange("p t n -> p n t"))
-            w2_rounded.append(rounded)
-            w2_codes.append(keep.tile([P, N], U32, name="w2_codes%d" % b, align_bytes=64))
-            w2_planes.append(keep.tile([P, N], U8, name="w2_plane%d" % b, align_bytes=64))
+            rows = w2[PASS * b : PASS * (b + 1), :].rearrange("(i t u) n -> t i u n", t=PACK, u=RUN)
+            for t in range(PACK):
+                nc.sync.dma_start(w2_raw[:, b, t, :], rows[t])
+            w2_rounded.append(tile([P, N, PACK], BF16, "w2_rounded%d" % b, tag))
+            nc.scalar.copy(*by_lines(w2_rounded[b][:], w2_raw[:, b, :, :]))
 
-        def pick_and_add(dst, b, t, i, beats, so_far):
+        def pick_and_add(dst, j, i, beats, so_far):
             entries = slice(beats.start // PER_COLUMN, beats.stop // PER_COLUMN)
-            nc.vector.tensor_tensor(dst, squares[PACK * b + t][:].indirect(pos_sb[i][:, entries]), so_far, ADD)
+            nc.vector.tensor_tensor(dst, squares[j][:].indirect(pos_sb[i][:, entries]), so_far, ADD)
 
-        def sum_of_picks(b, width):
-            total = keep.tile([P, PACK, width], F32, name="total%d" % b, align_bytes=64)
-            for pair in ((0, 1), (2, 3)):
-                so_far = {t: eps_wide[b][:, t, 0:width] for t in pair}
-                for i in range(3):
-                    for t in pair:
-                        if i < 2:
-                            part = partial.tile([P, width], F32, name="part", tag="part")
-                            dst = part[:]
-                        else:
-                            dst = total[:, t, :]
-                        pick_and_add(dst, b, t, i, slice(0, width), so_far[t])
-                        so_far[t] = dst
+        def picks(name, tag, i, beats, so_far):
+            total = tile([P, PACK, beats.stop - beats.start], F32, name, tag)
+            for t in range(PACK):
+                pick_and_add(total[:, t, :], PACK + t, i, beats, so_far[:, t, :])
             return total
 
-        def root(dst, total):
-            nc.scalar.activation(dst, total[:].rearrange("p t m -> p m t"), ACT.Sqrt)
+        def root(name, tag, total):
+            z = tile([P, total.shape[2], PACK], BF16, name, tag)
+            nc.scalar.activation(*by_lines(z[:], total[:]), ACT.Sqrt)
+            return z
 
-        def quantise_z(name, z):
-            width = z.shape[1]
-            codes = keep.tile([P, width], U32, name="z_codes_" + name, align_bytes=64)
-            plane = keep.tile([P, width], U8, name="z_plane_" + name, align_bytes=64)
-            nc.vector.quantize_mx(out=codes[:].bitcast(FP8X4), scales=plane[:], in_=z[:].rearrange("p m t -> p (m t)"))
+        def quantise(name, tag, rounded):
+            width = rounded.shape[1]
+            codes = tile([P, width], U32, name + "_codes", tag)
+            plane = tile([P, width], U8, name + "_plane")
+            nc.vector.quantize_mx(
+                out=codes[:].bitcast(FP8X4), scales=plane[:], in_=rounded[:].rearrange("p m t -> p (m t)")
+            )
             return codes, plane
 
+        total0 = tile([P, PACK, M], F32, "total0")
+        for pair in ((0, 1), (2, 3)):
+            so_far = {t: eps_wide[0][:, t, :] for t in pair}
+            for i in range(3):
+                for t in pair:
+                    if i < 2:
+                        part = partial.tile([P, M], F32, name="part", tag="part")
+                        dst = part[:]
+                    else:
+                        dst = total0[:, t, :]
+                    pick_and_add(dst, t, i, slice(0, M), so_far[t])
+                    so_far[t] = dst
+        z0 = root("z0", "picked", total0)
+        w2_q = [quantise("w2_%d" % b, "squares%d" % (3 - b), w2_rounded[b]) for b in range(2)]
+
+        chunks = [slice(0, 256), slice(256, 384), slice(384, 512)]
         y_banks = {}
 
-        def second_product(n, half, b, codes, plane):
-            if b == 0:
-                y_banks[n, half] = psum.tile(
-                    [P, BEATS_HALF], F32, name="y%d_%d" % (n, half), tag="bank%d" % (4 * half + n)
+        def second_product(c, b, codes, plane):
+            beats = chunks[c]
+            width = beats.stop - beats.start
+            per_bank = BANK // width
+            for n in range(N // P):
+                g, s = divmod(n, per_bank)
+                if b == 0 and s == 0:
+                    y_banks[c, g] = psum.tile(
+                        [P, per_bank, width], F32, name="y%d_%d" % (c, g), tag="bank%d" % (2 * c + g)
+                    )
+                nc.tensor.matmul_mx(
+                    out=y_banks[c, g][:, s, :],
+                    lhsT=w2_q[b][0][:, P * n : P * (n + 1)].bitcast(FP8X4),
+                    lhsT_scale=w2_q[b][1][:, P * n : P * (n + 1)],
+                    rhs=codes.bitcast(FP8X4),
+                    rhs_scale=plane,
+                    start=(b == 0 and s == 0),
+                    stop=(b == 1 and s == per_bank - 1),
                 )
-            nc.tensor.matmul_mx(
-                out=y_banks[n, half][:],
-                lhsT=w2_codes[b][:, P * n : P * (n + 1)].bitcast(FP8X4),
-                lhsT_scale=w2_planes[b][:, P * n : P * (n + 1)],
-                rhs=codes.bitcast(FP8X4),
-                rhs_scale=plane,
-                start=(b == 0),
-                stop=(b == 1),
-            )
 
-        def finish(half, z):
-            codes, plane = quantise_z("pass1_%d" % half, z)
-            for n in range(N // P):
-                second_product(n, half, 1, codes[:], plane[:])
-                result = keep.tile([P, BEATS_HALF], F32, name="result%d_%d" % (n, half))
-                nc.scalar.activation(result[:], y_banks[n, half][:], ACT.Silu)
-                nc.sync.dma_start(out[P * n : P * (n + 1), BEATS_HALF * half : BEATS_HALF * (half + 1)], result[:])
+        def finish(c):
+            beats = chunks[c]
+            width = beats.stop - beats.start
+            per_bank = BANK // width
+            for g in range(N // P // per_bank):
+                result = tile([P, per_bank, width], F32, "result%d_%d" % (c, g))
+                nc.scalar.activation(result[:], y_banks[c, g][:], ACT.Silu)
+                rows = out[P * per_bank * g : P * per_bank * (g + 1), beats]
+                nc.sync.dma_start(rows.rearrange("(s p) m -> p s m", p=P), result[:])
 
-        total_pass0 = sum_of_picks(0, M)
-        z_pass0 = keep.tile([P, M, PACK], BF16, name="z_pass0", align_bytes=64)
-        root(z_pass0[:], total_pass0)
-        total_first_half = sum_of_picks(1, BEATS_HALF)
-        for b in range(2):
-            nc.vector.quantize_mx(
-                out=w2_codes[b][:].bitcast(FP8X4),
-                scales=w2_planes[b][:],
-                in_=w2_rounded[b][:].rearrange("p n t -> p (n t)"),
-            )
-        codes_pass0, plane_pass0 = quantise_z("pass0", z_pass0)
-        for half in range(2):
-            beats = slice(BEATS_HALF * half, BEATS_HALF * (half + 1))
-            for n in range(N // P):
-                second_product(n, half, 0, codes_pass0[:, beats], plane_pass0[:, beats])
-        z_first_half = keep.tile([P, BEATS_HALF, PACK], BF16, name="z_first_half", tag="z_first_half", align_bytes=64)
-        root(z_first_half[:], total_first_half)
-        finish(0, z_first_half)
-
-        so_far = [eps_wide[1][:, t, 0:BEATS_HALF] for t in range(PACK)]
-        first_sum = keep.tile([P, PACK, BEATS_HALF], F32, name="first_sum")
-        second_sum = keep.tile([P, PACK, BEATS_HALF], F32, name="second_sum", tag="z_first_half", align_bytes=64)
-        for i, sums in enumerate((first_sum, second_sum)):
-            for t in range(PACK):
-                pick_and_add(sums[:, t, :], 1, t, i, slice(BEATS_HALF, M), so_far[t])
-                so_far[t] = sums[:, t, :]
-        z_second_half = keep.tile([P, BEATS_HALF, PACK], BF16, name="z_second_half", align_bytes=64)
-        for quarter in range(2):
-            within = slice(BEATS_QUARTER * quarter, BEATS_QUARTER * (quarter + 1))
-            beats = slice(BEATS_HALF + within.start, BEATS_HALF + within.stop)
-            total_quarter = keep.tile([P, PACK, BEATS_QUARTER], F32, name="total_quarter%d" % quarter)
-            for t in range(PACK):
-                pick_and_add(total_quarter[:, t, :], 1, t, 2, beats, so_far[t][:, within])
-            root(z_second_half[:, within, :], total_quarter)
-        finish(1, z_second_half)
+        first = chunks[0]
+        rest = slice(first.stop, M)
+        sum1 = picks("first_sum1", "v_pass1_1", 0, first, eps_wide[1][:, :, first])
+        sum2 = picks("first_sum2", None, 1, first, sum1)
+        codes0, plane0 = quantise("z0", "v_pass1_1", z0)
+        for c, beats in enumerate(chunks):
+            second_product(c, 0, codes0[:, beats], plane0[:, beats])
+        total_a = picks("total_a", "picked", 2, first, sum2)
+        z_a = root("z_a", None, total_a)
+        rest1 = picks("rest_sum1", None, 0, rest, eps_wide[1][:, :, rest])
+        codes_a, plane_a = quantise("z_a", "eps_wide1", z_a)
+        second_product(0, 1, codes_a[:], plane_a[:])
+        finish(0)
+        rest2 = picks("rest_sum2", "z_a", 1, rest, rest1)
+        total_b = picks("total_b", "eps_wide1", 2, chunks[1], rest2[:, :, 0:128])
+        z_b = root("z_b", None, total_b)
+        total_c = picks("total_c", None, 2, chunks[2], rest2[:, :, 128:256])
+        z_c = root("z_c", None, total_c)
+        codes_b, plane_b = quantise("z_b", "z_a", z_b)
+        second_product(1, 1, codes_b[:], plane_b[:])
+        codes_c, plane_c = quantise("z_c", None, z_c)
+        second_product(2, 1, codes_c[:], plane_c[:])
+        finish(1)
+        finish(2)

@@ -58,19 +58,19 @@ def tile_list_choir_blend_features_kernel(
         nc.sync.dma_start(
             scale_rows[0:QUADRANT, :].bitcast(I32), tab_scales.rearrange("a q t -> q a t").bitcast(I32)
         )
-        eps_rows = tile([2, PASS], F32, "eps_rows")
-        nc.sync.dma_start(eps_rows[:], eps.rearrange("(b r) -> b r", b=2))
-        words = [tile([P, T], I32, "words%d" % a) for a in range(2)]
-        nc.sync.dma_start(words[0][:], tab[0])
         w4_raw0 = load_w4_words(0, None)
-        for quad in range(4):
+        for r in range(4):
             nc.sync.dma_start(
-                w4_planes_raw[QUADRANT * quad : QUADRANT * quad + 4, :, :].bitcast(I32),
-                w4_scales[:, 4 * quad : 4 * quad + 4, :].rearrange("a r c -> r a c").bitcast(I32),
+                w4_planes_raw[r:P:QUADRANT, :, :].bitcast(I32),
+                w4_scales[:, r:16:4, :].rearrange("a q c -> q a c").bitcast(I32),
             )
-        nc.sync.dma_start(words[1][:], tab[1])
+        words = [tile([P, T], I32, "words%d" % a) for a in range(2)]
+        for a in range(2):
+            nc.sync.dma_start(words[a][:], tab[a])
         for i, pos in enumerate((pos1, pos2, pos3)):
             nc.sync.dma_start(pos_sb[i][:], pos)
+        eps_rows = tile([2, PASS], F32, "eps_rows")
+        nc.gpsimd.dma_start(eps_rows[:], eps.rearrange("(b r) -> b r", b=2))
 
         eps_dealt = tile([P, PACK, P], F32, "eps_dealt")
         nc.gpsimd.memset(eps_dealt[:], 0.0)
@@ -100,8 +100,8 @@ def tile_list_choir_blend_features_kernel(
 
         picked_scales = tile([P, S], U8, "picked_scales", "picked")
         nc.vector.tensor_copy(picked_scales[:], scale_rows[:].indirect(offs_sb[:]))
-        for quad in range(4):
-            nc.sync.dma_start(
+        for quad in (0, 2, 1, 3):
+            nc.scalar.dma_start(
                 v_planes[QUADRANT * quad : QUADRANT * quad + 4, :, :].bitcast(I32),
                 picked_scales[8 * quad : 8 * quad + 8, :].bitcast(I32),
             )
@@ -109,10 +109,6 @@ def tile_list_choir_blend_features_kernel(
         eps_sb = tile([P, 2, PACK], F32, "eps_sb")
         nc.scalar.copy(eps_sb[:], eps_turned[:, :, 0:2].rearrange("p t b -> p b t"))
 
-        eps_wide = []
-        for b in range(2):
-            eps_wide.append(tile([P, PACK, M], F32, "eps_wide%d" % b))
-            nc.scalar.copy(eps_wide[b][:], eps_sb[:, b, :].unsqueeze(2).to_broadcast([P, PACK, M]))
 
         v_pass0 = tile([P, S], U32, "v_pass0")
         nc.vector.tensor_copy(v_pass0[:], words[0][:].bitcast(U32).indirect(offs_sb[:]))
@@ -122,6 +118,8 @@ def tile_list_choir_blend_features_kernel(
             w4_planes[:].bitcast(I32).rearrange("p a (b t i) -> p a b t i", b=2, t=PACK),
             w4_planes_raw[:].bitcast(I32).rearrange("p a (b i t) -> p a b t i", b=2, t=PACK),
         )
+        eps_wide = [tile([P, PACK, M], F32, "eps_wide0", "w4_planes_raw"), None]
+        nc.vector.tensor_copy(eps_wide[0][:], eps_sb[:, 0, :].unsqueeze(2).to_broadcast([P, PACK, M]))
         v_codes = {(0, half): v_pass0[:, BANK * half : BANK * (half + 1)] for half in range(2)}
         for half in range(2):
             v_pass1 = tile([P, BANK], U32, "v_pass1_%d" % half)
@@ -129,6 +127,12 @@ def tile_list_choir_blend_features_kernel(
             nc.vector.tensor_copy(v_pass1[:], words[1][:].bitcast(U32).indirect(offs_sb[:, entries]))
             v_codes[1, half] = v_pass1[:]
         permute_w4_words(1, w4_raw1, "words1")
+
+        w2_raw = tile([P, 2, PACK, N], F32, "w2_raw", "picked")
+        for b in range(2):
+            rows = w2[PASS * b : PASS * (b + 1), :].rearrange("(i t u) n -> t i u n", t=PACK, u=RUN)
+            for t in range(PACK):
+                nc.sync.dma_start(w2_raw[:, b, t, :], rows[t])
 
         squares = [tile([P, S], F32, "squares%d" % j) for j in range(2 * PACK)]
         h_banks = {}
@@ -154,18 +158,17 @@ def tile_list_choir_blend_features_kernel(
                 for half in range(2):
                     first_product(j, half, a)
 
+        eps_wide[1] = tile([P, PACK, M], F32, "eps_wide1", "v_pass1_0")
+        nc.scalar.copy(eps_wide[1][:], eps_sb[:, 1, :].unsqueeze(2).to_broadcast([P, PACK, M]))
+
         def by_lines(dst, src):
             return (
                 dst.rearrange("p (c i) t -> p c t i", i=LINE),
                 src.rearrange("p t (c i) -> p c t i", i=LINE),
             )
 
-        w2_raw = tile([P, 2, PACK, N], F32, "w2_raw", "picked")
         w2_rounded = []
         for b, tag in enumerate(("v_pass0", "v_pass1_1")):
-            rows = w2[PASS * b : PASS * (b + 1), :].rearrange("(i t u) n -> t i u n", t=PACK, u=RUN)
-            for t in range(PACK):
-                nc.sync.dma_start(w2_raw[:, b, t, :], rows[t])
             w2_rounded.append(tile([P, N, PACK], BF16, "w2_rounded%d" % b, tag))
             nc.scalar.copy(*by_lines(w2_rounded[b][:], w2_raw[:, b, :, :]))
 
@@ -208,60 +211,51 @@ def tile_list_choir_blend_features_kernel(
         z0 = root("z0", "picked", total0)
         w2_q = [quantise("w2_%d" % b, "squares%d" % (3 - b), w2_rounded[b]) for b in range(2)]
 
-        chunks = [slice(0, 256), slice(256, 384), slice(384, 512)]
+        halves = [slice(0, 256), slice(256, 512)]
         y_banks = {}
 
-        def second_product(c, b, codes, plane):
-            beats = chunks[c]
-            width = beats.stop - beats.start
-            per_bank = BANK // width
+        def second_product(beats, b, codes, plane):
+            half, first = divmod(beats.start, 256)
             for n in range(N // P):
-                g, s = divmod(n, per_bank)
-                if b == 0 and s == 0:
-                    y_banks[c, g] = psum.tile(
-                        [P, per_bank, width], F32, name="y%d_%d" % (c, g), tag="bank%d" % (2 * c + g)
-                    )
+                if b == 0:
+                    y_banks[half, n] = psum.tile([P, 256], F32, name="y%d_%d" % (half, n), tag="bank%d" % (4 * half + n))
                 nc.tensor.matmul_mx(
-                    out=y_banks[c, g][:, s, :],
+                    out=y_banks[half, n][:, first : first + beats.stop - beats.start],
                     lhsT=w2_q[b][0][:, P * n : P * (n + 1)].bitcast(FP8X4),
                     lhsT_scale=w2_q[b][1][:, P * n : P * (n + 1)],
                     rhs=codes.bitcast(FP8X4),
                     rhs_scale=plane,
-                    start=(b == 0 and s == 0),
-                    stop=(b == 1 and s == per_bank - 1),
+                    start=(b == 0),
+                    stop=(b == 1 and beats.stop % 256 == 0),
                 )
 
-        def finish(c):
-            beats = chunks[c]
-            width = beats.stop - beats.start
-            per_bank = BANK // width
-            for g in range(N // P // per_bank):
-                result = tile([P, per_bank, width], F32, "result%d_%d" % (c, g))
-                nc.scalar.activation(result[:], y_banks[c, g][:], ACT.Silu)
-                rows = out[P * per_bank * g : P * per_bank * (g + 1), beats]
-                nc.sync.dma_start(rows.rearrange("(s p) m -> p s m", p=P), result[:])
+        def finish(half):
+            for n in range(N // P):
+                result = tile([P, 256], F32, "result%d_%d" % (half, n))
+                nc.scalar.activation(result[:], y_banks[half, n][:], ACT.Silu)
+                nc.sync.dma_start(out[P * n : P * (n + 1), halves[half]], result[:])
 
+        chunks = [slice(0, 256), slice(256, 384), slice(384, 512)]
         first = chunks[0]
         rest = slice(first.stop, M)
         sum1 = picks("first_sum1", "v_pass1_1", 0, first, eps_wide[1][:, :, first])
         sum2 = picks("first_sum2", None, 1, first, sum1)
         codes0, plane0 = quantise("z0", "v_pass1_1", z0)
-        for c, beats in enumerate(chunks):
-            second_product(c, 0, codes0[:, beats], plane0[:, beats])
+        for beats in halves:
+            second_product(beats, 0, codes0[:, beats], plane0[:, beats])
         total_a = picks("total_a", "picked", 2, first, sum2)
         z_a = root("z_a", None, total_a)
         rest1 = picks("rest_sum1", None, 0, rest, eps_wide[1][:, :, rest])
-        codes_a, plane_a = quantise("z_a", "eps_wide1", z_a)
-        second_product(0, 1, codes_a[:], plane_a[:])
+        codes_a, plane_a = quantise("z_a", "v_pass1_0", z_a)
+        second_product(chunks[0], 1, codes_a[:], plane_a[:])
         finish(0)
         rest2 = picks("rest_sum2", "z_a", 1, rest, rest1)
-        total_b = picks("total_b", "eps_wide1", 2, chunks[1], rest2[:, :, 0:128])
+        total_b = picks("total_b", "v_pass1_0", 2, chunks[1], rest2[:, :, 0:128])
         z_b = root("z_b", None, total_b)
         total_c = picks("total_c", None, 2, chunks[2], rest2[:, :, 128:256])
         z_c = root("z_c", None, total_c)
         codes_b, plane_b = quantise("z_b", "z_a", z_b)
-        second_product(1, 1, codes_b[:], plane_b[:])
+        second_product(chunks[1], 1, codes_b[:], plane_b[:])
         codes_c, plane_c = quantise("z_c", None, z_c)
-        second_product(2, 1, codes_c[:], plane_c[:])
+        second_product(chunks[2], 1, codes_c[:], plane_c[:])
         finish(1)
-        finish(2)

@@ -52,31 +52,34 @@ def tile_list_choir_blend_features_kernel(
             return raw
 
         w4_planes_raw = tile([P, 2, H], U8, "w4_planes_raw")
-        nc.vector.memset(w4_planes_raw[:].bitcast(I32), 0)
         nc.sync.dma_start(offs_sb[:], offs)
         scale_rows = tile([P, T], U8, "scale_rows")
         nc.sync.dma_start(
-            scale_rows[0:QUADRANT, :].bitcast(I32), tab_scales.rearrange("a q t -> q a t").bitcast(I32)
+            scale_rows[0:QUADRANT, :].bitcast(I32), tab_scales.rearrange("a q t -> (a q) t").bitcast(I32)
         )
-        w4_raw0 = load_w4_words(0, None)
+        eps_rows = tile([2, PASS], F32, "eps_rows")
+        nc.sync.dma_start(eps_rows[:], eps.rearrange("(b r) -> b r", b=2))
         for r in range(4):
             nc.sync.dma_start(
                 w4_planes_raw[r:P:QUADRANT, :, :].bitcast(I32),
                 w4_scales[:, r:16:4, :].rearrange("a q c -> q a c").bitcast(I32),
             )
         words = [tile([P, T], I32, "words%d" % a) for a in range(2)]
+        nc.sync.dma_start(words[0][:], tab[0])
+        w4_raw0 = load_w4_words(0, None)
+        nc.vector.memset(scale_rows[QUADRANT : 2 * QUADRANT, :].bitcast(I32), 0)
+        nc.vector.memset(scale_rows[2 * QUADRANT : P, :].bitcast(I32), 0)
+        v_planes = [tile([P, S], U8, "v_plane%d" % a) for a in range(2)]
         for a in range(2):
-            nc.sync.dma_start(words[a][:], tab[a])
-        for i, pos in enumerate((pos1, pos2, pos3)):
-            nc.sync.dma_start(pos_sb[i][:], pos)
-        eps_rows = tile([2, PASS], F32, "eps_rows")
-        nc.gpsimd.dma_start(eps_rows[:], eps.rearrange("(b r) -> b r", b=2))
+            nc.vector.memset(v_planes[a][:].bitcast(I32), 0)
 
+        w4_planes = tile([P, 2, H], U8, "w4_planes")
+        nc.vector.memset(w4_planes[:].bitcast(I32), 0)
         eps_dealt = tile([P, PACK, P], F32, "eps_dealt")
         nc.gpsimd.memset(eps_dealt[:], 0.0)
         identity = tile([P, P], F32, "identity")
         make_identity(nc, identity[:])
-        nc.gpsimd.tensor_copy(
+        nc.scalar.copy(
             eps_dealt[0:2, :, :].rearrange("b t (i u) -> b t i u", u=RUN),
             eps_rows[:].rearrange("b (i t u) -> b t i u", t=PACK, u=RUN),
         )
@@ -84,10 +87,6 @@ def tile_list_choir_blend_features_kernel(
         for t in range(PACK):
             nc.tensor.transpose(eps_turned[:, t, :], eps_dealt[:, t, :], identity[:])
 
-        nc.vector.memset(scale_rows[QUADRANT : 2 * QUADRANT, :].bitcast(I32), 0)
-        nc.vector.memset(scale_rows[2 * QUADRANT : P, :].bitcast(I32), 0)
-        v_planes = tile([P, 2, S], U8, "v_planes")
-        nc.vector.memset(v_planes[:].bitcast(I32), 0)
 
         w4_codes = []
 
@@ -100,39 +99,55 @@ def tile_list_choir_blend_features_kernel(
 
         picked_scales = tile([P, S], U8, "picked_scales", "picked")
         nc.vector.tensor_copy(picked_scales[:], scale_rows[:].indirect(offs_sb[:]))
-        for quad in (0, 2, 1, 3):
-            nc.scalar.dma_start(
-                v_planes[QUADRANT * quad : QUADRANT * quad + 4, :, :].bitcast(I32),
-                picked_scales[8 * quad : 8 * quad + 8, :].bitcast(I32),
+        for quad in range(4):
+            live = slice(QUADRANT * quad, QUADRANT * quad + 4)
+            nc.vector.tensor_copy(
+                w4_planes[live].bitcast(I32).rearrange("p a (c t i) -> p (a c) t i", c=2, t=PACK),
+                w4_planes_raw[live].bitcast(I32).rearrange("p a (c i t) -> p (a c) t i", c=2, t=PACK),
             )
+
+        def move_scale_rows(a, r):
+            nc.sync.dma_start(
+                v_planes[a][r:P:QUADRANT, :].bitcast(I32),
+                picked_scales[16 * a + r : 16 * (a + 1) : 4, :].bitcast(I32),
+            )
+
+        move_scale_rows(0, 0)
+        nc.sync.dma_start(words[1][:], tab[1])
+        for a in range(2):
+            for r in range(1 - a, 4):
+                move_scale_rows(a, r)
+        for i, pos in enumerate((pos1, pos2, pos3)):
+            nc.sync.dma_start(pos_sb[i][:], pos)
         w4_raw1 = load_w4_words(1, "picked")
         eps_sb = tile([P, 2, PACK], F32, "eps_sb")
         nc.scalar.copy(eps_sb[:], eps_turned[:, :, 0:2].rearrange("p t b -> p b t"))
+        eps_half = tile([P, PACK], F32, "eps_half")
+        nc.scalar.mul(eps_half[:], eps_turned[:, :, 1], 0.5)
 
 
         v_pass0 = tile([P, S], U32, "v_pass0")
         nc.vector.tensor_copy(v_pass0[:], words[0][:].bitcast(U32).indirect(offs_sb[:]))
         permute_w4_words(0, w4_raw0, None)
-        w4_planes = tile([P, 2, H], U8, "w4_planes", "words0")
-        nc.vector.tensor_copy(
-            w4_planes[:].bitcast(I32).rearrange("p a (b t i) -> p a b t i", b=2, t=PACK),
-            w4_planes_raw[:].bitcast(I32).rearrange("p a (b i t) -> p a b t i", b=2, t=PACK),
-        )
-        eps_wide = [tile([P, PACK, M], F32, "eps_wide0", "w4_planes_raw"), None]
-        nc.vector.tensor_copy(eps_wide[0][:], eps_sb[:, 0, :].unsqueeze(2).to_broadcast([P, PACK, M]))
         v_codes = {(0, half): v_pass0[:, BANK * half : BANK * (half + 1)] for half in range(2)}
         for half in range(2):
-            v_pass1 = tile([P, BANK], U32, "v_pass1_%d" % half)
+            v_pass1 = tile([P, BANK], U32, "v_pass1_%d" % half, ("w4_raw0", None)[half])
             entries = slice(BANK * half // PER_COLUMN, BANK * (half + 1) // PER_COLUMN)
             nc.vector.tensor_copy(v_pass1[:], words[1][:].bitcast(U32).indirect(offs_sb[:, entries]))
             v_codes[1, half] = v_pass1[:]
         permute_w4_words(1, w4_raw1, "words1")
 
-        w2_raw = tile([P, 2, PACK, N], F32, "w2_raw", "picked")
-        for b in range(2):
-            rows = w2[PASS * b : PASS * (b + 1), :].rearrange("(i t u) n -> t i u n", t=PACK, u=RUN)
-            for t in range(PACK):
-                nc.sync.dma_start(w2_raw[:, b, t, :], rows[t])
+
+        logs = {t: tile([P, 2 * S], F32, "logs%d" % t) for t in (1, 2, 3)}
+        spare = [logs[1 + k // 2][:, S + M * (k % 2) : S + M * (k % 2 + 1)] for k in range(6)]
+        for b, t, count in ((0, 0, 2), (0, 2, 2), (1, 0, 1)):
+            k = PACK * b + t
+            nc.scalar.copy(
+                logs[1 + k // 2][:, S : S + M * count].rearrange("p (t m) -> p t m", m=M),
+                eps_sb[:, b, t : t + count].unsqueeze(2).to_broadcast([P, count, M]),
+            )
+        warm = tile([P, 1], F32, "warm")
+        nc.scalar.activation(warm[:], eps_sb[:, 0, 0:1], ACT.Ln)
 
         squares = [tile([P, S], F32, "squares%d" % j) for j in range(2 * PACK)]
         h_banks = {}
@@ -140,26 +155,31 @@ def tile_list_choir_blend_features_kernel(
         def first_product(j, half, a):
             b, t = divmod(j, PACK)
             if a == 0:
-                h_banks[j, half] = psum.tile([P, BANK], F32, name="h%d_%d" % (j, half), tag="bank%d" % (2 * t + half))
+                h_banks[j, half] = psum.tile([P, BANK], F32, name="h%d_%d" % (j, half), tag="bank%d" % (2 * (j % 2) + half))
             nc.tensor.matmul_mx(
                 out=h_banks[j, half][:],
                 lhsT=w4_codes[b][:, a, 2 * P * t : 2 * P * (t + 1)].bitcast(FP4X4),
                 lhsT_scale=w4_planes[:, a, P * j : P * (j + 1)],
                 rhs=v_codes[a, half].bitcast(FP8X4),
-                rhs_scale=v_planes[:, a, BANK * half : BANK * (half + 1)],
+                rhs_scale=v_planes[a][:, BANK * half : BANK * (half + 1)],
                 start=(a == 0),
                 stop=(a == 1),
             )
             if a == 1:
                 nc.scalar.activation(squares[j][:, BANK * half : BANK * (half + 1)], h_banks[j, half][:], ACT.Square)
 
-        for j in range(2 * PACK):
+        for j in range(2):
             for a in range(2):
                 for half in range(2):
                     first_product(j, half, a)
+        for j in range(2, 2 * PACK):
+            for half in range(2):
+                for a in range(2):
+                    first_product(j, half, a)
+            if j > PACK:
+                t = j - PACK
+                nc.scalar.activation(logs[t][:, 0:S], squares[j][:], ACT.Ln, bias=eps_half[:, t : t + 1])
 
-        eps_wide[1] = tile([P, PACK, M], F32, "eps_wide1", "v_pass1_0")
-        nc.scalar.copy(eps_wide[1][:], eps_sb[:, 1, :].unsqueeze(2).to_broadcast([P, PACK, M]))
 
         def by_lines(dst, src):
             return (
@@ -167,10 +187,6 @@ def tile_list_choir_blend_features_kernel(
                 src.rearrange("p t (c i) -> p c t i", i=LINE),
             )
 
-        w2_rounded = []
-        for b, tag in enumerate(("v_pass0", "v_pass1_1")):
-            w2_rounded.append(tile([P, N, PACK], BF16, "w2_rounded%d" % b, tag))
-            nc.scalar.copy(*by_lines(w2_rounded[b][:], w2_raw[:, b, :, :]))
 
         def pick_and_add(dst, j, i, beats, so_far):
             entries = slice(beats.start // PER_COLUMN, beats.stop // PER_COLUMN)
@@ -184,7 +200,7 @@ def tile_list_choir_blend_features_kernel(
 
         def root(name, tag, total):
             z = tile([P, total.shape[2], PACK], BF16, name, tag)
-            nc.scalar.activation(*by_lines(z[:], total[:]), ACT.Sqrt)
+            nc.scalar.activation(*by_lines(z[:], total), ACT.Sqrt)
             return z
 
         def quantise(name, tag, rounded):
@@ -198,18 +214,30 @@ def tile_list_choir_blend_features_kernel(
 
         total0 = tile([P, PACK, M], F32, "total0")
         for pair in ((0, 1), (2, 3)):
-            so_far = {t: eps_wide[0][:, t, :] for t in pair}
+            so_far = {t: spare[t] for t in pair}
             for i in range(3):
                 for t in pair:
-                    if i < 2:
+                    if i == 0 and t == 0:
+                        dst = tile([P, M], F32, "first_part", "picked")[:]
+                    elif i == 0 and t == 1:
+                        dst = spare[PACK + 1]
+                    elif i < 2:
                         part = partial.tile([P, M], F32, name="part", tag="part")
                         dst = part[:]
                     else:
                         dst = total0[:, t, :]
                     pick_and_add(dst, t, i, slice(0, M), so_far[t])
                     so_far[t] = dst
-        z0 = root("z0", "picked", total0)
-        w2_q = [quantise("w2_%d" % b, "squares%d" % (3 - b), w2_rounded[b]) for b in range(2)]
+        w2_raw = tile([P, 2, PACK, N], F32, "w2_raw", "picked")
+        for b in range(2):
+            rows = w2[PASS * b : PASS * (b + 1), :].rearrange("(i t u) n -> t i u n", t=PACK, u=RUN)
+            for t in range(PACK):
+                nc.sync.dma_start(w2_raw[:, b, t, :], rows[t])
+        picked = tile([P, PACK - 1, 2, M], F32, "picked_by_scalar", "eps_half")
+        for t in logs:
+            for i in range(2):
+                nc.scalar.activation(picked[:, t - 1, i, :], logs[t][:].indirect(pos_sb[i][:]), ACT.Exp)
+        z0 = root("z0", "logs3", total0[:])
 
         halves = [slice(0, 256), slice(256, 512)]
         y_banks = {}
@@ -221,8 +249,8 @@ def tile_list_choir_blend_features_kernel(
                     y_banks[half, n] = psum.tile([P, 256], F32, name="y%d_%d" % (half, n), tag="bank%d" % (4 * half + n))
                 nc.tensor.matmul_mx(
                     out=y_banks[half, n][:, first : first + beats.stop - beats.start],
-                    lhsT=w2_q[b][0][:, P * n : P * (n + 1)].bitcast(FP8X4),
-                    lhsT_scale=w2_q[b][1][:, P * n : P * (n + 1)],
+                    lhsT=w2_q[b, n][0].bitcast(FP8X4),
+                    lhsT_scale=w2_q[b, n][1],
                     rhs=codes.bitcast(FP8X4),
                     rhs_scale=plane,
                     start=(b == 0),
@@ -235,27 +263,35 @@ def tile_list_choir_blend_features_kernel(
                 nc.scalar.activation(result[:], y_banks[half, n][:], ACT.Silu)
                 nc.sync.dma_start(out[P * n : P * (n + 1), halves[half]], result[:])
 
-        chunks = [slice(0, 256), slice(256, 384), slice(384, 512)]
-        first = chunks[0]
-        rest = slice(first.stop, M)
-        sum1 = picks("first_sum1", "v_pass1_1", 0, first, eps_wide[1][:, :, first])
-        sum2 = picks("first_sum2", None, 1, first, sum1)
-        codes0, plane0 = quantise("z0", "v_pass1_1", z0)
+        beats = slice(0, M)
+        sum2 = tile([P, PACK, M], F32, "sum2")
+        sum1 = tile([P, M], F32, "sum1")
+        pick_and_add(sum1[:], PACK, 0, beats, spare[PACK])
+        nc.vector.tensor_tensor(sum2[:, 1, :], picked[:, 0, 0, :], picked[:, 0, 1, :], ADD)
+        pick_and_add(sum2[:, 0, :], PACK, 1, beats, sum1[:])
+        nc.vector.tensor_tensor(sum2[:, 2, :], picked[:, 1, 0, :], picked[:, 1, 1, :], ADD)
+        rounded0 = tile([P, N, PACK], BF16, "w2_rounded0", "sum1")
+        nc.vector.tensor_copy(*by_lines(rounded0[:], w2_raw[:, 0, :, :]))
+        nc.vector.tensor_tensor(sum2[:, 3, :], picked[:, 2, 0, :], picked[:, 2, 1, :], ADD)
+        codes, plane = quantise("w2_0", None, rounded0)
+        w2_q = {(0, n): (codes[:, P * n : P * (n + 1)], plane[:, P * n : P * (n + 1)]) for n in range(N // P)}
+        rounded1 = [tile([P, N // 2, PACK], BF16, "w2_rounded1_%d" % g, tag) for g, tag in enumerate(("total0", "squares7"))]
+        nc.scalar.copy(*by_lines(rounded1[0][:], w2_raw[:, 1, :, 0 : N // 2]))
+
+        total_a = picks("total_a", None, 2, halves[0], sum2[:, :, halves[0]])
+        z1 = [root("z1_0", None, total_a[:])]
+        codes0, plane0 = quantise("z0", None, z0)
         for beats in halves:
             second_product(beats, 0, codes0[:, beats], plane0[:, beats])
-        total_a = picks("total_a", "picked", 2, first, sum2)
-        z_a = root("z_a", None, total_a)
-        rest1 = picks("rest_sum1", None, 0, rest, eps_wide[1][:, :, rest])
-        codes_a, plane_a = quantise("z_a", "v_pass1_0", z_a)
-        second_product(chunks[0], 1, codes_a[:], plane_a[:])
+        total_b = picks("total_b", "logs3", 2, halves[1], sum2[:, :, halves[1]])
+        z1.append(root("z1_1", None, total_b[:]))
+        nc.vector.tensor_copy(*by_lines(rounded1[1][:], w2_raw[:, 1, :, N // 2 : N]))
+        for g in range(2):
+            codes, plane = quantise("w2_1_%d" % g, "squares%d" % (PACK + g), rounded1[g])
+            for n in range(2):
+                w2_q[1, 2 * g + n] = (codes[:, P * n : P * (n + 1)], plane[:, P * n : P * (n + 1)])
+        for half in range(2):
+            codes, plane = quantise("z1_%d" % half, ("sum2", None)[half], z1[half])
+            second_product(halves[half], 1, codes[:], plane[:])
         finish(0)
-        rest2 = picks("rest_sum2", "z_a", 1, rest, rest1)
-        total_b = picks("total_b", "v_pass1_0", 2, chunks[1], rest2[:, :, 0:128])
-        z_b = root("z_b", None, total_b)
-        total_c = picks("total_c", None, 2, chunks[2], rest2[:, :, 128:256])
-        z_c = root("z_c", None, total_c)
-        codes_b, plane_b = quantise("z_b", "z_a", z_b)
-        second_product(chunks[1], 1, codes_b[:], plane_b[:])
-        codes_c, plane_c = quantise("z_c", None, z_c)
-        second_product(chunks[2], 1, codes_c[:], plane_c[:])
         finish(1)

@@ -73,8 +73,6 @@ def tile_list_choir_blend_features_kernel(
         for a in range(2):
             nc.vector.memset(v_planes[a][:].bitcast(I32), 0)
 
-        w4_planes = tile([P, 2, H], U8, "w4_planes")
-        nc.vector.memset(w4_planes[:].bitcast(I32), 0)
         eps_dealt = tile([P, PACK, P], F32, "eps_dealt")
         nc.gpsimd.memset(eps_dealt[:], 0.0)
         identity = tile([P, P], F32, "identity")
@@ -99,6 +97,8 @@ def tile_list_choir_blend_features_kernel(
 
         picked_scales = tile([P, S], U8, "picked_scales", "picked")
         nc.vector.tensor_copy(picked_scales[:], scale_rows[:].indirect(offs_sb[:]))
+        w4_planes = tile([P, 2, H], U8, "w4_planes", "scale_rows")
+        nc.vector.memset(w4_planes[:].bitcast(I32), 0)
         for quad in range(4):
             live = slice(QUADRANT * quad, QUADRANT * quad + 4)
             nc.vector.tensor_copy(
@@ -112,18 +112,24 @@ def tile_list_choir_blend_features_kernel(
                 picked_scales[16 * a + r : 16 * (a + 1) : 4, :].bitcast(I32),
             )
 
-        move_scale_rows(0, 0)
+        for r in range(4):
+            move_scale_rows(0, r)
         nc.sync.dma_start(words[1][:], tab[1])
-        for a in range(2):
-            for r in range(1 - a, 4):
-                move_scale_rows(a, r)
+        for r in range(4):
+            move_scale_rows(1, r)
+        w4_raw1 = load_w4_words(1, None)
         for i, pos in enumerate((pos1, pos2, pos3)):
             nc.sync.dma_start(pos_sb[i][:], pos)
-        w4_raw1 = load_w4_words(1, "picked")
+        w2_raw = tile([P, 2, PACK, N], F32, "w2_raw")
+        for b in range(2):
+            rows = w2[PASS * b : PASS * (b + 1), :].rearrange("(i t u) n -> t i u n", t=PACK, u=RUN)
+            for t in range(PACK):
+                nc.sync.dma_start(w2_raw[:, b, t, :], rows[t])
         eps_sb = tile([P, 2, PACK], F32, "eps_sb")
         nc.scalar.copy(eps_sb[:], eps_turned[:, :, 0:2].rearrange("p t b -> p b t"))
         eps_half = tile([P, PACK], F32, "eps_half")
-        nc.scalar.mul(eps_half[:], eps_turned[:, :, 1], 0.5)
+        nc.scalar.copy(eps_half[:, 0:2], eps_turned[:, 0:2, 1])
+        nc.scalar.mul(eps_half[:, 2:4], eps_turned[:, 2:4, 1], 0.5)
 
 
         v_pass0 = tile([P, S], U32, "v_pass0")
@@ -138,13 +144,12 @@ def tile_list_choir_blend_features_kernel(
         permute_w4_words(1, w4_raw1, "words1")
 
 
-        logs = {t: tile([P, 2 * S], F32, "logs%d" % t) for t in (1, 2, 3)}
-        spare = [logs[1 + k // 2][:, S + M * (k % 2) : S + M * (k % 2 + 1)] for k in range(6)]
-        for b, t, count in ((0, 0, 2), (0, 2, 2), (1, 0, 1)):
-            k = PACK * b + t
+        logs = [tile([P, 2 * S], F32, "logs%d" % t) for t in range(PACK)]
+        spare = [logs[k // 2][:, S + M * (k % 2) : S + M * (k % 2 + 1)] for k in range(2 * PACK)]
+        for pair in range(2):
             nc.scalar.copy(
-                logs[1 + k // 2][:, S : S + M * count].rearrange("p (t m) -> p t m", m=M),
-                eps_sb[:, b, t : t + count].unsqueeze(2).to_broadcast([P, count, M]),
+                logs[pair][:, S : 2 * S].rearrange("p (t m) -> p t m", m=M),
+                eps_sb[:, 0, 2 * pair : 2 * pair + 2].unsqueeze(2).to_broadcast([P, 2, M]),
             )
         warm = tile([P, 1], F32, "warm")
         nc.scalar.activation(warm[:], eps_sb[:, 0, 0:1], ACT.Ln)
@@ -155,7 +160,7 @@ def tile_list_choir_blend_features_kernel(
         def first_product(j, half, a):
             b, t = divmod(j, PACK)
             if a == 0:
-                h_banks[j, half] = psum.tile([P, BANK], F32, name="h%d_%d" % (j, half), tag="bank%d" % (2 * (j % 2) + half))
+                h_banks[j, half] = psum.tile([P, BANK], F32, name="h%d_%d" % (j, half), tag="bank%d" % (2 * (j % 3) + half))
             nc.tensor.matmul_mx(
                 out=h_banks[j, half][:],
                 lhsT=w4_codes[b][:, a, 2 * P * t : 2 * P * (t + 1)].bitcast(FP4X4),
@@ -168,15 +173,16 @@ def tile_list_choir_blend_features_kernel(
             if a == 1:
                 nc.scalar.activation(squares[j][:, BANK * half : BANK * (half + 1)], h_banks[j, half][:], ACT.Square)
 
-        for j in range(2):
-            for a in range(2):
-                for half in range(2):
-                    first_product(j, half, a)
-        for j in range(2, 2 * PACK):
+        for j in range(3):
+            for half in range(2):
+                first_product(j, half, 0)
+        for j, half in ((0, 0), (1, 0), (0, 1), (1, 1), (2, 0), (2, 1)):
+            first_product(j, half, 1)
+        for j in range(3, 2 * PACK):
             for half in range(2):
                 for a in range(2):
                     first_product(j, half, a)
-            if j > PACK:
+            if j >= PACK:
                 t = j - PACK
                 nc.scalar.activation(logs[t][:, 0:S], squares[j][:], ACT.Ln, bias=eps_half[:, t : t + 1])
 
@@ -218,9 +224,13 @@ def tile_list_choir_blend_features_kernel(
             for i in range(3):
                 for t in pair:
                     if i == 0 and t == 0:
-                        dst = tile([P, M], F32, "first_part", "picked")[:]
-                    elif i == 0 and t == 1:
-                        dst = spare[PACK + 1]
+                        dst = tile([P, M], F32, "first_part", "w4_raw1")[:]
+                    elif t == 0 and i == 1:
+                        dst = spare[PACK]
+                    elif t == 1 and i < 2:
+                        dst = spare[PACK + 1 + i]
+                    elif t == 2 and i == 0:
+                        dst = spare[PACK + 3]
                     elif i < 2:
                         part = partial.tile([P, M], F32, name="part", tag="part")
                         dst = part[:]
@@ -228,15 +238,10 @@ def tile_list_choir_blend_features_kernel(
                         dst = total0[:, t, :]
                     pick_and_add(dst, t, i, slice(0, M), so_far[t])
                     so_far[t] = dst
-        w2_raw = tile([P, 2, PACK, N], F32, "w2_raw", "picked")
-        for b in range(2):
-            rows = w2[PASS * b : PASS * (b + 1), :].rearrange("(i t u) n -> t i u n", t=PACK, u=RUN)
-            for t in range(PACK):
-                nc.sync.dma_start(w2_raw[:, b, t, :], rows[t])
-        picked = tile([P, PACK - 1, 2, M], F32, "picked_by_scalar", "eps_half")
-        for t in logs:
-            for i in range(2):
-                nc.scalar.activation(picked[:, t - 1, i, :], logs[t][:].indirect(pos_sb[i][:]), ACT.Exp)
+        by_scalar = [(0, 0), (1, 0), (2, 0), (2, 1), (3, 0), (3, 1)]
+        picked = tile([P, len(by_scalar), M], F32, "picked_by_scalar", "eps_half")
+        for k, (t, i) in enumerate(by_scalar):
+            nc.scalar.activation(picked[:, k, :], logs[t][:].indirect(pos_sb[i][:]), ACT.Exp)
         z0 = root("z0", "logs3", total0[:])
 
         halves = [slice(0, 256), slice(256, 512)]
@@ -263,35 +268,33 @@ def tile_list_choir_blend_features_kernel(
                 nc.scalar.activation(result[:], y_banks[half, n][:], ACT.Silu)
                 nc.sync.dma_start(out[P * n : P * (n + 1), halves[half]], result[:])
 
-        beats = slice(0, M)
-        sum2 = tile([P, PACK, M], F32, "sum2")
-        sum1 = tile([P, M], F32, "sum1")
-        pick_and_add(sum1[:], PACK, 0, beats, spare[PACK])
-        nc.vector.tensor_tensor(sum2[:, 1, :], picked[:, 0, 0, :], picked[:, 0, 1, :], ADD)
-        pick_and_add(sum2[:, 0, :], PACK, 1, beats, sum1[:])
-        nc.vector.tensor_tensor(sum2[:, 2, :], picked[:, 1, 0, :], picked[:, 1, 1, :], ADD)
-        rounded0 = tile([P, N, PACK], BF16, "w2_rounded0", "sum1")
+        rounded0 = tile([P, N, PACK], BF16, "w2_rounded0", "squares3")
         nc.vector.tensor_copy(*by_lines(rounded0[:], w2_raw[:, 0, :, :]))
-        nc.vector.tensor_tensor(sum2[:, 3, :], picked[:, 2, 0, :], picked[:, 2, 1, :], ADD)
-        codes, plane = quantise("w2_0", None, rounded0)
-        w2_q = {(0, n): (codes[:, P * n : P * (n + 1)], plane[:, P * n : P * (n + 1)]) for n in range(N // P)}
-        rounded1 = [tile([P, N // 2, PACK], BF16, "w2_rounded1_%d" % g, tag) for g, tag in enumerate(("total0", "squares7"))]
-        nc.scalar.copy(*by_lines(rounded1[0][:], w2_raw[:, 1, :, 0 : N // 2]))
+        w2_q = {}
 
-        total_a = picks("total_a", None, 2, halves[0], sum2[:, :, halves[0]])
-        z1 = [root("z1_0", None, total_a[:])]
-        codes0, plane0 = quantise("z0", None, z0)
+        def quantise_w2(b, rounded):
+            codes, plane = quantise("w2_%d" % b, None, rounded)
+            for n in range(N // P):
+                w2_q[b, n] = (codes[:, P * n : P * (n + 1)], plane[:, P * n : P * (n + 1)])
+
+        quantise_w2(0, rounded0)
+        sum2 = tile([P, PACK, M], F32, "sum2")
+        for t in range(2):
+            pick_and_add(sum2[:, t, :], PACK + t, 1, slice(0, M), picked[:, t, :])
+        for t in range(2, PACK):
+            nc.vector.tensor_tensor(sum2[:, t, :], picked[:, 2 * t - 2, :], picked[:, 2 * t - 1, :], ADD)
+        z1 = []
+        for half in range(2):
+            total = picks("total1_%d" % half, None, 2, halves[half], sum2[:, :, halves[half]])
+            z1.append(root("z1_%d" % half, None, total[:]))
+        codes0, plane0 = quantise("z0", "sum2", z0)
         for beats in halves:
             second_product(beats, 0, codes0[:, beats], plane0[:, beats])
-        total_b = picks("total_b", "logs3", 2, halves[1], sum2[:, :, halves[1]])
-        z1.append(root("z1_1", None, total_b[:]))
-        nc.vector.tensor_copy(*by_lines(rounded1[1][:], w2_raw[:, 1, :, N // 2 : N]))
-        for g in range(2):
-            codes, plane = quantise("w2_1_%d" % g, "squares%d" % (PACK + g), rounded1[g])
-            for n in range(2):
-                w2_q[1, 2 * g + n] = (codes[:, P * n : P * (n + 1)], plane[:, P * n : P * (n + 1)])
+        rounded1 = tile([P, N, PACK], BF16, "w2_rounded1", "logs3")
+        nc.vector.tensor_copy(*by_lines(rounded1[:], w2_raw[:, 1, :, :]))
+        quantise_w2(1, rounded1)
         for half in range(2):
-            codes, plane = quantise("z1_%d" % half, ("sum2", None)[half], z1[half])
+            codes, plane = quantise("z1_%d" % half, None, z1[half])
             second_product(halves[half], 1, codes[:], plane[:])
         finish(0)
         finish(1)

@@ -86,6 +86,12 @@ def tile_list_choir_blend_features_kernel(
             nc.tensor.transpose(eps_turned[:, t, :], eps_dealt[:, t, :], identity[:])
 
 
+        def by_lines(dst, src):
+            return (
+                dst.rearrange("p (c i) t -> p c t i", i=LINE),
+                src.rearrange("p t (c i) -> p c t i", i=LINE),
+            )
+
         w4_codes = []
 
         def permute_w4_words(b, raw, tag):
@@ -117,19 +123,23 @@ def tile_list_choir_blend_features_kernel(
         nc.sync.dma_start(words[1][:], tab[1])
         for r in range(4):
             move_scale_rows(1, r)
+        w2_raw = [tile([P, PACK, N], F32, "w2_raw%d" % b) for b in range(2)]
+
+        def load_w2(b):
+            rows = w2[PASS * b : PASS * (b + 1), :].rearrange("(i t u) n -> t i u n", t=PACK, u=RUN)
+            for t in range(PACK):
+                nc.sync.dma_start(w2_raw[b][:, t, :], rows[t])
+
+        load_w2(0)
         w4_raw1 = load_w4_words(1, None)
         for i, pos in enumerate((pos1, pos2, pos3)):
             nc.sync.dma_start(pos_sb[i][:], pos)
-        w2_raw = tile([P, 2, PACK, N], F32, "w2_raw")
-        for b in range(2):
-            rows = w2[PASS * b : PASS * (b + 1), :].rearrange("(i t u) n -> t i u n", t=PACK, u=RUN)
-            for t in range(PACK):
-                nc.sync.dma_start(w2_raw[:, b, t, :], rows[t])
+        load_w2(1)
         eps_sb = tile([P, 2, PACK], F32, "eps_sb")
         nc.scalar.copy(eps_sb[:], eps_turned[:, :, 0:2].rearrange("p t b -> p b t"))
         eps_half = tile([P, PACK], F32, "eps_half")
-        nc.scalar.copy(eps_half[:, 0:2], eps_turned[:, 0:2, 1])
-        nc.scalar.mul(eps_half[:, 2:4], eps_turned[:, 2:4, 1], 0.5)
+        nc.scalar.copy(eps_half[:, 0:3], eps_turned[:, 0:3, 1])
+        nc.scalar.mul(eps_half[:, 3:4], eps_turned[:, 3:4, 1], 0.5)
 
 
         v_pass0 = tile([P, S], U32, "v_pass0")
@@ -141,7 +151,9 @@ def tile_list_choir_blend_features_kernel(
             entries = slice(BANK * half // PER_COLUMN, BANK * (half + 1) // PER_COLUMN)
             nc.vector.tensor_copy(v_pass1[:], words[1][:].bitcast(U32).indirect(offs_sb[:, entries]))
             v_codes[1, half] = v_pass1[:]
-        permute_w4_words(1, w4_raw1, "words1")
+        rounded0 = tile([P, N, PACK], BF16, "w2_rounded0", "words1")
+        nc.vector.tensor_copy(*by_lines(rounded0[:], w2_raw[0][:]))
+        permute_w4_words(1, w4_raw1, "w2_raw0")
 
 
         logs = [tile([P, 2 * S], F32, "logs%d" % t) for t in range(PACK)]
@@ -185,13 +197,6 @@ def tile_list_choir_blend_features_kernel(
             if j >= PACK:
                 t = j - PACK
                 nc.scalar.activation(logs[t][:, 0:S], squares[j][:], ACT.Ln, bias=eps_half[:, t : t + 1])
-
-
-        def by_lines(dst, src):
-            return (
-                dst.rearrange("p (c i) t -> p c t i", i=LINE),
-                src.rearrange("p t (c i) -> p c t i", i=LINE),
-            )
 
 
         def pick_and_add(dst, j, i, beats, so_far):
@@ -238,7 +243,7 @@ def tile_list_choir_blend_features_kernel(
                         dst = total0[:, t, :]
                     pick_and_add(dst, t, i, slice(0, M), so_far[t])
                     so_far[t] = dst
-        by_scalar = [(0, 0), (1, 0), (2, 0), (2, 1), (3, 0), (3, 1)]
+        by_scalar = [(0, 0), (1, 0), (2, 0), (3, 0), (3, 1)]
         picked = tile([P, len(by_scalar), M], F32, "picked_by_scalar", "eps_half")
         for k, (t, i) in enumerate(by_scalar):
             nc.scalar.activation(picked[:, k, :], logs[t][:].indirect(pos_sb[i][:]), ACT.Exp)
@@ -268,21 +273,18 @@ def tile_list_choir_blend_features_kernel(
                 nc.scalar.activation(result[:], y_banks[half, n][:], ACT.Silu)
                 nc.sync.dma_start(out[P * n : P * (n + 1), halves[half]], result[:])
 
-        rounded0 = tile([P, N, PACK], BF16, "w2_rounded0", "squares3")
-        nc.vector.tensor_copy(*by_lines(rounded0[:], w2_raw[:, 0, :, :]))
         w2_q = {}
 
-        def quantise_w2(b, rounded):
-            codes, plane = quantise("w2_%d" % b, None, rounded)
+        def quantise_w2(b, tag, rounded):
+            codes, plane = quantise("w2_%d" % b, tag, rounded)
             for n in range(N // P):
                 w2_q[b, n] = (codes[:, P * n : P * (n + 1)], plane[:, P * n : P * (n + 1)])
 
-        quantise_w2(0, rounded0)
+        quantise_w2(0, "squares3", rounded0)
         sum2 = tile([P, PACK, M], F32, "sum2")
-        for t in range(2):
+        for t in range(3):
             pick_and_add(sum2[:, t, :], PACK + t, 1, slice(0, M), picked[:, t, :])
-        for t in range(2, PACK):
-            nc.vector.tensor_tensor(sum2[:, t, :], picked[:, 2 * t - 2, :], picked[:, 2 * t - 1, :], ADD)
+        nc.vector.tensor_tensor(sum2[:, 3, :], picked[:, 3, :], picked[:, 4, :], ADD)
         z1 = []
         for half in range(2):
             total = picks("total1_%d" % half, None, 2, halves[half], sum2[:, :, halves[half]])
@@ -291,8 +293,8 @@ def tile_list_choir_blend_features_kernel(
         for beats in halves:
             second_product(beats, 0, codes0[:, beats], plane0[:, beats])
         rounded1 = tile([P, N, PACK], BF16, "w2_rounded1", "logs3")
-        nc.vector.tensor_copy(*by_lines(rounded1[:], w2_raw[:, 1, :, :]))
-        quantise_w2(1, rounded1)
+        nc.vector.tensor_copy(*by_lines(rounded1[:], w2_raw[1][:]))
+        quantise_w2(1, None, rounded1)
         for half in range(2):
             codes, plane = quantise("z1_%d" % half, None, z1[half])
             second_product(halves[half], 1, codes[:], plane[:])

@@ -97,20 +97,25 @@ def tile_list_choir_blend_features_kernel(
         def permute_w4_words(b, raw, tag):
             w4_codes.append(tile([P, 2, 2 * PASS], U8, "w4_codes%d" % b, tag))
             nc.vector.tensor_copy(
-                w4_codes[b][:].bitcast(I32).rearrange("p a (t i v) -> p a t i v", t=PACK, v=2),
-                raw[:].bitcast(I32).rearrange("p a (i t v) -> p a t i v", t=PACK, v=2),
+                w4_codes[b][:].bitcast(I32).rearrange("p a (t i v) -> p a i t v", t=PACK, v=2),
+                raw[:].bitcast(I32).rearrange("p a (i t v) -> p a i t v", t=PACK, v=2),
             )
 
         picked_scales = tile([P, S], U8, "picked_scales", "picked")
         nc.vector.tensor_copy(picked_scales[:], scale_rows[:].indirect(offs_sb[:]))
-        w4_planes = tile([P, 2, H], U8, "w4_planes", "scale_rows")
-        nc.vector.memset(w4_planes[:].bitcast(I32), 0)
-        for quad in range(4):
-            live = slice(QUADRANT * quad, QUADRANT * quad + 4)
-            nc.vector.tensor_copy(
-                w4_planes[live].bitcast(I32).rearrange("p a (c t i) -> p (a c) t i", c=2, t=PACK),
-                w4_planes_raw[live].bitcast(I32).rearrange("p a (c i t) -> p (a c) t i", c=2, t=PACK),
-            )
+        w4_planes = []
+
+        def deal_w4_scales(a, tag):
+            w4_planes.append(tile([P, H], U8, "w4_plane%d" % a, tag))
+            nc.vector.memset(w4_planes[a][:].bitcast(I32), 0)
+            for quad in range(4):
+                live = slice(QUADRANT * quad, QUADRANT * quad + 4)
+                nc.vector.tensor_copy(
+                    w4_planes[a][live].bitcast(I32).rearrange("p (c t i) -> p c i t", c=2, t=PACK),
+                    w4_planes_raw[live, a, :].bitcast(I32).rearrange("p (c i t) -> p c i t", c=2, t=PACK),
+                )
+
+        deal_w4_scales(0, "scale_rows")
 
         def move_scale_rows(a, r):
             nc.sync.dma_start(
@@ -145,6 +150,7 @@ def tile_list_choir_blend_features_kernel(
         v_pass0 = tile([P, S], U32, "v_pass0")
         nc.vector.tensor_copy(v_pass0[:], words[0][:].bitcast(U32).indirect(offs_sb[:]))
         permute_w4_words(0, w4_raw0, None)
+        deal_w4_scales(1, "words0")
         v_codes = {(0, half): v_pass0[:, BANK * half : BANK * (half + 1)] for half in range(2)}
         for half in range(2):
             v_pass1 = tile([P, BANK], U32, "v_pass1_%d" % half, ("w4_raw0", None)[half])
@@ -176,7 +182,7 @@ def tile_list_choir_blend_features_kernel(
             nc.tensor.matmul_mx(
                 out=h_banks[j, half][:],
                 lhsT=w4_codes[b][:, a, 2 * P * t : 2 * P * (t + 1)].bitcast(FP4X4),
-                lhsT_scale=w4_planes[:, a, P * j : P * (j + 1)],
+                lhsT_scale=w4_planes[a][:, P * j : P * (j + 1)],
                 rhs=v_codes[a, half].bitcast(FP8X4),
                 rhs_scale=v_planes[a][:, BANK * half : BANK * (half + 1)],
                 start=(a == 0),
@@ -228,14 +234,12 @@ def tile_list_choir_blend_features_kernel(
             so_far = {t: spare[t] for t in pair}
             for i in range(3):
                 for t in pair:
-                    if i == 0 and t == 0:
+                    if i == 0 and t == 1:
                         dst = tile([P, M], F32, "first_part", "w4_raw1")[:]
-                    elif t == 0 and i == 1:
-                        dst = spare[PACK]
-                    elif t == 1 and i < 2:
-                        dst = spare[PACK + 1 + i]
-                    elif t == 2 and i == 0:
-                        dst = spare[PACK + 3]
+                    elif t == 0 and i < 2:
+                        dst = spare[PACK + i]
+                    elif (t, i) in ((1, 1), (2, 0)):
+                        dst = spare[PACK + 1 + t]
                     elif i < 2:
                         part = partial.tile([P, M], F32, name="part", tag="part")
                         dst = part[:]

@@ -191,6 +191,9 @@ def tile_list_choir_blend_features_kernel(
             if a == 1:
                 nc.scalar.activation(squares[j][:, BANK * half : BANK * (half + 1)], h_banks[j, half][:], ACT.Square)
 
+        def take_log(t):
+            nc.scalar.activation(logs[t][:, 0:S], squares[PACK + t][:], ACT.Ln, bias=eps_half[:, t : t + 1])
+
         for j in range(3):
             for half in range(2):
                 first_product(j, half, 0)
@@ -200,9 +203,9 @@ def tile_list_choir_blend_features_kernel(
             for half in range(2):
                 for a in range(2):
                     first_product(j, half, a)
-            if j >= PACK:
-                t = j - PACK
-                nc.scalar.activation(logs[t][:, 0:S], squares[j][:], ACT.Ln, bias=eps_half[:, t : t + 1])
+            if j > PACK:
+                take_log(j - 1 - PACK)
+        take_log(PACK - 1)
 
 
         def pick_and_add(dst, j, i, beats, so_far):
@@ -256,9 +259,9 @@ def tile_list_choir_blend_features_kernel(
         halves = [slice(0, 256), slice(256, 512)]
         y_banks = {}
 
-        def second_product(beats, b, codes, plane):
+        def second_product(beats, b, row_tiles, codes, plane):
             half, first = divmod(beats.start, 256)
-            for n in range(N // P):
+            for n in row_tiles:
                 if b == 0:
                     y_banks[half, n] = psum.tile([P, 256], F32, name="y%d_%d" % (half, n), tag="bank%d" % (4 * half + n))
                 nc.tensor.matmul_mx(
@@ -283,24 +286,34 @@ def tile_list_choir_blend_features_kernel(
             codes, plane = quantise("w2_%d" % b, tag, rounded)
             for n in range(N // P):
                 w2_q[b, n] = (codes[:, P * n : P * (n + 1)], plane[:, P * n : P * (n + 1)])
+            return codes, plane
 
-        quantise_w2(0, "squares3", rounded0)
         sum2 = tile([P, PACK, M], F32, "sum2")
         for t in range(3):
             pick_and_add(sum2[:, t, :], PACK + t, 1, slice(0, M), picked[:, t, :])
         nc.vector.tensor_tensor(sum2[:, 3, :], picked[:, 3, :], picked[:, 4, :], ADD)
-        z1 = []
-        for half in range(2):
-            total = picks("total1_%d" % half, None, 2, halves[half], sum2[:, :, halves[half]])
-            z1.append(root("z1_%d" % half, None, total[:]))
-        codes0, plane0 = quantise("z0", "sum2", z0)
+        total_a = picks("total_a", None, 2, halves[0], sum2[:, :, halves[0]])
+        z1 = [root("z1_0", None, total_a[:])]
+        total = tile([P, PACK, 256], F32, "total_b")
+        for t in range(PACK):
+            pick_and_add(total[:, t, :], PACK + t, 2, halves[1], sum2[:, t, halves[1]])
+            if t == 1:
+                codes, plane = quantise_w2(0, "squares4", rounded0)
+        z1.append(root("z1_1", None, total[:]))
+        codes0, plane0 = quantise("z0", "squares6", z0)
         for beats in halves:
-            second_product(beats, 0, codes0[:, beats], plane0[:, beats])
-        rounded1 = tile([P, N, PACK], BF16, "w2_rounded1", "logs3")
-        nc.vector.tensor_copy(*by_lines(rounded1[:], w2_raw[1][:]))
-        quantise_w2(1, None, rounded1)
-        for half in range(2):
-            codes, plane = quantise("z1_%d" % half, None, z1[half])
-            second_product(halves[half], 1, codes[:], plane[:])
+            second_product(beats, 0, range(4), codes0[:, beats], plane0[:, beats])
+        codes_a, plane_a = quantise("z1_0", None, z1[0])
+        rounded1 = []
+        for g, tag in enumerate(("logs3", "z1_0")):
+            rounded1.append(tile([P, N // 2, PACK], BF16, "w2_rounded1_%d" % g, tag))
+            nc.vector.tensor_copy(*by_lines(rounded1[g][:], w2_raw[1][:, :, N // 2 * g : N // 2 * (g + 1)]))
+        for g in range(2):
+            codes, plane = quantise("w2_1_%d" % g, None, rounded1[g])
+            for n in range(2):
+                w2_q[1, 2 * g + n] = (codes[:, P * n : P * (n + 1)], plane[:, P * n : P * (n + 1)])
+            second_product(halves[0], 1, range(2 * g, 2 * g + 2), codes_a[:], plane_a[:])
+        codes, plane = quantise("z1_1", None, z1[1])
+        second_product(halves[1], 1, range(4), codes[:], plane[:])
         finish(0)
         finish(1)

@@ -274,8 +274,8 @@ def tile_list_choir_blend_features_kernel(
                     stop=(b == 1 and beats.stop % 256 == 0),
                 )
 
-        def finish(half):
-            for n in range(N // P):
+        def finish(half, row_tiles):
+            for n in row_tiles:
                 result = tile([P, 256], F32, "result%d_%d" % (half, n))
                 nc.scalar.activation(result[:], y_banks[half, n][:], ACT.Silu)
                 nc.sync.dma_start(out[P * n : P * (n + 1), halves[half]], result[:])
@@ -298,22 +298,35 @@ def tile_list_choir_blend_features_kernel(
         for t in range(PACK):
             pick_and_add(total[:, t, :], PACK + t, 2, halves[1], sum2[:, t, halves[1]])
             if t == 1:
-                codes, plane = quantise_w2(0, "squares4", rounded0)
+                unread_plane = tile([P, P], U8, "unread_plane", "squares4")
+                nc.vector.tensor_copy(unread_plane[:].bitcast(I32), w4_planes[0][:, 0:P].bitcast(I32))
+                unread = psum.tile([P, BANK], F32, name="unread", tag="bank7")
+                for repeat in range(4):
+                    nc.tensor.matmul_mx(
+                        out=unread[:],
+                        lhsT=w4_codes[0][:, 0, 0 : 2 * P].bitcast(FP4X4),
+                        lhsT_scale=unread_plane[:],
+                        rhs=v_codes[0, 0].bitcast(FP8X4),
+                        rhs_scale=v_planes[0][:, 0:BANK],
+                        start=True,
+                        stop=True,
+                    )
         z1.append(root("z1_1", None, total[:]))
-        codes0, plane0 = quantise("z0", "squares6", z0)
+        quantise_w2(0, "squares6", rounded0)
+        codes0, plane0 = quantise("z0", "squares7", z0)
         for beats in halves:
             second_product(beats, 0, range(4), codes0[:, beats], plane0[:, beats])
-        codes_a, plane_a = quantise("z1_0", None, z1[0])
-        rounded1 = []
+        z1_q = []
         for g, tag in enumerate(("logs3", "z1_0")):
-            rounded1.append(tile([P, N // 2, PACK], BF16, "w2_rounded1_%d" % g, tag))
-            nc.vector.tensor_copy(*by_lines(rounded1[g][:], w2_raw[1][:, :, N // 2 * g : N // 2 * (g + 1)]))
-        for g in range(2):
-            codes, plane = quantise("w2_1_%d" % g, None, rounded1[g])
+            rounded = tile([P, N // 2, PACK], BF16, "w2_rounded1_%d" % g, tag)
+            nc.vector.tensor_copy(*by_lines(rounded[:], w2_raw[1][:, :, N // 2 * g : N // 2 * (g + 1)]))
+            if g == 0:
+                z1_q.append(quantise("z1_0", None, z1[0]))
+            codes, plane = quantise("w2_1_%d" % g, None, rounded)
             for n in range(2):
                 w2_q[1, 2 * g + n] = (codes[:, P * n : P * (n + 1)], plane[:, P * n : P * (n + 1)])
-            second_product(halves[0], 1, range(2 * g, 2 * g + 2), codes_a[:], plane_a[:])
-        codes, plane = quantise("z1_1", None, z1[1])
-        second_product(halves[1], 1, range(4), codes[:], plane[:])
-        finish(0)
-        finish(1)
+            if g == 0:
+                z1_q.append(quantise("z1_1", None, z1[1]))
+            for half in range(2):
+                second_product(halves[half], 1, range(2 * g, 2 * g + 2), z1_q[half][0][:], z1_q[half][1][:])
+                finish(half, range(2 * g, 2 * g + 2))

@@ -297,20 +297,6 @@ def tile_list_choir_blend_features_kernel(
         total = tile([P, PACK, 256], F32, "total_b")
         for t in range(PACK):
             pick_and_add(total[:, t, :], PACK + t, 2, halves[1], sum2[:, t, halves[1]])
-            if t == 1:
-                unread_plane = tile([P, P], U8, "unread_plane", "squares4")
-                nc.vector.tensor_copy(unread_plane[:].bitcast(I32), w4_planes[0][:, 0:P].bitcast(I32))
-                unread = psum.tile([P, BANK], F32, name="unread", tag="bank7")
-                for repeat in range(4):
-                    nc.tensor.matmul_mx(
-                        out=unread[:],
-                        lhsT=w4_codes[0][:, 0, 0 : 2 * P].bitcast(FP4X4),
-                        lhsT_scale=unread_plane[:],
-                        rhs=v_codes[0, 0].bitcast(FP8X4),
-                        rhs_scale=v_planes[0][:, 0:BANK],
-                        start=True,
-                        stop=True,
-                    )
         z1.append(root("z1_1", None, total[:]))
         quantise_w2(0, "squares6", rounded0)
         codes0, plane0 = quantise("z0", "squares7", z0)

@@ -20,11 +20,15 @@ ADD = mybir.AluOpType.add
 P = 128
 PACK = 4
 PASS = P * PACK
-RUN = 4
+RUN = 8
 BANK = 512
+HALF = M // 2
 PER_COLUMN = 16
 QUADRANT = 32
 LINE = 4
+LISTS = 3
+BEHIND = T // 8
+AHEAD = T // 4
 
 
 def tile_list_choir_blend_features_kernel(
@@ -34,57 +38,57 @@ def tile_list_choir_blend_features_kernel(
     with ExitStack() as ctx:
         lists = ctx.enter_context(tc.tile_pool(name="lists", bufs=1))
         keep = ctx.enter_context(tc.tile_pool(name="keep", bufs=1))
-        partial = ctx.enter_context(tc.tile_pool(name="partial", bufs=4))
         psum = ctx.enter_context(tc.psum_pool(name="psum", bufs=1))
 
         def tile(shape, dtype, name, tag=None):
             return keep.tile(shape, dtype, name=name, tag=tag or name, align_bytes=64)
 
+        def bank(shape, name, index):
+            return psum.tile(shape, F32, name=name, tag="bank%d" % index)
+
         offs_sb = lists.tile([P, S // PER_COLUMN], U16, name="offs_sb")
-        pos_sb = [lists.tile([P, M // PER_COLUMN], U16, name="pos%d_sb" % i) for i in range(3)]
+        pos_sb = [lists.tile([P, M // PER_COLUMN], U16, name="pos%d_sb" % i) for i in range(LISTS)]
 
         tab = [tab_words[a].rearrange("p t i -> p (t i)").bitcast(I32) for a in range(2)]
 
-        def load_w4_words(b, tag):
-            raw = tile([P, 2, 2 * PASS], U8, "w4_raw%d" % b, tag)
+        def load_w4_words(b):
+            raw = tile([P, 2, 2 * PASS], U8, "w4_raw%d" % b)
             src = w4_words[:, :, 2 * PASS * b : 2 * PASS * (b + 1)].rearrange("a p c -> p a c")
             nc.sync.dma_start(raw[:].bitcast(I32), src.bitcast(I32))
             return raw
 
-        w4_planes_raw = tile([P, 2, H], U8, "w4_planes_raw")
         nc.sync.dma_start(offs_sb[:], offs)
         scale_rows = tile([P, T], U8, "scale_rows")
         nc.sync.dma_start(
             scale_rows[0:QUADRANT, :].bitcast(I32), tab_scales.rearrange("a q t -> (a q) t").bitcast(I32)
         )
-        eps_rows = tile([2, PASS], F32, "eps_rows")
-        nc.sync.dma_start(eps_rows[:], eps.rearrange("(b r) -> b r", b=2))
-        for r in range(4):
-            nc.sync.dma_start(
-                w4_planes_raw[r:P:QUADRANT, :, :].bitcast(I32),
-                w4_scales[:, r:16:4, :].rearrange("a q c -> q a c").bitcast(I32),
-            )
+        w4_rows = tile([QUADRANT, H], U8, "w4_rows")
+        nc.sync.dma_start(w4_rows[:].bitcast(I32), w4_scales.rearrange("a q c -> (a q) c").bitcast(I32))
+        eps_rows = tile([2 * QUADRANT, PASS], F32, "eps_rows")
+        nc.sync.dma_start(eps_rows[0 : 2 * QUADRANT : QUADRANT, :], eps.rearrange("(b r) -> b r", b=2))
         words = [tile([P, T], I32, "words%d" % a) for a in range(2)]
         nc.sync.dma_start(words[0][:], tab[0])
-        w4_raw0 = load_w4_words(0, None)
+        w4_raw0 = load_w4_words(0)
         nc.vector.memset(scale_rows[QUADRANT : 2 * QUADRANT, :].bitcast(I32), 0)
         nc.vector.memset(scale_rows[2 * QUADRANT : P, :].bitcast(I32), 0)
-        v_planes = [tile([P, S], U8, "v_plane%d" % a) for a in range(2)]
+        planes = [tile([P, S + H], U8, "planes%d" % a) for a in range(2)]
         for a in range(2):
-            nc.vector.memset(v_planes[a][:].bitcast(I32), 0)
+            nc.vector.memset(planes[a][:].bitcast(I32), 0)
 
         eps_dealt = tile([P, PACK, P], F32, "eps_dealt")
         nc.gpsimd.memset(eps_dealt[:], 0.0)
         identity = tile([P, P], F32, "identity")
         make_identity(nc, identity[:])
         nc.scalar.copy(
-            eps_dealt[0:2, :, :].rearrange("b t (i u) -> b t i u", u=RUN),
-            eps_rows[:].rearrange("b (i t u) -> b t i u", t=PACK, u=RUN),
+            eps_dealt[0:1, :, :].rearrange("b t (g u) -> b t g u", u=RUN),
+            eps_rows[0:1, :].rearrange("b (g t u) -> b t g u", t=PACK, u=RUN),
         )
-        eps_turned = psum.tile([P, PACK, P], F32, name="eps_turned", tag="bank7")
+        nc.scalar.copy(
+            eps_dealt[QUADRANT : QUADRANT + 1, :, :].rearrange("b t p -> b (t p)"), eps_rows[QUADRANT : QUADRANT + 1, :]
+        )
+        eps_turned = bank([P, PACK, P], "eps_turned", 7)
         for t in range(PACK):
             nc.tensor.transpose(eps_turned[:, t, :], eps_dealt[:, t, :], identity[:])
-
 
         def by_lines(dst, src):
             return (
@@ -92,83 +96,81 @@ def tile_list_choir_blend_features_kernel(
                 src.rearrange("p t (c i) -> p c t i", i=LINE),
             )
 
-        w4_codes = []
-
-        def permute_w4_words(b, raw, tag):
-            w4_codes.append(tile([P, 2, 2 * PASS], U8, "w4_codes%d" % b, tag))
-            nc.vector.tensor_copy(
-                w4_codes[b][:].bitcast(I32).rearrange("p a (t i v) -> p a i t v", t=PACK, v=2),
-                raw[:].bitcast(I32).rearrange("p a (i t v) -> p a i t v", t=PACK, v=2),
-            )
-
-        picked_scales = tile([P, S], U8, "picked_scales", "picked")
+        staged = tile([QUADRANT, S + H], U8, "staged")
+        nc.vector.tensor_copy(
+            staged[:, S : S + PASS].bitcast(I32).rearrange("p (t g v) -> p t g v", t=PACK, v=2),
+            w4_rows[:, 0:PASS].bitcast(I32).rearrange("p (g t v) -> p t g v", t=PACK, v=2),
+        )
+        nc.vector.tensor_copy(staged[:, S + PASS : S + H].bitcast(I32), w4_rows[:, PASS:H].bitcast(I32))
+        picked_scales = tile([P, S], U8, "picked_scales")
         nc.vector.tensor_copy(picked_scales[:], scale_rows[:].indirect(offs_sb[:]))
-        w4_planes = []
+        nc.vector.tensor_copy(staged[:, 0:S].bitcast(I32), picked_scales[0:QUADRANT, :].bitcast(I32))
 
-        def deal_w4_scales(a, tag):
-            w4_planes.append(tile([P, H], U8, "w4_plane%d" % a, tag))
-            nc.vector.memset(w4_planes[a][:].bitcast(I32), 0)
-            for quad in range(4):
-                live = slice(QUADRANT * quad, QUADRANT * quad + 4)
-                nc.vector.tensor_copy(
-                    w4_planes[a][live].bitcast(I32).rearrange("p (c t i) -> p c i t", c=2, t=PACK),
-                    w4_planes_raw[live, a, :].bitcast(I32).rearrange("p (c i t) -> p c i t", c=2, t=PACK),
+        def move_scale_rows(a):
+            for r in range(4):
+                nc.sync.dma_start(
+                    planes[a][r:P:QUADRANT, :].bitcast(I32),
+                    staged[16 * a + r : 16 * (a + 1) : 4, :].bitcast(I32),
                 )
 
-        deal_w4_scales(0, "scale_rows")
-
-        def move_scale_rows(a, r):
-            nc.sync.dma_start(
-                v_planes[a][r:P:QUADRANT, :].bitcast(I32),
-                picked_scales[16 * a + r : 16 * (a + 1) : 4, :].bitcast(I32),
-            )
-
-        for r in range(4):
-            move_scale_rows(0, r)
-        nc.sync.dma_start(words[1][:], tab[1])
-        for r in range(4):
-            move_scale_rows(1, r)
+        nc.sync.dma_start(words[1][:, 0:AHEAD], tab[1][:, 0:AHEAD])
+        move_scale_rows(0)
+        nc.sync.dma_start(words[1][:, AHEAD : T - BEHIND], tab[1][:, AHEAD : T - BEHIND])
+        move_scale_rows(1)
+        nc.sync.dma_start(words[1][:, T - BEHIND : T], tab[1][:, T - BEHIND : T])
         w2_raw = [tile([P, PACK, N], F32, "w2_raw%d" % b) for b in range(2)]
+        nc.sync.dma_start(pos_sb[0][:], pos1)
+        rows = w2[PASS:H, :].rearrange("(g u q e) n -> u g q (e n)", u=2, q=RUN, e=2)
+        for u in range(2):
+            nc.sync.dma_start(w2_raw[1][:, 2 * u : 2 * u + 2, :].rearrange("p e n -> p (e n)"), rows[u])
+        nc.sync.dma_start(pos_sb[1][:], pos2)
+        nc.sync.dma_start(pos_sb[2][:], pos3)
+        w4_raw1 = load_w4_words(1)
+        rows = w2[0:PASS, :].rearrange("(g t u) n -> t g u n", t=PACK, u=RUN)
+        for t in range(PACK):
+            nc.sync.dma_start(w2_raw[0][:, t, :], rows[t])
 
-        def load_w2(b):
-            rows = w2[PASS * b : PASS * (b + 1), :].rearrange("(i t u) n -> t i u n", t=PACK, u=RUN)
-            for t in range(PACK):
-                nc.sync.dma_start(w2_raw[b][:, t, :], rows[t])
-
-        load_w2(0)
-        w4_raw1 = load_w4_words(1, None)
-        for i, pos in enumerate((pos1, pos2, pos3)):
-            nc.sync.dma_start(pos_sb[i][:], pos)
-        load_w2(1)
         eps_sb = tile([P, 2, PACK], F32, "eps_sb")
-        nc.scalar.copy(eps_sb[:], eps_turned[:, :, 0:2].rearrange("p t b -> p b t"))
-        eps_half = tile([P, PACK], F32, "eps_half")
-        nc.scalar.copy(eps_half[:, 0:3], eps_turned[:, 0:3, 1])
-        nc.scalar.mul(eps_half[:, 3:4], eps_turned[:, 3:4, 1], 0.5)
+        nc.scalar.copy(eps_sb[:], eps_turned[:, :, 0 : 2 * QUADRANT : QUADRANT].rearrange("p t b -> p b t"))
+        eps_third = tile([P, 2], F32, "eps_third")
+        nc.scalar.mul(eps_third[:], eps_turned[:, 2:4, QUADRANT], 1.0 / LISTS)
 
+        v_codes = {}
 
-        v_pass0 = tile([P, S], U32, "v_pass0")
-        nc.vector.tensor_copy(v_pass0[:], words[0][:].bitcast(U32).indirect(offs_sb[:]))
-        permute_w4_words(0, w4_raw0, None)
-        deal_w4_scales(1, "words0")
-        v_codes = {(0, half): v_pass0[:, BANK * half : BANK * (half + 1)] for half in range(2)}
-        for half in range(2):
-            v_pass1 = tile([P, BANK], U32, "v_pass1_%d" % half, ("w4_raw0", None)[half])
+        def pick_words(a, half, tag):
+            codes = tile([P, BANK], U32, "v_codes%d_%d" % (a, half), tag)
             entries = slice(BANK * half // PER_COLUMN, BANK * (half + 1) // PER_COLUMN)
-            nc.vector.tensor_copy(v_pass1[:], words[1][:].bitcast(U32).indirect(offs_sb[:, entries]))
-            v_codes[1, half] = v_pass1[:]
-        rounded0 = tile([P, N, PACK], BF16, "w2_rounded0", "words1")
-        nc.vector.tensor_copy(*by_lines(rounded0[:], w2_raw[0][:]))
-        permute_w4_words(1, w4_raw1, "w2_raw0")
+            nc.vector.tensor_copy(codes[:], words[a][:].bitcast(U32).indirect(offs_sb[:, entries]))
+            v_codes[a, half] = codes[:]
 
+        pick_words(0, 0, None)
+        w4_dealt = tile([P, 2, 2 * PASS], U8, "w4_dealt")
+        nc.vector.tensor_copy(
+            w4_dealt[:].bitcast(I32).rearrange("p a (t g v) -> p a t g v", t=PACK, v=4),
+            w4_raw0[:].bitcast(I32).rearrange("p a (g t v) -> p a t g v", t=PACK, v=4),
+        )
+        w4_codes = [w4_dealt, w4_raw1]
+        pick_words(0, 1, "w4_raw0")
+        for half in range(2):
+            pick_words(1, half, None)
 
-        logs = [tile([P, 2 * S], F32, "logs%d" % t) for t in range(PACK)]
-        spare = [logs[k // 2][:, S + M * (k % 2) : S + M * (k % 2 + 1)] for k in range(2 * PACK)]
+        def round_w2(b, columns, tag):
+            rounded = tile([P, columns.stop - columns.start, PACK], BF16, "w2_rounded%d_%d" % (b, columns.start), tag)
+            nc.vector.tensor_copy(*by_lines(rounded[:], w2_raw[b][:, :, columns]))
+            return rounded
+
+        rounded1 = round_w2(1, slice(0, N), None)
+
+        logs = [tile([P, 2 * S], F32, "logs%d" % i) for i in range(2)]
+        eps_wide = tile([P, 2, M], F32, "eps_wide")
         for pair in range(2):
             nc.scalar.copy(
                 logs[pair][:, S : 2 * S].rearrange("p (t m) -> p t m", m=M),
                 eps_sb[:, 0, 2 * pair : 2 * pair + 2].unsqueeze(2).to_broadcast([P, 2, M]),
             )
+        nc.scalar.copy(eps_wide[:], eps_sb[:, 1, 0:2].unsqueeze(2).to_broadcast([P, 2, M]))
+        spread = [logs[j // 2][:, S + M * (j % 2) : S + M * (j % 2 + 1)] for j in range(PACK)]
+        spread.extend(eps_wide[:, i, :] for i in range(2))
         warm = tile([P, 1], F32, "warm")
         nc.scalar.activation(warm[:], eps_sb[:, 0, 0:1], ACT.Ln)
 
@@ -178,50 +180,41 @@ def tile_list_choir_blend_features_kernel(
         def first_product(j, half, a):
             b, t = divmod(j, PACK)
             if a == 0:
-                h_banks[j, half] = psum.tile([P, BANK], F32, name="h%d_%d" % (j, half), tag="bank%d" % (2 * (j % 3) + half))
+                h_banks[j, half] = bank([P, BANK], "h%d_%d" % (j, half), 2 * (j % 4) + half)
             nc.tensor.matmul_mx(
                 out=h_banks[j, half][:],
                 lhsT=w4_codes[b][:, a, 2 * P * t : 2 * P * (t + 1)].bitcast(FP4X4),
-                lhsT_scale=w4_planes[a][:, P * j : P * (j + 1)],
+                lhsT_scale=planes[a][:, S + P * j : S + P * (j + 1)],
                 rhs=v_codes[a, half].bitcast(FP8X4),
-                rhs_scale=v_planes[a][:, BANK * half : BANK * (half + 1)],
+                rhs_scale=planes[a][:, BANK * half : BANK * (half + 1)],
                 start=(a == 0),
                 stop=(a == 1),
             )
             if a == 1:
                 nc.scalar.activation(squares[j][:, BANK * half : BANK * (half + 1)], h_banks[j, half][:], ACT.Square)
 
-        def take_log(t):
-            nc.scalar.activation(logs[t][:, 0:S], squares[PACK + t][:], ACT.Ln, bias=eps_half[:, t : t + 1])
-
-        for j in range(3):
-            for half in range(2):
+        for half in range(2):
+            for j in range(PACK):
                 first_product(j, half, 0)
-        for j, half in ((0, 0), (1, 0), (0, 1), (1, 1), (2, 0), (2, 1)):
+        for j, half in ((0, 0), (1, 0), (2, 0), (0, 1), (1, 1), (3, 0), (2, 1), (3, 1)):
             first_product(j, half, 1)
-        for j in range(3, 2 * PACK):
+        for j in range(PACK, 2 * PACK):
             for half in range(2):
                 for a in range(2):
                     first_product(j, half, a)
-            if j > PACK:
-                take_log(j - 1 - PACK)
-        take_log(PACK - 1)
+        for i in range(2):
+            nc.scalar.activation(logs[i][:, 0:S], squares[6 + i][:], ACT.Ln, bias=eps_third[:, i : i + 1])
 
+        halves = [slice(0, HALF), slice(HALF, M)]
 
         def pick_and_add(dst, j, i, beats, so_far):
             entries = slice(beats.start // PER_COLUMN, beats.stop // PER_COLUMN)
             nc.vector.tensor_tensor(dst, squares[j][:].indirect(pos_sb[i][:, entries]), so_far, ADD)
 
-        def picks(name, tag, i, beats, so_far):
-            total = tile([P, PACK, beats.stop - beats.start], F32, name, tag)
-            for t in range(PACK):
-                pick_and_add(total[:, t, :], PACK + t, i, beats, so_far[:, t, :])
-            return total
-
-        def root(name, tag, total):
-            z = tile([P, total.shape[2], PACK], BF16, name, tag)
-            nc.scalar.activation(*by_lines(z[:], total), ACT.Sqrt)
-            return z
+        def pick(j, i, so_far):
+            part = tile([P, M], F32, "part%d_%d" % (j, i), "part%d_%d" % (j % 2, i))
+            pick_and_add(part[:], j, i, slice(0, M), so_far)
+            return part[:]
 
         def quantise(name, tag, rounded):
             width = rounded.shape[1]
@@ -232,87 +225,120 @@ def tile_list_choir_blend_features_kernel(
             )
             return codes, plane
 
-        total0 = tile([P, PACK, M], F32, "total0")
-        for pair in ((0, 1), (2, 3)):
-            so_far = {t: spare[t] for t in pair}
-            for i in range(3):
-                for t in pair:
-                    if i == 0 and t == 1:
-                        dst = tile([P, M], F32, "first_part", "w4_raw1")[:]
-                    elif t == 0 and i < 2:
-                        dst = spare[PACK + i]
-                    elif (t, i) in ((1, 1), (2, 0)):
-                        dst = spare[PACK + 1 + t]
-                    elif i < 2:
-                        part = partial.tile([P, M], F32, name="part", tag="part")
-                        dst = part[:]
-                    else:
-                        dst = total0[:, t, :]
-                    pick_and_add(dst, t, i, slice(0, M), so_far[t])
-                    so_far[t] = dst
-        by_scalar = [(0, 0), (1, 0), (2, 0), (3, 0), (3, 1)]
-        picked = tile([P, len(by_scalar), M], F32, "picked_by_scalar", "eps_half")
-        for k, (t, i) in enumerate(by_scalar):
-            nc.scalar.activation(picked[:, k, :], logs[t][:].indirect(pos_sb[i][:]), ACT.Exp)
-        z0 = root("z0", "logs3", total0[:])
+        totals = [tile([P, PACK, HALF], F32, "total%d" % half) for half in range(2)]
 
-        halves = [slice(0, 256), slice(256, 512)]
-        y_banks = {}
+        def last_picks(pair, so_far):
+            for half in range(2):
+                for j in pair:
+                    pick_and_add(totals[half][:, j, :], j, 2, halves[half], so_far[j][:, halves[half]])
 
-        def second_product(beats, b, row_tiles, codes, plane):
-            half, first = divmod(beats.start, 256)
-            for n in row_tiles:
-                if b == 0:
-                    y_banks[half, n] = psum.tile([P, 256], F32, name="y%d_%d" % (half, n), tag="bank%d" % (4 * half + n))
-                nc.tensor.matmul_mx(
-                    out=y_banks[half, n][:, first : first + beats.stop - beats.start],
-                    lhsT=w2_q[b, n][0].bitcast(FP8X4),
-                    lhsT_scale=w2_q[b, n][1],
-                    rhs=codes.bitcast(FP8X4),
-                    rhs_scale=plane,
-                    start=(b == 0),
-                    stop=(b == 1 and beats.stop % 256 == 0),
+        sums = [bank([P, PASS], "sums%d" % c, c) for c in range(M // P)]
+
+        def add_turned(t, term, first=False, last=False):
+            for c in range(M // P):
+                nc.tensor.matmul(
+                    sums[c][:, P * t : P * (t + 1)],
+                    lhsT=term[:, P * c : P * (c + 1)],
+                    rhs=identity[:],
+                    is_transpose=True,
+                    start=first,
+                    stop=last,
                 )
-
-        def finish(half, row_tiles):
-            for n in row_tiles:
-                result = tile([P, 256], F32, "result%d_%d" % (half, n))
-                nc.scalar.activation(result[:], y_banks[half, n][:], ACT.Silu)
-                nc.sync.dma_start(out[P * n : P * (n + 1), halves[half]], result[:])
 
         w2_q = {}
 
-        def quantise_w2(b, tag, rounded):
-            codes, plane = quantise("w2_%d" % b, tag, rounded)
-            for n in range(N // P):
-                w2_q[b, n] = (codes[:, P * n : P * (n + 1)], plane[:, P * n : P * (n + 1)])
-            return codes, plane
+        def quantise_w2(b, first, rounded):
+            codes, plane = quantise("w2_%d_%d" % (b, first), None, rounded)
+            for n in range(rounded.shape[1] // P):
+                w2_q[b, first + n] = (codes[:, P * n : P * (n + 1)], plane[:, P * n : P * (n + 1)])
 
-        sum2 = tile([P, PACK, M], F32, "sum2")
-        for t in range(3):
-            pick_and_add(sum2[:, t, :], PACK + t, 1, slice(0, M), picked[:, t, :])
-        nc.vector.tensor_tensor(sum2[:, 3, :], picked[:, 3, :], picked[:, 4, :], ADD)
-        total_a = picks("total_a", None, 2, halves[0], sum2[:, :, halves[0]])
-        z1 = [root("z1_0", None, total_a[:])]
-        total = tile([P, PACK, 256], F32, "total_b")
-        for t in range(PACK):
-            pick_and_add(total[:, t, :], PACK + t, 2, halves[1], sum2[:, t, halves[1]])
-        z1.append(root("z1_1", None, total[:]))
-        quantise_w2(0, "squares6", rounded0)
-        codes0, plane0 = quantise("z0", "squares7", z0)
-        for beats in halves:
-            second_product(beats, 0, range(4), codes0[:, beats], plane0[:, beats])
-        z1_q = []
-        for g, tag in enumerate(("logs3", "z1_0")):
-            rounded = tile([P, N // 2, PACK], BF16, "w2_rounded1_%d" % g, tag)
-            nc.vector.tensor_copy(*by_lines(rounded[:], w2_raw[1][:, :, N // 2 * g : N // 2 * (g + 1)]))
-            if g == 0:
-                z1_q.append(quantise("z1_0", None, z1[0]))
-            codes, plane = quantise("w2_1_%d" % g, None, rounded)
-            for n in range(2):
-                w2_q[1, 2 * g + n] = (codes[:, P * n : P * (n + 1)], plane[:, P * n : P * (n + 1)])
-            if g == 0:
-                z1_q.append(quantise("z1_1", None, z1[1]))
-            for half in range(2):
-                second_product(halves[half], 1, range(2 * g, 2 * g + 2), z1_q[half][0][:], z1_q[half][1][:])
-                finish(half, range(2 * g, 2 * g + 2))
+        quantise_w2(1, 0, rounded1)
+        so_far = dict(enumerate(spread))
+        for i in range(2):
+            for j in (0, 1):
+                so_far[j] = pick(j, i, so_far[j])
+        last_picks((0, 1), so_far)
+        for i in range(2):
+            for j in (4, 5):
+                so_far[j] = pick(j, i, so_far[j])
+        whole = [tile([P, M], F32, "whole%d" % t) for t in range(2)]
+        for t in range(2):
+            pick_and_add(whole[t][:], PACK + t, 2, slice(0, M), so_far[PACK + t])
+        picked = [tile([P, LISTS, M], F32, "picked%d" % i, ("eps_third", None)[i]) for i in range(2)]
+        for i in range(2):
+            for k in range(LISTS):
+                nc.scalar.activation(picked[i][:, k, :], logs[i][:].indirect(pos_sb[k][:]), ACT.Exp)
+        add_turned(2, picked[0][:, 0, :], first=True)
+        add_turned(2, picked[0][:, 1, :])
+        add_turned(0, whole[0][:])
+        add_turned(2, picked[0][:, 2, :])
+        add_turned(1, whole[1][:])
+        for k in range(LISTS):
+            add_turned(3, picked[1][:, k, :], last=(k == LISTS - 1))
+        for i in range(2):
+            for j in (2, 3):
+                so_far[j] = pick(j, i, so_far[j])
+        last_picks((2, 3), so_far)
+
+        backs = []
+        for half in range(2):
+            backs.append(bank([P, 2, HALF], "back%d" % half, 4 + half))
+            for c in range(2):
+                turned = tile([P, PASS], BF16, "turned%d_%d" % (half, c))
+                nc.scalar.activation(
+                    turned[:].rearrange("m (u g w) -> m u g w", u=2, w=16),
+                    sums[2 * half + c][:].rearrange("m (g u w) -> m u g w", u=2, w=16),
+                    ACT.Sqrt,
+                )
+                for u in range(2):
+                    nc.tensor.transpose(
+                        backs[half][:, u, P * c : P * (c + 1)],
+                        turned[:].bitcast(F32)[:, P * u : P * (u + 1)],
+                        identity[:],
+                    )
+
+        def copy_back(half, tag):
+            z = tile([P, HALF, PACK], BF16, "z1_%d" % half, tag)
+            nc.vector.tensor_copy(
+                z[:].rearrange("p m t -> p (m t)").bitcast(F32).rearrange("p (m u) -> p m u", u=2),
+                backs[half][:].rearrange("p u m -> p m u"),
+            )
+            return z
+
+        z0 = []
+        for half in range(2):
+            z0.append(tile([P, HALF, PACK], BF16, "z0_%d" % half, "turned%d_0" % half))
+            nc.scalar.activation(*by_lines(z0[half][:], totals[half][:]), ACT.Sqrt)
+
+        y_banks = {}
+
+        def second_product(half, b, row_tiles, z_q):
+            for n in row_tiles:
+                if b == 1:
+                    y_banks[half, n] = bank([P, HALF], "y%d_%d" % (half, n), ((0, 1, 2, 3), (6, 7, 4, 5))[half][n])
+                nc.tensor.matmul_mx(
+                    out=y_banks[half, n][:],
+                    lhsT=w2_q[b, n][0].bitcast(FP8X4),
+                    lhsT_scale=w2_q[b, n][1],
+                    rhs=z_q[0][:].bitcast(FP8X4),
+                    rhs_scale=z_q[1][:],
+                    start=(b == 1),
+                    stop=(b == 0),
+                )
+                if b == 0:
+                    result = tile([P, HALF], F32, "result%d_%d" % (half, n))
+                    nc.scalar.activation(result[:], y_banks[half, n][:], ACT.Silu)
+                    nc.sync.dma_start(out[P * n : P * (n + 1), halves[half]], result[:])
+
+        z1_a = copy_back(0, None)
+        rounded = round_w2(0, slice(0, N // 2), "turned0_1")
+        second_product(0, 1, range(4), quantise("z1_0", None, z1_a))
+        quantise_w2(0, 0, rounded)
+        z0_a = quantise("z0_0", None, z0[0])
+        second_product(0, 0, range(2), z0_a)
+        rounded = round_w2(0, slice(N // 2, N), "total0")
+        z1_b = copy_back(1, "turned0_0")
+        quantise_w2(0, 2, rounded)
+        second_product(0, 0, range(2, 4), z0_a)
+        second_product(1, 1, range(4), quantise("z1_1", None, z1_b))
+        second_product(1, 0, range(4), quantise("z0_1", None, z0[1]))

@@ -27,8 +27,6 @@ PER_COLUMN = 16
 QUADRANT = 32
 LINE = 4
 LISTS = 3
-BEHIND = T // 8
-AHEAD = T // 4
 
 
 def tile_list_choir_blend_features_kernel(
@@ -62,16 +60,20 @@ def tile_list_choir_blend_features_kernel(
         nc.sync.dma_start(
             scale_rows[0:QUADRANT, :].bitcast(I32), tab_scales.rearrange("a q t -> (a q) t").bitcast(I32)
         )
-        w4_rows = tile([QUADRANT, H], U8, "w4_rows")
-        nc.sync.dma_start(w4_rows[:].bitcast(I32), w4_scales.rearrange("a q c -> (a q) c").bitcast(I32))
         eps_rows = tile([2 * QUADRANT, PASS], F32, "eps_rows")
         nc.sync.dma_start(eps_rows[0 : 2 * QUADRANT : QUADRANT, :], eps.rearrange("(b r) -> b r", b=2))
+        w4_rows = tile([P, 2, H], U8, "w4_rows")
+        for r in range(4):
+            nc.sync.dma_start(
+                w4_rows[r:P:QUADRANT, :, :].bitcast(I32),
+                w4_scales[:, r:16:4, :].rearrange("a q c -> q a c").bitcast(I32),
+            )
         words = [tile([P, T], I32, "words%d" % a) for a in range(2)]
         nc.sync.dma_start(words[0][:], tab[0])
         w4_raw0 = load_w4_words(0)
         nc.vector.memset(scale_rows[QUADRANT : 2 * QUADRANT, :].bitcast(I32), 0)
         nc.vector.memset(scale_rows[2 * QUADRANT : P, :].bitcast(I32), 0)
-        planes = [tile([P, S + H], U8, "planes%d" % a) for a in range(2)]
+        planes = [tile([P, S], U8, "planes%d" % a) for a in range(2)]
         for a in range(2):
             nc.vector.memset(planes[a][:].bitcast(I32), 0)
 
@@ -96,28 +98,28 @@ def tile_list_choir_blend_features_kernel(
                 src.rearrange("p t (c i) -> p c t i", i=LINE),
             )
 
-        staged = tile([QUADRANT, S + H], U8, "staged")
-        nc.vector.tensor_copy(
-            staged[:, S : S + PASS].bitcast(I32).rearrange("p (t g v) -> p t g v", t=PACK, v=2),
-            w4_rows[:, 0:PASS].bitcast(I32).rearrange("p (g t v) -> p t g v", t=PACK, v=2),
-        )
-        nc.vector.tensor_copy(staged[:, S + PASS : S + H].bitcast(I32), w4_rows[:, PASS:H].bitcast(I32))
         picked_scales = tile([P, S], U8, "picked_scales")
         nc.vector.tensor_copy(picked_scales[:], scale_rows[:].indirect(offs_sb[:]))
-        nc.vector.tensor_copy(staged[:, 0:S].bitcast(I32), picked_scales[0:QUADRANT, :].bitcast(I32))
+        w4_planes = tile([P, 2, H], U8, "w4_planes", "scale_rows")
+        nc.vector.memset(w4_planes[:].bitcast(I32), 0)
+        for quad in range(4):
+            live = slice(QUADRANT * quad, QUADRANT * quad + 4)
+            nc.vector.tensor_copy(
+                w4_planes[live, :, 0:PASS].bitcast(I32).rearrange("p a (t g v) -> p a t g v", t=PACK, v=2),
+                w4_rows[live, :, 0:PASS].bitcast(I32).rearrange("p a (g t v) -> p a t g v", t=PACK, v=2),
+            )
+            nc.vector.tensor_copy(w4_planes[live, :, PASS:H].bitcast(I32), w4_rows[live, :, PASS:H].bitcast(I32))
 
         def move_scale_rows(a):
             for r in range(4):
                 nc.sync.dma_start(
                     planes[a][r:P:QUADRANT, :].bitcast(I32),
-                    staged[16 * a + r : 16 * (a + 1) : 4, :].bitcast(I32),
+                    picked_scales[16 * a + r : 16 * (a + 1) : 4, :].bitcast(I32),
                 )
 
-        nc.sync.dma_start(words[1][:, 0:AHEAD], tab[1][:, 0:AHEAD])
         move_scale_rows(0)
-        nc.sync.dma_start(words[1][:, AHEAD : T - BEHIND], tab[1][:, AHEAD : T - BEHIND])
+        nc.sync.dma_start(words[1][:], tab[1])
         move_scale_rows(1)
-        nc.sync.dma_start(words[1][:, T - BEHIND : T], tab[1][:, T - BEHIND : T])
         w2_raw = [tile([P, PACK, N], F32, "w2_raw%d" % b) for b in range(2)]
         nc.sync.dma_start(pos_sb[0][:], pos1)
         rows = w2[PASS:H, :].rearrange("(g u q e) n -> u g q (e n)", u=2, q=RUN, e=2)
@@ -184,7 +186,7 @@ def tile_list_choir_blend_features_kernel(
             nc.tensor.matmul_mx(
                 out=h_banks[j, half][:],
                 lhsT=w4_codes[b][:, a, 2 * P * t : 2 * P * (t + 1)].bitcast(FP4X4),
-                lhsT_scale=planes[a][:, S + P * j : S + P * (j + 1)],
+                lhsT_scale=w4_planes[:, a, P * j : P * (j + 1)],
                 rhs=v_codes[a, half].bitcast(FP8X4),
                 rhs_scale=planes[a][:, BANK * half : BANK * (half + 1)],
                 start=(a == 0),

@@ -70,7 +70,7 @@ def tile_list_choir_blend_features_kernel(
             )
         words = [tile([P, T], I32, "words%d" % a) for a in range(2)]
         nc.sync.dma_start(words[0][:], tab[0])
-        w4_raw0 = load_w4_words(0)
+        w4_raw1 = load_w4_words(1)
         nc.vector.memset(scale_rows[QUADRANT : 2 * QUADRANT, :].bitcast(I32), 0)
         nc.vector.memset(scale_rows[2 * QUADRANT : P, :].bitcast(I32), 0)
         planes = [tile([P, S], U8, "planes%d" % a) for a in range(2)]
@@ -120,17 +120,19 @@ def tile_list_choir_blend_features_kernel(
         move_scale_rows(0)
         nc.sync.dma_start(words[1][:], tab[1])
         move_scale_rows(1)
-        w2_raw = [tile([P, PACK, N], F32, "w2_raw%d" % b) for b in range(2)]
+        w4_raw0 = load_w4_words(0)
+        columns = [slice(0, N // 2), slice(N // 2, N)]
+        w2_rows1 = [tile([P, PACK, N // 2], F32, "w2_rows1_%d" % g) for g in range(2)]
+        rows = w2[PASS:H, :].rearrange("(p t) n -> p t n", t=PACK)
+        nc.sync.dma_start(w2_rows1[0][:], rows[:, :, columns[0]])
         nc.sync.dma_start(pos_sb[0][:], pos1)
-        rows = w2[PASS:H, :].rearrange("(g u q e) n -> u g q (e n)", u=2, q=RUN, e=2)
-        for u in range(2):
-            nc.sync.dma_start(w2_raw[1][:, 2 * u : 2 * u + 2, :].rearrange("p e n -> p (e n)"), rows[u])
         nc.sync.dma_start(pos_sb[1][:], pos2)
+        nc.sync.dma_start(w2_rows1[1][:], rows[:, :, columns[1]])
         nc.sync.dma_start(pos_sb[2][:], pos3)
-        w4_raw1 = load_w4_words(1)
+        w2_rows0 = tile([P, PACK, N], F32, "w2_rows0")
         rows = w2[0:PASS, :].rearrange("(g t u) n -> t g u n", t=PACK, u=RUN)
         for t in range(PACK):
-            nc.sync.dma_start(w2_raw[0][:, t, :], rows[t])
+            nc.sync.dma_start(w2_rows0[:, t, :], rows[t])
 
         eps_sb = tile([P, 2, PACK], F32, "eps_sb")
         nc.scalar.copy(eps_sb[:], eps_turned[:, :, 0 : 2 * QUADRANT : QUADRANT].rearrange("p t b -> p b t"))
@@ -139,29 +141,29 @@ def tile_list_choir_blend_features_kernel(
 
         v_codes = {}
 
-        def pick_words(a, half, tag):
-            codes = tile([P, BANK], U32, "v_codes%d_%d" % (a, half), tag)
+        def pick_words(a, half):
+            codes = tile([P, BANK], U32, "v_codes%d_%d" % (a, half))
             entries = slice(BANK * half // PER_COLUMN, BANK * (half + 1) // PER_COLUMN)
             nc.vector.tensor_copy(codes[:], words[a][:].bitcast(U32).indirect(offs_sb[:, entries]))
             v_codes[a, half] = codes[:]
 
-        pick_words(0, 0, None)
+        for a in range(2):
+            for half in range(2):
+                pick_words(a, half)
+
         w4_dealt = tile([P, 2, 2 * PASS], U8, "w4_dealt")
         nc.vector.tensor_copy(
             w4_dealt[:].bitcast(I32).rearrange("p a (t g v) -> p a t g v", t=PACK, v=4),
             w4_raw0[:].bitcast(I32).rearrange("p a (g t v) -> p a t g v", t=PACK, v=4),
         )
         w4_codes = [w4_dealt, w4_raw1]
-        pick_words(0, 1, "w4_raw0")
-        for half in range(2):
-            pick_words(1, half, None)
+        rounded1 = tile([P, N, PACK], BF16, "w2_rounded1")
+        nc.vector.tensor_copy(*by_lines(rounded1[:, columns[0], :], w2_rows1[0][:]))
 
-        def round_w2(b, columns, tag):
-            rounded = tile([P, columns.stop - columns.start, PACK], BF16, "w2_rounded%d_%d" % (b, columns.start), tag)
-            nc.vector.tensor_copy(*by_lines(rounded[:], w2_raw[b][:, :, columns]))
+        def round_w2(g, tag):
+            rounded = tile([P, N // 2, PACK], BF16, "w2_rounded0_%d" % g, tag)
+            nc.vector.tensor_copy(*by_lines(rounded[:], w2_rows0[:, :, columns[g]]))
             return rounded
-
-        rounded1 = round_w2(1, slice(0, N), None)
 
         logs = [tile([P, 2 * S], F32, "logs%d" % i) for i in range(2)]
         eps_wide = tile([P, 2, M], F32, "eps_wide")
@@ -196,14 +198,10 @@ def tile_list_choir_blend_features_kernel(
                 nc.scalar.activation(squares[j][:, BANK * half : BANK * (half + 1)], h_banks[j, half][:], ACT.Square)
 
         for half in range(2):
-            for j in range(PACK):
+            for j in range(PACK, 2 * PACK):
                 first_product(j, half, 0)
-        for j, half in ((0, 0), (1, 0), (2, 0), (0, 1), (1, 1), (3, 0), (2, 1), (3, 1)):
-            first_product(j, half, 1)
-        for j in range(PACK, 2 * PACK):
-            for half in range(2):
-                for a in range(2):
-                    first_product(j, half, a)
+        for t, half in ((0, 0), (1, 0), (2, 0), (0, 1), (1, 1), (3, 0), (2, 1), (3, 1)):
+            first_product(PACK + t, half, 1)
         for i in range(2):
             nc.scalar.activation(logs[i][:, 0:S], squares[6 + i][:], ACT.Ln, bias=eps_third[:, i : i + 1])
 
@@ -234,8 +232,6 @@ def tile_list_choir_blend_features_kernel(
                 for j in pair:
                     pick_and_add(totals[half][:, j, :], j, 2, halves[half], so_far[j][:, halves[half]])
 
-        sums = [bank([P, PASS], "sums%d" % c, c) for c in range(M // P)]
-
         def add_turned(t, term, first=False, last=False):
             for c in range(M // P):
                 nc.tensor.matmul(
@@ -254,33 +250,44 @@ def tile_list_choir_blend_features_kernel(
             for n in range(rounded.shape[1] // P):
                 w2_q[b, first + n] = (codes[:, P * n : P * (n + 1)], plane[:, P * n : P * (n + 1)])
 
-        quantise_w2(1, 0, rounded1)
+        def whole_tiles(pair):
+            for j in pair:
+                for half in range(2):
+                    for a in range(2):
+                        first_product(j, half, a)
+
         so_far = dict(enumerate(spread))
-        for i in range(2):
-            for j in (0, 1):
-                so_far[j] = pick(j, i, so_far[j])
-        last_picks((0, 1), so_far)
-        for i in range(2):
-            for j in (4, 5):
-                so_far[j] = pick(j, i, so_far[j])
+        for j in (4, 5):
+            so_far[j] = pick(j, 0, so_far[j])
+        nc.vector.tensor_copy(*by_lines(rounded1[:, columns[1], :], w2_rows1[1][:]))
+        so_far[4] = pick(4, 1, so_far[4])
+        quantise_w2(1, 0, rounded1)
+        so_far[5] = pick(5, 1, so_far[5])
         whole = [tile([P, M], F32, "whole%d" % t) for t in range(2)]
         for t in range(2):
             pick_and_add(whole[t][:], PACK + t, 2, slice(0, M), so_far[PACK + t])
+        whole_tiles((0, 1))
         picked = [tile([P, LISTS, M], F32, "picked%d" % i, ("eps_third", None)[i]) for i in range(2)]
-        for i in range(2):
-            for k in range(LISTS):
-                nc.scalar.activation(picked[i][:, k, :], logs[i][:].indirect(pos_sb[k][:]), ACT.Exp)
-        add_turned(2, picked[0][:, 0, :], first=True)
-        add_turned(2, picked[0][:, 1, :])
-        add_turned(0, whole[0][:])
-        add_turned(2, picked[0][:, 2, :])
-        add_turned(1, whole[1][:])
-        for k in range(LISTS):
-            add_turned(3, picked[1][:, k, :], last=(k == LISTS - 1))
-        for i in range(2):
-            for j in (2, 3):
-                so_far[j] = pick(j, i, so_far[j])
-        last_picks((2, 3), so_far)
+        by_scalar = [(i, k) for i in range(2) for k in range(LISTS)]
+
+        def pick_on_scalar(i, k):
+            nc.scalar.activation(picked[i][:, k, :], logs[i][:].indirect(pos_sb[k][:]), ACT.Exp)
+
+        for i, k in by_scalar[:4]:
+            pick_on_scalar(i, k)
+        whole_tiles((2, 3))
+        for i, k in by_scalar[4:]:
+            pick_on_scalar(i, k)
+        sums = [bank([P, PASS], "sums%d" % c, c) for c in range(M // P)]
+        for t in range(2):
+            add_turned(t, whole[t][:], first=(t == 0))
+        for i, k in by_scalar:
+            add_turned(2 + i, picked[i][:, k, :], last=((i, k) == by_scalar[-1]))
+        for pair in ((0, 1), (2, 3)):
+            for i in range(2):
+                for j in pair:
+                    so_far[j] = pick(j, i, so_far[j])
+            last_picks(pair, so_far)
 
         backs = []
         for half in range(2):
@@ -288,8 +295,8 @@ def tile_list_choir_blend_features_kernel(
             for c in range(2):
                 turned = tile([P, PASS], BF16, "turned%d_%d" % (half, c))
                 nc.scalar.activation(
-                    turned[:].rearrange("m (u g w) -> m u g w", u=2, w=16),
-                    sums[2 * half + c][:].rearrange("m (g u w) -> m u g w", u=2, w=16),
+                    turned[:].rearrange("m (u p e) -> m u p e", u=2, e=2),
+                    sums[2 * half + c][:].rearrange("m (p u e) -> m u p e", u=2, e=2),
                     ACT.Sqrt,
                 )
                 for u in range(2):
@@ -333,12 +340,12 @@ def tile_list_choir_blend_features_kernel(
                     nc.sync.dma_start(out[P * n : P * (n + 1), halves[half]], result[:])
 
         z1_a = copy_back(0, None)
-        rounded = round_w2(0, slice(0, N // 2), "turned0_1")
+        rounded = round_w2(0, "turned0_1")
         second_product(0, 1, range(4), quantise("z1_0", None, z1_a))
         quantise_w2(0, 0, rounded)
         z0_a = quantise("z0_0", None, z0[0])
         second_product(0, 0, range(2), z0_a)
-        rounded = round_w2(0, slice(N // 2, N), "total0")
+        rounded = round_w2(1, "total0")
         z1_b = copy_back(1, "turned0_0")
         quantise_w2(0, 2, rounded)
         second_product(0, 0, range(2, 4), z0_a)

@@ -245,8 +245,8 @@ def tile_list_choir_blend_features_kernel(
 
         w2_q = {}
 
-        def quantise_w2(b, first, rounded):
-            codes, plane = quantise("w2_%d_%d" % (b, first), None, rounded)
+        def quantise_w2(b, first, rounded, tag):
+            codes, plane = quantise("w2_%d_%d" % (b, first), tag, rounded)
             for n in range(rounded.shape[1] // P):
                 w2_q[b, first + n] = (codes[:, P * n : P * (n + 1)], plane[:, P * n : P * (n + 1)])
 
@@ -261,7 +261,7 @@ def tile_list_choir_blend_features_kernel(
             so_far[j] = pick(j, 0, so_far[j])
         nc.vector.tensor_copy(*by_lines(rounded1[:, columns[1], :], w2_rows1[1][:]))
         so_far[4] = pick(4, 1, so_far[4])
-        quantise_w2(1, 0, rounded1)
+        quantise_w2(1, 0, rounded1, None)
         so_far[5] = pick(5, 1, so_far[5])
         whole = [tile([P, M], F32, "whole%d" % t) for t in range(2)]
         for t in range(2):
@@ -289,34 +289,38 @@ def tile_list_choir_blend_features_kernel(
                     so_far[j] = pick(j, i, so_far[j])
             last_picks(pair, so_far)
 
-        backs = []
-        for half in range(2):
-            backs.append(bank([P, 2, HALF], "back%d" % half, 4 + half))
-            for c in range(2):
-                turned = tile([P, PASS], BF16, "turned%d_%d" % (half, c))
-                nc.scalar.activation(
-                    turned[:].rearrange("m (u p e) -> m u p e", u=2, e=2),
-                    sums[2 * half + c][:].rearrange("m (p u e) -> m u p e", u=2, e=2),
-                    ACT.Sqrt,
-                )
-                for u in range(2):
-                    nc.tensor.transpose(
-                        backs[half][:, u, P * c : P * (c + 1)],
-                        turned[:].bitcast(F32)[:, P * u : P * (u + 1)],
-                        identity[:],
-                    )
+        backs = [bank([P, 2, HALF], "back%d" % half, 4 + half) for half in range(2)]
 
-        def copy_back(half, tag):
-            z = tile([P, HALF, PACK], BF16, "z1_%d" % half, tag)
-            nc.vector.tensor_copy(
+        def root_and_turn_back(c):
+            half, part = divmod(c, 2)
+            turned = tile([P, PASS], BF16, "turned%d" % c)
+            nc.scalar.activation(
+                turned[:].rearrange("m (u p e) -> m u p e", u=2, e=2),
+                sums[c][:].rearrange("m (p u e) -> m u p e", u=2, e=2),
+                ACT.Sqrt,
+            )
+            for u in range(2):
+                nc.tensor.transpose(
+                    backs[half][:, u, P * part : P * (part + 1)],
+                    turned[:].bitcast(F32)[:, P * u : P * (u + 1)],
+                    identity[:],
+                )
+
+        def copy_back(half, copy):
+            z = tile([P, HALF, PACK], BF16, "z1_%d" % half)
+            copy(
                 z[:].rearrange("p m t -> p (m t)").bitcast(F32).rearrange("p (m u) -> p m u", u=2),
                 backs[half][:].rearrange("p u m -> p m u"),
             )
             return z
 
+        for c in range(3):
+            root_and_turn_back(c)
+        z1 = [copy_back(0, nc.scalar.copy)]
+        root_and_turn_back(3)
         z0 = []
         for half in range(2):
-            z0.append(tile([P, HALF, PACK], BF16, "z0_%d" % half, "turned%d_0" % half))
+            z0.append(tile([P, HALF, PACK], BF16, "z0_%d" % half, "turned%d" % (2 * half)))
             nc.scalar.activation(*by_lines(z0[half][:], totals[half][:]), ACT.Sqrt)
 
         y_banks = {}
@@ -339,15 +343,16 @@ def tile_list_choir_blend_features_kernel(
                     nc.scalar.activation(result[:], y_banks[half, n][:], ACT.Silu)
                     nc.sync.dma_start(out[P * n : P * (n + 1), halves[half]], result[:])
 
-        z1_a = copy_back(0, None)
-        rounded = round_w2(0, "turned0_1")
-        second_product(0, 1, range(4), quantise("z1_0", None, z1_a))
-        quantise_w2(0, 0, rounded)
-        z0_a = quantise("z0_0", None, z0[0])
-        second_product(0, 0, range(2), z0_a)
+        second_product(0, 1, range(4), quantise("z1_0", None, z1[0]))
+        z1.append(copy_back(1, nc.vector.tensor_copy))
+        rounded = round_w2(0, "z1_0")
+        second_product(1, 1, range(4), quantise("z1_1", None, z1[1]))
+        quantise_w2(0, 0, rounded, None)
+        z0_q = [quantise("z0_0", None, z0[0])]
+        second_product(0, 0, range(2), z0_q[0])
         rounded = round_w2(1, "total0")
-        z1_b = copy_back(1, "turned0_0")
-        quantise_w2(0, 2, rounded)
-        second_product(0, 0, range(2, 4), z0_a)
-        second_product(1, 1, range(4), quantise("z1_1", None, z1_b))
-        second_product(1, 0, range(4), quantise("z0_1", None, z0[1]))
+        z0_q.append(quantise("z0_1", None, z0[1]))
+        second_product(1, 0, range(2), z0_q[1])
+        quantise_w2(0, 2, rounded, "total1")
+        for half in range(2):
+            second_product(half, 0, range(2, 4), z0_q[half])

@@ -16,6 +16,7 @@ FP8X4 = mybir.dt.float8_e4m3fn_x4
 FP4X4 = mybir.dt.float4_e2m1fn_x4
 ACT = mybir.ActivationFunctionType
 ADD = mybir.AluOpType.add
+MULT = mybir.AluOpType.mult
 
 P = 128
 PACK = 4
@@ -157,8 +158,8 @@ def tile_list_choir_blend_features_kernel(
             w4_raw0[:].bitcast(I32).rearrange("p a (g t v) -> p a t g v", t=PACK, v=4),
         )
         w4_codes = [w4_dealt, w4_raw1]
-        rounded1 = tile([P, N, PACK], BF16, "w2_rounded1")
-        nc.vector.tensor_copy(*by_lines(rounded1[:, columns[0], :], w2_rows1[0][:]))
+        rounded1 = [tile([P, N // 2, PACK], BF16, "w2_rounded1_0")]
+        nc.vector.tensor_copy(*by_lines(rounded1[0][:], w2_rows1[0][:]))
 
         def round_w2(g, tag):
             rounded = tile([P, N // 2, PACK], BF16, "w2_rounded0_%d" % g, tag)
@@ -256,16 +257,22 @@ def tile_list_choir_blend_features_kernel(
                     for a in range(2):
                         first_product(j, half, a)
 
+        def round_on_gpsimd(dst, src):
+            nc.gpsimd.tensor_scalar(dst, src.rearrange("p t n -> p n t"), 1.0, 0.0, MULT, ADD)
+
         so_far = dict(enumerate(spread))
-        for j in (4, 5):
-            so_far[j] = pick(j, 0, so_far[j])
-        nc.vector.tensor_copy(*by_lines(rounded1[:, columns[1], :], w2_rows1[1][:]))
-        so_far[4] = pick(4, 1, so_far[4])
-        quantise_w2(1, 0, rounded1, None)
-        so_far[5] = pick(5, 1, so_far[5])
-        whole = [tile([P, M], F32, "whole%d" % t) for t in range(2)]
+        terms = [tile([P, LISTS, M], F32, "terms%d" % t) for t in range(2)]
+        for i in range(2):
+            for t in range(2):
+                nc.vector.tensor_copy(terms[t][:, i, :], squares[PACK + t][:].indirect(pos_sb[i][:]))
+        rounded1.append(tile([P, N // 2, PACK], BF16, "w2_rounded1_1", "w2_rows1_0"))
+        round_on_gpsimd(rounded1[1][:], w2_rows1[1][:])
+        rounded0 = tile([P, N // 2, PACK], BF16, "w2_rounded0_0")
+        round_on_gpsimd(rounded0[:], w2_rows0[:, :, columns[0]])
         for t in range(2):
-            pick_and_add(whole[t][:], PACK + t, 2, slice(0, M), so_far[PACK + t])
+            pick_and_add(terms[t][:, 2, :], PACK + t, 2, slice(0, M), so_far[PACK + t])
+        for g in range(2):
+            quantise_w2(1, 2 * g, rounded1[g], "squares%d" % (PACK + g))
         whole_tiles((0, 1))
         picked = [tile([P, LISTS, M], F32, "picked%d" % i, ("eps_third", None)[i]) for i in range(2)]
         by_scalar = [(i, k) for i in range(2) for k in range(LISTS)]
@@ -279,8 +286,9 @@ def tile_list_choir_blend_features_kernel(
         for i, k in by_scalar[4:]:
             pick_on_scalar(i, k)
         sums = [bank([P, PASS], "sums%d" % c, c) for c in range(M // P)]
-        for t in range(2):
-            add_turned(t, whole[t][:], first=(t == 0))
+        for i in range(LISTS):
+            for t in range(2):
+                add_turned(t, terms[t][:, i, :], first=(i == 0 and t == 0))
         for i, k in by_scalar:
             add_turned(2 + i, picked[i][:, k, :], last=((i, k) == by_scalar[-1]))
         for pair in ((0, 1), (2, 3)):
@@ -314,10 +322,8 @@ def tile_list_choir_blend_features_kernel(
             )
             return z
 
-        for c in range(3):
+        for c in range(M // P):
             root_and_turn_back(c)
-        z1 = [copy_back(0, nc.scalar.copy)]
-        root_and_turn_back(3)
         z0 = []
         for half in range(2):
             z0.append(tile([P, HALF, PACK], BF16, "z0_%d" % half, "turned%d" % (2 * half)))
@@ -343,14 +349,14 @@ def tile_list_choir_blend_features_kernel(
                     nc.scalar.activation(result[:], y_banks[half, n][:], ACT.Silu)
                     nc.sync.dma_start(out[P * n : P * (n + 1), halves[half]], result[:])
 
+        z1 = [copy_back(0, nc.vector.tensor_copy)]
+        quantise_w2(0, 0, rounded0, "turned1")
         second_product(0, 1, range(4), quantise("z1_0", None, z1[0]))
         z1.append(copy_back(1, nc.vector.tensor_copy))
-        rounded = round_w2(0, "z1_0")
-        second_product(1, 1, range(4), quantise("z1_1", None, z1[1]))
-        quantise_w2(0, 0, rounded, None)
         z0_q = [quantise("z0_0", None, z0[0])]
         second_product(0, 0, range(2), z0_q[0])
-        rounded = round_w2(1, "total0")
+        second_product(1, 1, range(4), quantise("z1_1", "total0", z1[1]))
+        rounded = round_w2(1, "turned0")
         z0_q.append(quantise("z0_1", None, z0[1]))
         second_product(1, 0, range(2), z0_q[1])
         quantise_w2(0, 2, rounded, "total1")

@@ -137,8 +137,9 @@ def tile_list_choir_blend_features_kernel(
 
         eps_sb = tile([P, 2, PACK], F32, "eps_sb")
         nc.scalar.copy(eps_sb[:], eps_turned[:, :, 0 : 2 * QUADRANT : QUADRANT].rearrange("p t b -> p b t"))
-        eps_third = tile([P, 2], F32, "eps_third")
-        nc.scalar.mul(eps_third[:], eps_turned[:, 2:4, QUADRANT], 1.0 / LISTS)
+        eps_share = tile([P, 2], F32, "eps_share")
+        for i, shares in enumerate((3, 2)):
+            nc.scalar.mul(eps_share[:, i : i + 1], eps_turned[:, 2 + i, QUADRANT : QUADRANT + 1], 1.0 / shares)
 
         v_codes = {}
 
@@ -160,11 +161,6 @@ def tile_list_choir_blend_features_kernel(
         w4_codes = [w4_dealt, w4_raw1]
         rounded1 = [tile([P, N // 2, PACK], BF16, "w2_rounded1_0")]
         nc.vector.tensor_copy(*by_lines(rounded1[0][:], w2_rows1[0][:]))
-
-        def round_w2(g, tag):
-            rounded = tile([P, N // 2, PACK], BF16, "w2_rounded0_%d" % g, tag)
-            nc.vector.tensor_copy(*by_lines(rounded[:], w2_rows0[:, :, columns[g]]))
-            return rounded
 
         logs = [tile([P, 2 * S], F32, "logs%d" % i) for i in range(2)]
         eps_wide = tile([P, 2, M], F32, "eps_wide")
@@ -201,10 +197,10 @@ def tile_list_choir_blend_features_kernel(
         for half in range(2):
             for j in range(PACK, 2 * PACK):
                 first_product(j, half, 0)
-        for t, half in ((0, 0), (1, 0), (2, 0), (0, 1), (1, 1), (3, 0), (2, 1), (3, 1)):
+        for t, half in ((0, 0), (1, 0), (0, 1), (1, 1), (2, 0), (2, 1), (3, 0), (3, 1)):
             first_product(PACK + t, half, 1)
         for i in range(2):
-            nc.scalar.activation(logs[i][:, 0:S], squares[6 + i][:], ACT.Ln, bias=eps_third[:, i : i + 1])
+            nc.scalar.activation(logs[i][:, 0:S], squares[6 + i][:], ACT.Ln, bias=eps_share[:, i : i + 1])
 
         halves = [slice(0, HALF), slice(HALF, M)]
 
@@ -265,17 +261,17 @@ def tile_list_choir_blend_features_kernel(
         for i in range(2):
             for t in range(2):
                 nc.vector.tensor_copy(terms[t][:, i, :], squares[PACK + t][:].indirect(pos_sb[i][:]))
+        last_term = tile([P, M], F32, "last_term")
+        nc.vector.tensor_copy(last_term[:], squares[2 * PACK - 1][:].indirect(pos_sb[2][:]))
         rounded1.append(tile([P, N // 2, PACK], BF16, "w2_rounded1_1", "w2_rows1_0"))
         round_on_gpsimd(rounded1[1][:], w2_rows1[1][:])
-        rounded0 = tile([P, N // 2, PACK], BF16, "w2_rounded0_0")
-        round_on_gpsimd(rounded0[:], w2_rows0[:, :, columns[0]])
+        rounded0 = tile([P, N, PACK], BF16, "w2_rounded0")
+        round_on_gpsimd(rounded0[:], w2_rows0[:])
         for t in range(2):
             pick_and_add(terms[t][:, 2, :], PACK + t, 2, slice(0, M), so_far[PACK + t])
-        for g in range(2):
-            quantise_w2(1, 2 * g, rounded1[g], "squares%d" % (PACK + g))
         whole_tiles((0, 1))
-        picked = [tile([P, LISTS, M], F32, "picked%d" % i, ("eps_third", None)[i]) for i in range(2)]
-        by_scalar = [(i, k) for i in range(2) for k in range(LISTS)]
+        picked = [tile([P, LISTS - i, M], F32, "picked%d" % i, ("eps_share", None)[i]) for i in range(2)]
+        by_scalar = [(0, 0), (0, 1), (0, 2), (1, 0), (1, 1)]
 
         def pick_on_scalar(i, k):
             nc.scalar.activation(picked[i][:, k, :], logs[i][:].indirect(pos_sb[k][:]), ACT.Exp)
@@ -289,6 +285,7 @@ def tile_list_choir_blend_features_kernel(
         for i in range(LISTS):
             for t in range(2):
                 add_turned(t, terms[t][:, i, :], first=(i == 0 and t == 0))
+        add_turned(3, last_term[:])
         for i, k in by_scalar:
             add_turned(2 + i, picked[i][:, k, :], last=((i, k) == by_scalar[-1]))
         for pair in ((0, 1), (2, 3)):
@@ -350,15 +347,13 @@ def tile_list_choir_blend_features_kernel(
                     nc.sync.dma_start(out[P * n : P * (n + 1), halves[half]], result[:])
 
         z1 = [copy_back(0, nc.vector.tensor_copy)]
-        quantise_w2(0, 0, rounded0, "turned1")
-        second_product(0, 1, range(4), quantise("z1_0", None, z1[0]))
+        quantise_w2(1, 0, rounded1[0], "turned1")
+        z1_q = [quantise("z1_0", None, z1[0])]
+        second_product(0, 1, range(2), z1_q[0])
+        quantise_w2(1, 2, rounded1[1], "z1_0")
+        second_product(0, 1, range(2, 4), z1_q[0])
         z1.append(copy_back(1, nc.vector.tensor_copy))
-        z0_q = [quantise("z0_0", None, z0[0])]
-        second_product(0, 0, range(2), z0_q[0])
+        quantise_w2(0, 0, rounded0, "turned3")
+        second_product(0, 0, range(4), quantise("z0_0", None, z0[0]))
         second_product(1, 1, range(4), quantise("z1_1", "total0", z1[1]))
-        rounded = round_w2(1, "turned0")
-        z0_q.append(quantise("z0_1", None, z0[1]))
-        second_product(1, 0, range(2), z0_q[1])
-        quantise_w2(0, 2, rounded, "total1")
-        for half in range(2):
-            second_product(half, 0, range(2, 4), z0_q[half])
+        second_product(1, 0, range(4), quantise("z0_1", None, z0[1]))

@@ -163,15 +163,12 @@ def tile_list_choir_blend_features_kernel(
         nc.vector.tensor_copy(*by_lines(rounded1[0][:], w2_rows1[0][:]))
 
         logs = [tile([P, 2 * S], F32, "logs%d" % i) for i in range(2)]
-        eps_wide = tile([P, 2, M], F32, "eps_wide")
         for pair in range(2):
             nc.scalar.copy(
                 logs[pair][:, S : 2 * S].rearrange("p (t m) -> p t m", m=M),
                 eps_sb[:, 0, 2 * pair : 2 * pair + 2].unsqueeze(2).to_broadcast([P, 2, M]),
             )
-        nc.scalar.copy(eps_wide[:], eps_sb[:, 1, 0:2].unsqueeze(2).to_broadcast([P, 2, M]))
         spread = [logs[j // 2][:, S + M * (j % 2) : S + M * (j % 2 + 1)] for j in range(PACK)]
-        spread.extend(eps_wide[:, i, :] for i in range(2))
         warm = tile([P, 1], F32, "warm")
         nc.scalar.activation(warm[:], eps_sb[:, 0, 0:1], ACT.Ln)
 
@@ -181,7 +178,7 @@ def tile_list_choir_blend_features_kernel(
         def first_product(j, half, a):
             b, t = divmod(j, PACK)
             if a == 0:
-                h_banks[j, half] = bank([P, BANK], "h%d_%d" % (j, half), 2 * (j % 4) + half)
+                h_banks[j, half] = bank([P, BANK], "h%d_%d" % (j, half), 2 * (t if b == 1 else 2 + t % 2) + half)
             nc.tensor.matmul_mx(
                 out=h_banks[j, half][:],
                 lhsT=w4_codes[b][:, a, 2 * P * t : 2 * P * (t + 1)].bitcast(FP4X4),
@@ -224,10 +221,14 @@ def tile_list_choir_blend_features_kernel(
 
         totals = [tile([P, PACK, HALF], F32, "total%d" % half) for half in range(2)]
 
-        def last_picks(pair, so_far):
-            for half in range(2):
-                for j in pair:
-                    pick_and_add(totals[half][:, j, :], j, 2, halves[half], so_far[j][:, halves[half]])
+        root_steps = [[halves[0]], [slice(HALF, HALF + P), slice(HALF + P, M)]]
+
+        def within(half, beats):
+            return slice(beats.start - HALF * half, beats.stop - HALF * half)
+
+        def last_picks(pair, half, beats, so_far):
+            for j in pair:
+                pick_and_add(totals[half][:, j, within(half, beats)], j, 2, beats, so_far[j][:, beats])
 
         def add_turned(t, term, first=False, last=False):
             for c in range(M // P):
@@ -258,17 +259,16 @@ def tile_list_choir_blend_features_kernel(
 
         so_far = dict(enumerate(spread))
         terms = [tile([P, LISTS, M], F32, "terms%d" % t) for t in range(2)]
-        for i in range(2):
+        for i in range(LISTS):
             for t in range(2):
                 nc.vector.tensor_copy(terms[t][:, i, :], squares[PACK + t][:].indirect(pos_sb[i][:]))
         last_term = tile([P, M], F32, "last_term")
         nc.vector.tensor_copy(last_term[:], squares[2 * PACK - 1][:].indirect(pos_sb[2][:]))
         rounded1.append(tile([P, N // 2, PACK], BF16, "w2_rounded1_1", "w2_rows1_0"))
         round_on_gpsimd(rounded1[1][:], w2_rows1[1][:])
-        rounded0 = tile([P, N, PACK], BF16, "w2_rounded0")
-        round_on_gpsimd(rounded0[:], w2_rows0[:])
-        for t in range(2):
-            pick_and_add(terms[t][:, 2, :], PACK + t, 2, slice(0, M), so_far[PACK + t])
+        rounded0 = [tile([P, N // 2, PACK], BF16, "w2_rounded0_%d" % g) for g in range(2)]
+        for g in range(2):
+            round_on_gpsimd(rounded0[g][:], w2_rows0[:, :, columns[g]])
         whole_tiles((0, 1))
         picked = [tile([P, LISTS - i, M], F32, "picked%d" % i, ("eps_share", None)[i]) for i in range(2)]
         by_scalar = [(0, 0), (0, 1), (0, 2), (1, 0), (1, 1)]
@@ -282,17 +282,26 @@ def tile_list_choir_blend_features_kernel(
         for i, k in by_scalar[4:]:
             pick_on_scalar(i, k)
         sums = [bank([P, PASS], "sums%d" % c, c) for c in range(M // P)]
+        for t in range(2):
+            add_turned(t, eps_sb[:, 1, t : t + 1].to_broadcast([P, M]), first=(t == 0))
         for i in range(LISTS):
             for t in range(2):
-                add_turned(t, terms[t][:, i, :], first=(i == 0 and t == 0))
+                add_turned(t, terms[t][:, i, :])
         add_turned(3, last_term[:])
         for i, k in by_scalar:
             add_turned(2 + i, picked[i][:, k, :], last=((i, k) == by_scalar[-1]))
-        for pair in ((0, 1), (2, 3)):
-            for i in range(2):
-                for j in pair:
-                    so_far[j] = pick(j, i, so_far[j])
-            last_picks(pair, so_far)
+        for i in range(2):
+            for j in (0, 1):
+                so_far[j] = pick(j, i, so_far[j])
+        for half in range(2):
+            last_picks((0, 1), half, halves[half], so_far)
+        first = {j: pick(j, 0, so_far[j]) for j in (2, 3)}
+        second = {j: tile([P, M], F32, "second%d" % j, "part%d_1" % (j % 2))[:] for j in (2, 3)}
+        for half in range(2):
+            for j in (2, 3):
+                pick_and_add(second[j][:, halves[half]], j, 1, halves[half], first[j][:, halves[half]])
+            for beats in root_steps[half]:
+                last_picks((2, 3), half, beats, second)
 
         backs = [bank([P, 2, HALF], "back%d" % half, 4 + half) for half in range(2)]
 
@@ -321,10 +330,13 @@ def tile_list_choir_blend_features_kernel(
 
         for c in range(M // P):
             root_and_turn_back(c)
+        z1 = [copy_back(0, nc.scalar.copy)]
         z0 = []
         for half in range(2):
             z0.append(tile([P, HALF, PACK], BF16, "z0_%d" % half, "turned%d" % (2 * half)))
-            nc.scalar.activation(*by_lines(z0[half][:], totals[half][:]), ACT.Sqrt)
+            for beats in root_steps[half]:
+                part = within(half, beats)
+                nc.scalar.activation(*by_lines(z0[half][:, part, :], totals[half][:, :, part]), ACT.Sqrt)
 
         y_banks = {}
 
@@ -346,14 +358,19 @@ def tile_list_choir_blend_features_kernel(
                     nc.scalar.activation(result[:], y_banks[half, n][:], ACT.Silu)
                     nc.sync.dma_start(out[P * n : P * (n + 1), halves[half]], result[:])
 
-        z1 = [copy_back(0, nc.vector.tensor_copy)]
         quantise_w2(1, 0, rounded1[0], "turned1")
+        z1.append(copy_back(1, nc.vector.tensor_copy))
         z1_q = [quantise("z1_0", None, z1[0])]
         second_product(0, 1, range(2), z1_q[0])
-        quantise_w2(1, 2, rounded1[1], "z1_0")
-        second_product(0, 1, range(2, 4), z1_q[0])
-        z1.append(copy_back(1, nc.vector.tensor_copy))
-        quantise_w2(0, 0, rounded0, "turned3")
-        second_product(0, 0, range(4), quantise("z0_0", None, z0[0]))
-        second_product(1, 1, range(4), quantise("z1_1", "total0", z1[1]))
+        quantise_w2(0, 0, rounded0[0], "turned3")
+        z1_q.append(quantise("z1_1", None, z1[1]))
+        second_product(1, 1, range(2), z1_q[1])
+        z0_q = [quantise("z0_0", None, z0[0])]
+        second_product(0, 0, range(2), z0_q[0])
+        quantise_w2(1, 2, rounded1[1], "total0")
+        quantise_w2(0, 2, rounded0[1], "turned0")
+        for n in (2, 3):
+            second_product(0, 1, [n], z1_q[0])
+            second_product(0, 0, [n], z0_q[0])
+        second_product(1, 1, range(2, 4), z1_q[1])
         second_product(1, 0, range(4), quantise("z0_1", None, z0[1]))

@@ -28,6 +28,7 @@ PER_COLUMN = 16
 QUADRANT = 32
 LINE = 4
 LISTS = 3
+AHEAD = T // 4
 
 
 def tile_list_choir_blend_features_kernel(
@@ -118,8 +119,9 @@ def tile_list_choir_blend_features_kernel(
                     picked_scales[16 * a + r : 16 * (a + 1) : 4, :].bitcast(I32),
                 )
 
+        nc.sync.dma_start(words[1][:, 0:AHEAD], tab[1][:, 0:AHEAD])
         move_scale_rows(0)
-        nc.sync.dma_start(words[1][:], tab[1])
+        nc.sync.dma_start(words[1][:, AHEAD:T], tab[1][:, AHEAD:T])
         move_scale_rows(1)
         w4_raw0 = load_w4_words(0)
         columns = [slice(0, N // 2), slice(N // 2, N)]

@@ -333,6 +333,17 @@ def tile_list_choir_blend_features_kernel(
         for c in range(M // P):
             root_and_turn_back(c)
         z1 = [copy_back(0, nc.scalar.copy)]
+        unread = bank([P, BANK], "unread", 3)
+        for j in range(4):
+            nc.tensor.matmul_mx(
+                out=unread[:],
+                lhsT=w4_codes[0][:, 0, 2 * P * j : 2 * P * (j + 1)].bitcast(FP4X4),
+                lhsT_scale=w4_planes[:, 0, P * j : P * (j + 1)],
+                rhs=v_codes[0, 0].bitcast(FP8X4),
+                rhs_scale=planes[0][:, 0:BANK],
+                start=True,
+                stop=True,
+            )
         z0 = []
         for half in range(2):
             z0.append(tile([P, HALF, PACK], BF16, "z0_%d" % half, "turned%d" % (2 * half)))

@@ -140,8 +140,7 @@ def tile_list_choir_blend_features_kernel(
         eps_sb = tile([P, 2, PACK], F32, "eps_sb")
         nc.scalar.copy(eps_sb[:], eps_turned[:, :, 0 : 2 * QUADRANT : QUADRANT].rearrange("p t b -> p b t"))
         eps_share = tile([P, 2], F32, "eps_share")
-        for i, shares in enumerate((3, 2)):
-            nc.scalar.mul(eps_share[:, i : i + 1], eps_turned[:, 2 + i, QUADRANT : QUADRANT + 1], 1.0 / shares)
+        nc.scalar.mul(eps_share[:], eps_turned[:, 2:4, QUADRANT], 1.0 / LISTS)
 
         v_codes = {}
 
@@ -161,8 +160,6 @@ def tile_list_choir_blend_features_kernel(
             w4_raw0[:].bitcast(I32).rearrange("p a (g t v) -> p a t g v", t=PACK, v=4),
         )
         w4_codes = [w4_dealt, w4_raw1]
-        rounded1 = [tile([P, N // 2, PACK], BF16, "w2_rounded1_0")]
-        nc.vector.tensor_copy(*by_lines(rounded1[0][:], w2_rows1[0][:]))
 
         logs = [tile([P, 2 * S], F32, "logs%d" % i) for i in range(2)]
         for pair in range(2):
@@ -174,7 +171,8 @@ def tile_list_choir_blend_features_kernel(
         warm = tile([P, 1], F32, "warm")
         nc.scalar.activation(warm[:], eps_sb[:, 0, 0:1], ACT.Ln)
 
-        squares = [tile([P, S], F32, "squares%d" % j) for j in range(2 * PACK)]
+        squares = [tile([P, S], F32, "squares%d" % j) for j in range(2 * PACK - 1)]
+        squares.append(tile([P, S], F32, "squares7", "w4_raw0"))
         h_banks = {}
 
         def first_product(j, half, a):
@@ -190,13 +188,17 @@ def tile_list_choir_blend_features_kernel(
                 start=(a == 0),
                 stop=(a == 1),
             )
-            if a == 1:
+            if a == 1 and (j, half) == (2 * PACK - 1, 0):
+                h_copy = tile([P, BANK], F32, "h_copy")
+                nc.vector.tensor_copy(h_copy[:], h_banks[j, half][:])
+                nc.gpsimd.tensor_tensor(squares[j][:, 0:BANK], h_copy[:], h_copy[:], MULT)
+            elif a == 1:
                 nc.scalar.activation(squares[j][:, BANK * half : BANK * (half + 1)], h_banks[j, half][:], ACT.Square)
 
         for half in range(2):
             for j in range(PACK, 2 * PACK):
                 first_product(j, half, 0)
-        for t, half in ((0, 0), (1, 0), (0, 1), (1, 1), (2, 0), (2, 1), (3, 0), (3, 1)):
+        for t, half in ((0, 0), (3, 0), (0, 1), (1, 0), (1, 1), (2, 0), (2, 1), (3, 1)):
             first_product(PACK + t, half, 1)
         for i in range(2):
             nc.scalar.activation(logs[i][:, 0:S], squares[6 + i][:], ACT.Ln, bias=eps_share[:, i : i + 1])
@@ -217,20 +219,11 @@ def tile_list_choir_blend_features_kernel(
             codes = tile([P, width], U32, name + "_codes", tag)
             plane = tile([P, width], U8, name + "_plane")
             nc.vector.quantize_mx(
-                out=codes[:].bitcast(FP8X4), scales=plane[:], in_=rounded[:].rearrange("p m t -> p (m t)")
+                out=codes[:].bitcast(FP8X4), scales=plane[:], in_=rounded.rearrange("p m t -> p (m t)")
             )
             return codes, plane
 
         totals = [tile([P, PACK, HALF], F32, "total%d" % half) for half in range(2)]
-
-        root_steps = [[halves[0]], [slice(HALF, HALF + P), slice(HALF + P, M)]]
-
-        def within(half, beats):
-            return slice(beats.start - HALF * half, beats.stop - HALF * half)
-
-        def last_picks(pair, half, beats, so_far):
-            for j in pair:
-                pick_and_add(totals[half][:, j, within(half, beats)], j, 2, beats, so_far[j][:, beats])
 
         def add_turned(t, term, first=False, last=False):
             for c in range(M // P):
@@ -264,16 +257,15 @@ def tile_list_choir_blend_features_kernel(
         for i in range(LISTS):
             for t in range(2):
                 nc.vector.tensor_copy(terms[t][:, i, :], squares[PACK + t][:].indirect(pos_sb[i][:]))
-        last_term = tile([P, M], F32, "last_term")
-        nc.vector.tensor_copy(last_term[:], squares[2 * PACK - 1][:].indirect(pos_sb[2][:]))
-        rounded1.append(tile([P, N // 2, PACK], BF16, "w2_rounded1_1", "w2_rows1_0"))
-        round_on_gpsimd(rounded1[1][:], w2_rows1[1][:])
-        rounded0 = [tile([P, N // 2, PACK], BF16, "w2_rounded0_%d" % g) for g in range(2)]
-        for g in range(2):
-            round_on_gpsimd(rounded0[g][:], w2_rows0[:, :, columns[g]])
+        rounded1 = []
+        for g, tag in enumerate(("h_copy", "w2_rows1_0")):
+            rounded1.append(tile([P, N // 2, PACK], BF16, "w2_rounded1_%d" % g, tag))
+            round_on_gpsimd(rounded1[g][:], w2_rows1[g][:])
+        rounded0 = tile([P, N, PACK], BF16, "w2_rounded0")
+        round_on_gpsimd(rounded0[:], w2_rows0[:])
         whole_tiles((0, 1))
-        picked = [tile([P, LISTS - i, M], F32, "picked%d" % i, ("eps_share", None)[i]) for i in range(2)]
-        by_scalar = [(0, 0), (0, 1), (0, 2), (1, 0), (1, 1)]
+        picked = [tile([P, LISTS, M], F32, "picked%d" % i, ("eps_share", None)[i]) for i in range(2)]
+        by_scalar = [(i, k) for i in range(2) for k in range(LISTS)]
 
         def pick_on_scalar(i, k):
             nc.scalar.activation(picked[i][:, k, :], logs[i][:].indirect(pos_sb[k][:]), ACT.Exp)
@@ -289,21 +281,15 @@ def tile_list_choir_blend_features_kernel(
         for i in range(LISTS):
             for t in range(2):
                 add_turned(t, terms[t][:, i, :])
-        add_turned(3, last_term[:])
         for i, k in by_scalar:
             add_turned(2 + i, picked[i][:, k, :], last=((i, k) == by_scalar[-1]))
-        for i in range(2):
-            for j in (0, 1):
-                so_far[j] = pick(j, i, so_far[j])
-        for half in range(2):
-            last_picks((0, 1), half, halves[half], so_far)
-        first = {j: pick(j, 0, so_far[j]) for j in (2, 3)}
-        second = {j: tile([P, M], F32, "second%d" % j, "part%d_1" % (j % 2))[:] for j in (2, 3)}
-        for half in range(2):
-            for j in (2, 3):
-                pick_and_add(second[j][:, halves[half]], j, 1, halves[half], first[j][:, halves[half]])
-            for beats in root_steps[half]:
-                last_picks((2, 3), half, beats, second)
+        for pair in ((0, 1), (2, 3)):
+            for i in range(2):
+                for j in pair:
+                    so_far[j] = pick(j, i, so_far[j])
+            for half in range(2):
+                for j in pair:
+                    pick_and_add(totals[half][:, j, :], j, 2, halves[half], so_far[j][:, halves[half]])
 
         backs = [bank([P, 2, HALF], "back%d" % half, 4 + half) for half in range(2)]
 
@@ -322,9 +308,9 @@ def tile_list_choir_blend_features_kernel(
                     identity[:],
                 )
 
-        def copy_back(half, copy):
+        def copy_back(half):
             z = tile([P, HALF, PACK], BF16, "z1_%d" % half)
-            copy(
+            nc.vector.tensor_copy(
                 z[:].rearrange("p m t -> p (m t)").bitcast(F32).rearrange("p (m u) -> p m u", u=2),
                 backs[half][:].rearrange("p u m -> p m u"),
             )
@@ -332,7 +318,6 @@ def tile_list_choir_blend_features_kernel(
 
         for c in range(M // P):
             root_and_turn_back(c)
-        z1 = [copy_back(0, nc.scalar.copy)]
         unread = bank([P, BANK], "unread", 3)
         for j in range(4):
             nc.tensor.matmul_mx(
@@ -347,9 +332,7 @@ def tile_list_choir_blend_features_kernel(
         z0 = []
         for half in range(2):
             z0.append(tile([P, HALF, PACK], BF16, "z0_%d" % half, "turned%d" % (2 * half)))
-            for beats in root_steps[half]:
-                part = within(half, beats)
-                nc.scalar.activation(*by_lines(z0[half][:, part, :], totals[half][:, :, part]), ACT.Sqrt)
+            nc.scalar.activation(*by_lines(z0[half][:], totals[half][:]), ACT.Sqrt)
 
         y_banks = {}
 
@@ -371,19 +354,21 @@ def tile_list_choir_blend_features_kernel(
                     nc.scalar.activation(result[:], y_banks[half, n][:], ACT.Silu)
                     nc.sync.dma_start(out[P * n : P * (n + 1), halves[half]], result[:])
 
-        quantise_w2(1, 0, rounded1[0], "turned1")
-        z1.append(copy_back(1, nc.vector.tensor_copy))
-        z1_q = [quantise("z1_0", None, z1[0])]
+        z1 = [copy_back(0)]
+        quantise_w2(1, 0, rounded1[0][:], "turned1")
+        z1_q = [quantise("z1_0", None, z1[0][:])]
         second_product(0, 1, range(2), z1_q[0])
-        quantise_w2(0, 0, rounded0[0], "turned3")
-        z1_q.append(quantise("z1_1", None, z1[1]))
-        second_product(1, 1, range(2), z1_q[1])
-        z0_q = [quantise("z0_0", None, z0[0])]
+        z1.append(copy_back(1))
+        quantise_w2(0, 0, rounded0[:, columns[0], :], "turned3")
+        z0_q = [quantise("z0_0", None, z0[0][:])]
         second_product(0, 0, range(2), z0_q[0])
-        quantise_w2(1, 2, rounded1[1], "total0")
-        quantise_w2(0, 2, rounded0[1], "turned0")
+        quantise_w2(1, 2, rounded1[1][:], "total0")
+        quantise_w2(0, 2, rounded0[:, columns[1], :], "turned0")
         for n in (2, 3):
             second_product(0, 1, [n], z1_q[0])
             second_product(0, 0, [n], z0_q[0])
-        second_product(1, 1, range(2, 4), z1_q[1])
-        second_product(1, 0, range(4), quantise("z0_1", None, z0[1]))
+        z1_q.append(quantise("z1_1", "total1", z1[1][:]))
+        z0_q.append(quantise("z0_1", None, z0[1][:]))
+        for n in range(4):
+            second_product(1, 1, [n], z1_q[1])
+            second_product(1, 0, [n], z0_q[1])

@@ -26,9 +26,15 @@ BANK = 512
 HALF = M // 2
 PER_COLUMN = 16
 QUADRANT = 32
+LIVE = 4
+BLOCKS = PASS // 32
 LINE = 4
 LISTS = 3
+DEALT, TURNED = 0, 1
 AHEAD = T // 4
+LOGGED = (6, 7)
+HANDED_OVER = (7, 0)
+WARM_PASSES = 4
 
 
 def tile_list_choir_blend_features_kernel(
@@ -65,47 +71,42 @@ def tile_list_choir_blend_features_kernel(
         eps_rows = tile([2 * QUADRANT, PASS], F32, "eps_rows")
         nc.sync.dma_start(eps_rows[0 : 2 * QUADRANT : QUADRANT, :], eps.rearrange("(b r) -> b r", b=2))
         w4_rows = tile([P, 2, H], U8, "w4_rows")
-        for r in range(4):
+        for row in range(LIVE):
             nc.sync.dma_start(
-                w4_rows[r:P:QUADRANT, :, :].bitcast(I32),
-                w4_scales[:, r:16:4, :].rearrange("a q c -> q a c").bitcast(I32),
+                w4_rows[row:P:QUADRANT, :, :].bitcast(I32),
+                w4_scales[:, row:BLOCKS:LIVE, :].rearrange("a q c -> q a c").bitcast(I32),
             )
         words = [tile([P, T], I32, "words%d" % a) for a in range(2)]
         nc.sync.dma_start(words[0][:], tab[0])
-        w4_raw1 = load_w4_words(1)
+        w4_turned = load_w4_words(TURNED)
         nc.vector.memset(scale_rows[QUADRANT : 2 * QUADRANT, :].bitcast(I32), 0)
         nc.vector.memset(scale_rows[2 * QUADRANT : P, :].bitcast(I32), 0)
-        planes = [tile([P, S], U8, "planes%d" % a) for a in range(2)]
+        v_planes = [tile([P, S], U8, "v_plane%d" % a) for a in range(2)]
         for a in range(2):
-            nc.vector.memset(planes[a][:].bitcast(I32), 0)
+            nc.vector.memset(v_planes[a][:].bitcast(I32), 0)
 
-        eps_dealt = tile([P, PACK, P], F32, "eps_dealt")
-        nc.gpsimd.memset(eps_dealt[:], 0.0)
+        eps_ordered = tile([P, PACK, P], F32, "eps_ordered")
+        nc.gpsimd.memset(eps_ordered[:], 0.0)
         identity = tile([P, P], F32, "identity")
         make_identity(nc, identity[:])
         nc.scalar.copy(
-            eps_dealt[0:1, :, :].rearrange("b t (g u) -> b t g u", u=RUN),
+            eps_ordered[0:1, :, :].rearrange("b t (g u) -> b t g u", u=RUN),
             eps_rows[0:1, :].rearrange("b (g t u) -> b t g u", t=PACK, u=RUN),
         )
         nc.scalar.copy(
-            eps_dealt[QUADRANT : QUADRANT + 1, :, :].rearrange("b t p -> b (t p)"), eps_rows[QUADRANT : QUADRANT + 1, :]
+            eps_ordered[QUADRANT : QUADRANT + 1, :, :].rearrange("b t p -> b (t p)"),
+            eps_rows[QUADRANT : QUADRANT + 1, :],
         )
-        eps_turned = bank([P, PACK, P], "eps_turned", 7)
+        eps_psum = bank([P, PACK, P], "eps_psum", 7)
         for t in range(PACK):
-            nc.tensor.transpose(eps_turned[:, t, :], eps_dealt[:, t, :], identity[:])
-
-        def by_lines(dst, src):
-            return (
-                dst.rearrange("p (c i) t -> p c t i", i=LINE),
-                src.rearrange("p t (c i) -> p c t i", i=LINE),
-            )
+            nc.tensor.transpose(eps_psum[:, t, :], eps_ordered[:, t, :], identity[:])
 
         picked_scales = tile([P, S], U8, "picked_scales")
         nc.vector.tensor_copy(picked_scales[:], scale_rows[:].indirect(offs_sb[:]))
         w4_planes = tile([P, 2, H], U8, "w4_planes", "scale_rows")
         nc.vector.memset(w4_planes[:].bitcast(I32), 0)
-        for quad in range(4):
-            live = slice(QUADRANT * quad, QUADRANT * quad + 4)
+        for quad in range(P // QUADRANT):
+            live = slice(QUADRANT * quad, QUADRANT * quad + LIVE)
             nc.vector.tensor_copy(
                 w4_planes[live, :, 0:PASS].bitcast(I32).rearrange("p a (t g v) -> p a t g v", t=PACK, v=2),
                 w4_rows[live, :, 0:PASS].bitcast(I32).rearrange("p a (g t v) -> p a t g v", t=PACK, v=2),
@@ -113,117 +114,126 @@ def tile_list_choir_blend_features_kernel(
             nc.vector.tensor_copy(w4_planes[live, :, PASS:H].bitcast(I32), w4_rows[live, :, PASS:H].bitcast(I32))
 
         def move_scale_rows(a):
-            for r in range(4):
+            for row in range(LIVE):
                 nc.sync.dma_start(
-                    planes[a][r:P:QUADRANT, :].bitcast(I32),
-                    picked_scales[16 * a + r : 16 * (a + 1) : 4, :].bitcast(I32),
+                    v_planes[a][row:P:QUADRANT, :].bitcast(I32),
+                    picked_scales[BLOCKS * a + row : BLOCKS * (a + 1) : LIVE, :].bitcast(I32),
                 )
 
         nc.sync.dma_start(words[1][:, 0:AHEAD], tab[1][:, 0:AHEAD])
         move_scale_rows(0)
         nc.sync.dma_start(words[1][:, AHEAD:T], tab[1][:, AHEAD:T])
         move_scale_rows(1)
-        w4_raw0 = load_w4_words(0)
-        columns = [slice(0, N // 2), slice(N // 2, N)]
-        w2_rows1 = [tile([P, PACK, N // 2], F32, "w2_rows1_%d" % g) for g in range(2)]
-        rows = w2[PASS:H, :].rearrange("(p t) n -> p t n", t=PACK)
-        nc.sync.dma_start(w2_rows1[0][:], rows[:, :, columns[0]])
+        w4_raw = load_w4_words(DEALT)
         nc.sync.dma_start(pos_sb[0][:], pos1)
+        columns = [slice(0, N // 2), slice(N // 2, N)]
+        w2_turned = [tile([P, PACK, N // 2], F32, "w2_turned%d" % g) for g in range(2)]
+        turned_rows = w2[PASS:H, :].rearrange("(p i) n -> p i n", i=PACK)
+        nc.sync.dma_start(w2_turned[0][:], turned_rows[:, :, columns[0]])
         nc.sync.dma_start(pos_sb[1][:], pos2)
-        nc.sync.dma_start(w2_rows1[1][:], rows[:, :, columns[1]])
+        nc.sync.dma_start(w2_turned[1][:], turned_rows[:, :, columns[1]])
         nc.sync.dma_start(pos_sb[2][:], pos3)
-        w2_rows0 = tile([P, PACK, N], F32, "w2_rows0")
-        rows = w2[0:PASS, :].rearrange("(g t u) n -> t g u n", t=PACK, u=RUN)
+        w2_dealt = tile([P, PACK, N], F32, "w2_dealt")
+        dealt_rows = w2[0:PASS, :].rearrange("(g t u) n -> t g u n", t=PACK, u=RUN)
         for t in range(PACK):
-            nc.sync.dma_start(w2_rows0[:, t, :], rows[t])
+            nc.sync.dma_start(w2_dealt[:, t, :], dealt_rows[t])
 
         eps_sb = tile([P, 2, PACK], F32, "eps_sb")
-        nc.scalar.copy(eps_sb[:], eps_turned[:, :, 0 : 2 * QUADRANT : QUADRANT].rearrange("p t b -> p b t"))
-        eps_share = tile([P, 2], F32, "eps_share")
-        nc.scalar.mul(eps_share[:], eps_turned[:, 2:4, QUADRANT], 1.0 / LISTS)
+        nc.scalar.copy(eps_sb[:], eps_psum[:, :, 0 : 2 * QUADRANT : QUADRANT].rearrange("p t b -> p b t"))
+        eps_third = tile([P, len(LOGGED)], F32, "eps_third")
+        nc.scalar.mul(eps_third[:], eps_psum[:, LOGGED[0] - PACK : PACK, QUADRANT], 1.0 / LISTS)
 
         v_codes = {}
-
-        def pick_words(a, half):
-            codes = tile([P, BANK], U32, "v_codes%d_%d" % (a, half))
-            entries = slice(BANK * half // PER_COLUMN, BANK * (half + 1) // PER_COLUMN)
-            nc.vector.tensor_copy(codes[:], words[a][:].bitcast(U32).indirect(offs_sb[:, entries]))
-            v_codes[a, half] = codes[:]
-
         for a in range(2):
             for half in range(2):
-                pick_words(a, half)
+                codes = tile([P, BANK], U32, "v_codes%d_%d" % (a, half))
+                entries = slice(BANK * half // PER_COLUMN, BANK * (half + 1) // PER_COLUMN)
+                nc.vector.tensor_copy(codes[:], words[a][:].bitcast(U32).indirect(offs_sb[:, entries]))
+                v_codes[a, half] = codes[:]
 
         w4_dealt = tile([P, 2, 2 * PASS], U8, "w4_dealt")
         nc.vector.tensor_copy(
             w4_dealt[:].bitcast(I32).rearrange("p a (t g v) -> p a t g v", t=PACK, v=4),
-            w4_raw0[:].bitcast(I32).rearrange("p a (g t v) -> p a t g v", t=PACK, v=4),
+            w4_raw[:].bitcast(I32).rearrange("p a (g t v) -> p a t g v", t=PACK, v=4),
         )
-        w4_codes = [w4_dealt, w4_raw1]
+        w4_codes = {DEALT: w4_dealt, TURNED: w4_turned}
 
-        logs = [tile([P, 2 * S], F32, "logs%d" % i) for i in range(2)]
+        logs = [tile([P, 2 * S], F32, "logs%d" % i) for i in range(len(LOGGED))]
         for pair in range(2):
             nc.scalar.copy(
                 logs[pair][:, S : 2 * S].rearrange("p (t m) -> p t m", m=M),
-                eps_sb[:, 0, 2 * pair : 2 * pair + 2].unsqueeze(2).to_broadcast([P, 2, M]),
+                eps_sb[:, DEALT, 2 * pair : 2 * pair + 2].unsqueeze(2).to_broadcast([P, 2, M]),
             )
-        spread = [logs[j // 2][:, S + M * (j % 2) : S + M * (j % 2 + 1)] for j in range(PACK)]
+        so_far = {j: logs[j // 2][:, S + M * (j % 2) : S + M * (j % 2 + 1)] for j in range(PACK)}
         warm = tile([P, 1], F32, "warm")
-        nc.scalar.activation(warm[:], eps_sb[:, 0, 0:1], ACT.Ln)
+        nc.scalar.activation(warm[:], eps_sb[:, DEALT, 0:1], ACT.Ln)
+
+        def round_on_gpsimd(name, tag, rows):
+            rounded = tile([P, rows.shape[2], PACK], BF16, name, tag)
+            nc.gpsimd.tensor_scalar(rounded[:], rows.rearrange("p t n -> p n t"), 1.0, 0.0, MULT, ADD)
+            return rounded
 
         squares = [tile([P, S], F32, "squares%d" % j) for j in range(2 * PACK - 1)]
-        squares.append(tile([P, S], F32, "squares7", "w4_raw0"))
+        rounded_turned = [round_on_gpsimd("rounded_turned0", "w4_raw%d" % DEALT, w2_turned[0][:])]
+        squares.append(tile([P, S], F32, "squares7", "w2_turned0"))
         h_banks = {}
 
         def first_product(j, half, a):
             b, t = divmod(j, PACK)
             if a == 0:
-                h_banks[j, half] = bank([P, BANK], "h%d_%d" % (j, half), 2 * (t if b == 1 else 2 + t % 2) + half)
+                h_banks[j, half] = bank([P, BANK], "h%d_%d" % (j, half), 2 * (t if b == TURNED else t % 2) + half)
             nc.tensor.matmul_mx(
                 out=h_banks[j, half][:],
                 lhsT=w4_codes[b][:, a, 2 * P * t : 2 * P * (t + 1)].bitcast(FP4X4),
                 lhsT_scale=w4_planes[:, a, P * j : P * (j + 1)],
                 rhs=v_codes[a, half].bitcast(FP8X4),
-                rhs_scale=planes[a][:, BANK * half : BANK * (half + 1)],
+                rhs_scale=v_planes[a][:, BANK * half : BANK * (half + 1)],
                 start=(a == 0),
                 stop=(a == 1),
             )
-            if a == 1 and (j, half) == (2 * PACK - 1, 0):
-                h_copy = tile([P, BANK], F32, "h_copy")
-                nc.vector.tensor_copy(h_copy[:], h_banks[j, half][:])
-                nc.gpsimd.tensor_tensor(squares[j][:, 0:BANK], h_copy[:], h_copy[:], MULT)
-            elif a == 1:
-                nc.scalar.activation(squares[j][:, BANK * half : BANK * (half + 1)], h_banks[j, half][:], ACT.Square)
+            if a == 1:
+                frames = slice(BANK * half, BANK * (half + 1))
+                if (j, half) == HANDED_OVER:
+                    h_copy = tile([P, BANK], F32, "h_copy")
+                    nc.vector.tensor_copy(h_copy[:], h_banks[j, half][:])
+                    nc.gpsimd.tensor_tensor(squares[j][:, frames], h_copy[:], h_copy[:], MULT)
+                else:
+                    nc.scalar.activation(squares[j][:, frames], h_banks[j, half][:], ACT.Square)
+
+        def whole_tiles(pair):
+            for j in pair:
+                for half in range(2):
+                    for a in range(2):
+                        first_product(j, half, a)
 
         for half in range(2):
             for j in range(PACK, 2 * PACK):
                 first_product(j, half, 0)
-        for t, half in ((0, 0), (3, 0), (0, 1), (1, 0), (1, 1), (2, 0), (2, 1), (3, 1)):
-            first_product(PACK + t, half, 1)
-        for i in range(2):
-            nc.scalar.activation(logs[i][:, 0:S], squares[6 + i][:], ACT.Ln, bias=eps_share[:, i : i + 1])
+        for j, half in ((4, 0), (5, 0), HANDED_OVER, (4, 1), (5, 1), (6, 0), (6, 1), (7, 1)):
+            first_product(j, half, 1)
+        for i, j in enumerate(LOGGED):
+            nc.scalar.activation(logs[i][:, 0:S], squares[j][:], ACT.Ln, bias=eps_third[:, i : i + 1])
 
-        halves = [slice(0, HALF), slice(HALF, M)]
+        terms = [tile([P, LISTS, M], F32, "terms%d" % t) for t in range(2)]
+        for i in range(LISTS):
+            for t in range(2):
+                nc.vector.tensor_copy(terms[t][:, i, :], squares[PACK + t][:].indirect(pos_sb[i][:]))
+        rounded_turned.append(round_on_gpsimd("rounded_turned1", "h_copy", w2_turned[1][:]))
+        rounded_dealt = round_on_gpsimd("rounded_dealt", None, w2_dealt[:])
+        whole_tiles((0, 1))
+        picked = [tile([P, LISTS, M], F32, "picked%d" % i, ("eps_third", None)[i]) for i in range(len(LOGGED))]
+        by_scalar = [(i, k) for i in range(len(LOGGED)) for k in range(LISTS)]
 
-        def pick_and_add(dst, j, i, beats, so_far):
-            entries = slice(beats.start // PER_COLUMN, beats.stop // PER_COLUMN)
-            nc.vector.tensor_tensor(dst, squares[j][:].indirect(pos_sb[i][:, entries]), so_far, ADD)
+        def pick_on_scalar(i, k):
+            nc.scalar.activation(picked[i][:, k, :], logs[i][:].indirect(pos_sb[k][:]), ACT.Exp)
 
-        def pick(j, i, so_far):
-            part = tile([P, M], F32, "part%d_%d" % (j, i), "part%d_%d" % (j % 2, i))
-            pick_and_add(part[:], j, i, slice(0, M), so_far)
-            return part[:]
+        for i, k in by_scalar[:LISTS]:
+            pick_on_scalar(i, k)
+        whole_tiles((2, 3))
+        for i, k in by_scalar[LISTS:]:
+            pick_on_scalar(i, k)
 
-        def quantise(name, tag, rounded):
-            width = rounded.shape[1]
-            codes = tile([P, width], U32, name + "_codes", tag)
-            plane = tile([P, width], U8, name + "_plane")
-            nc.vector.quantize_mx(
-                out=codes[:].bitcast(FP8X4), scales=plane[:], in_=rounded.rearrange("p m t -> p (m t)")
-            )
-            return codes, plane
-
-        totals = [tile([P, PACK, HALF], F32, "total%d" % half) for half in range(2)]
+        sums = [bank([P, PASS], "sums%d" % c, PACK + c) for c in range(M // P)]
 
         def add_turned(t, term, first=False, last=False):
             for c in range(M // P):
@@ -236,139 +246,146 @@ def tile_list_choir_blend_features_kernel(
                     stop=last,
                 )
 
-        w2_q = {}
-
-        def quantise_w2(b, first, rounded, tag):
-            codes, plane = quantise("w2_%d_%d" % (b, first), tag, rounded)
-            for n in range(rounded.shape[1] // P):
-                w2_q[b, first + n] = (codes[:, P * n : P * (n + 1)], plane[:, P * n : P * (n + 1)])
-
-        def whole_tiles(pair):
-            for j in pair:
-                for half in range(2):
-                    for a in range(2):
-                        first_product(j, half, a)
-
-        def round_on_gpsimd(dst, src):
-            nc.gpsimd.tensor_scalar(dst, src.rearrange("p t n -> p n t"), 1.0, 0.0, MULT, ADD)
-
-        so_far = dict(enumerate(spread))
-        terms = [tile([P, LISTS, M], F32, "terms%d" % t) for t in range(2)]
-        for i in range(LISTS):
-            for t in range(2):
-                nc.vector.tensor_copy(terms[t][:, i, :], squares[PACK + t][:].indirect(pos_sb[i][:]))
-        rounded1 = []
-        for g, tag in enumerate(("h_copy", "w2_rows1_0")):
-            rounded1.append(tile([P, N // 2, PACK], BF16, "w2_rounded1_%d" % g, tag))
-            round_on_gpsimd(rounded1[g][:], w2_rows1[g][:])
-        rounded0 = tile([P, N, PACK], BF16, "w2_rounded0")
-        round_on_gpsimd(rounded0[:], w2_rows0[:])
-        whole_tiles((0, 1))
-        picked = [tile([P, LISTS, M], F32, "picked%d" % i, ("eps_share", None)[i]) for i in range(2)]
-        by_scalar = [(i, k) for i in range(2) for k in range(LISTS)]
-
-        def pick_on_scalar(i, k):
-            nc.scalar.activation(picked[i][:, k, :], logs[i][:].indirect(pos_sb[k][:]), ACT.Exp)
-
-        for i, k in by_scalar[:4]:
-            pick_on_scalar(i, k)
-        whole_tiles((2, 3))
-        for i, k in by_scalar[4:]:
-            pick_on_scalar(i, k)
-        sums = [bank([P, PASS], "sums%d" % c, c) for c in range(M // P)]
         for t in range(2):
-            add_turned(t, eps_sb[:, 1, t : t + 1].to_broadcast([P, M]), first=(t == 0))
+            add_turned(t, eps_sb[:, TURNED, t : t + 1].to_broadcast([P, M]), first=(t == 0))
         for i in range(LISTS):
             for t in range(2):
                 add_turned(t, terms[t][:, i, :])
         for i, k in by_scalar:
-            add_turned(2 + i, picked[i][:, k, :], last=((i, k) == by_scalar[-1]))
-        for pair in ((0, 1), (2, 3)):
-            for i in range(2):
-                for j in pair:
-                    so_far[j] = pick(j, i, so_far[j])
-            for half in range(2):
-                for j in pair:
-                    pick_and_add(totals[half][:, j, :], j, 2, halves[half], so_far[j][:, halves[half]])
+            add_turned(LOGGED[i] - PACK, picked[i][:, k, :], last=((i, k) == by_scalar[-1]))
 
-        backs = [bank([P, 2, HALF], "back%d" % half, 4 + half) for half in range(2)]
+        halves = [slice(0, HALF), slice(HALF, M)]
+        totals = [tile([P, PACK, HALF], F32, "total%d" % half) for half in range(2)]
 
-        def root_and_turn_back(c):
+        def pick_and_add(dst, j, i, beats, before):
+            entries = slice(beats.start // PER_COLUMN, beats.stop // PER_COLUMN)
+            nc.vector.tensor_tensor(dst, squares[j][:].indirect(pos_sb[i][:, entries]), before[:, beats], ADD)
+
+        part_tags = [("squares%d" % (PACK + t), "second_sum%d" % t) for t in range(2)]
+        root_steps = [[halves[0]], [slice(HALF, M - HALF // 2), slice(M - HALF // 2, M)]]
+
+        def within(half, beats):
+            return slice(beats.start - HALF * half, beats.stop - HALF * half)
+
+        def whole_list(pair, i):
+            for j in pair:
+                part = tile([P, M], F32, "part%d_%d" % (j, i), part_tags[j % 2][i])
+                pick_and_add(part[:], j, i, slice(0, M), so_far[j])
+                so_far[j] = part[:]
+
+        def last_list(pair, half, beats, before):
+            for j in pair:
+                pick_and_add(totals[half][:, j, within(half, beats)], j, LISTS - 1, beats, before[j])
+
+        for i in range(LISTS - 1):
+            whole_list((0, 1), i)
+        for half in range(2):
+            last_list((0, 1), half, halves[half], so_far)
+        whole_list((2, 3), 0)
+        second = {j: tile([P, M], F32, "part%d_1" % j, part_tags[j % 2][1])[:] for j in (2, 3)}
+        for half in range(2):
+            for j in (2, 3):
+                pick_and_add(second[j][:, halves[half]], j, 1, halves[half], so_far[j])
+            for beats in root_steps[half]:
+                last_list((2, 3), half, beats, second)
+
+        backs = [bank([P, 2, HALF], "back%d" % half, half) for half in range(2)]
+        for c in range(M // P):
             half, part = divmod(c, 2)
-            turned = tile([P, PASS], BF16, "turned%d" % c)
+            roots = tile([P, PASS], BF16, "roots%d" % c)
             nc.scalar.activation(
-                turned[:].rearrange("m (u p e) -> m u p e", u=2, e=2),
+                roots[:].rearrange("m (u p e) -> m u p e", u=2, e=2),
                 sums[c][:].rearrange("m (p u e) -> m u p e", u=2, e=2),
                 ACT.Sqrt,
             )
             for u in range(2):
                 nc.tensor.transpose(
                     backs[half][:, u, P * part : P * (part + 1)],
-                    turned[:].bitcast(F32)[:, P * u : P * (u + 1)],
+                    roots[:].bitcast(F32)[:, P * u : P * (u + 1)],
                     identity[:],
+                )
+        unread = bank([P, BANK], "unread", 2 * PACK - 1)
+        for t in range(WARM_PASSES):
+            nc.tensor.matmul_mx(
+                out=unread[:],
+                lhsT=w4_dealt[:, 0, 2 * P * t : 2 * P * (t + 1)].bitcast(FP4X4),
+                lhsT_scale=w4_planes[:, 0, P * t : P * (t + 1)],
+                rhs=v_codes[0, 0].bitcast(FP8X4),
+                rhs_scale=v_planes[0][:, 0:BANK],
+                start=True,
+                stop=True,
+            )
+        z_dealt = []
+        for half in range(2):
+            z_dealt.append(tile([P, HALF, PACK], BF16, "z_dealt%d" % half, "roots%d" % (2 * half)))
+            for beats in root_steps[half]:
+                nc.scalar.activation(
+                    z_dealt[half][:, within(half, beats), :].rearrange("p (c i) t -> p c t i", i=LINE),
+                    totals[half][:, :, within(half, beats)].rearrange("p t (c i) -> p c t i", i=LINE),
+                    ACT.Sqrt,
                 )
 
         def copy_back(half):
-            z = tile([P, HALF, PACK], BF16, "z1_%d" % half)
+            z = tile([P, HALF, PACK], BF16, "z_turned%d" % half)
             nc.vector.tensor_copy(
                 z[:].rearrange("p m t -> p (m t)").bitcast(F32).rearrange("p (m u) -> p m u", u=2),
                 backs[half][:].rearrange("p u m -> p m u"),
             )
             return z
 
-        for c in range(M // P):
-            root_and_turn_back(c)
-        unread = bank([P, BANK], "unread", 3)
-        for j in range(4):
-            nc.tensor.matmul_mx(
-                out=unread[:],
-                lhsT=w4_codes[0][:, 0, 2 * P * j : 2 * P * (j + 1)].bitcast(FP4X4),
-                lhsT_scale=w4_planes[:, 0, P * j : P * (j + 1)],
-                rhs=v_codes[0, 0].bitcast(FP8X4),
-                rhs_scale=planes[0][:, 0:BANK],
-                start=True,
-                stop=True,
+        def quantise(name, tag, rounded):
+            width = rounded.shape[1]
+            codes = tile([P, width], U32, name + "_codes", tag)
+            plane = tile([P, width], U8, name + "_plane")
+            nc.vector.quantize_mx(
+                out=codes[:].bitcast(FP8X4), scales=plane[:], in_=rounded.rearrange("p m t -> p (m t)")
             )
-        z0 = []
-        for half in range(2):
-            z0.append(tile([P, HALF, PACK], BF16, "z0_%d" % half, "turned%d" % (2 * half)))
-            nc.scalar.activation(*by_lines(z0[half][:], totals[half][:]), ACT.Sqrt)
+            return codes, plane
 
+        w2_q = {}
+
+        def quantise_w2(b, g, tag, rounded):
+            codes, plane = quantise("w2_%d_%d" % (b, g), tag, rounded)
+            for n in range(2):
+                w2_q[b, 2 * g + n] = (codes[:, P * n : P * (n + 1)], plane[:, P * n : P * (n + 1)])
+
+        y_places = ((4, 5, 6, 7), (2, 3, 0, 1))
         y_banks = {}
 
-        def second_product(half, b, row_tiles, z_q):
-            for n in row_tiles:
-                if b == 1:
-                    y_banks[half, n] = bank([P, HALF], "y%d_%d" % (half, n), ((0, 1, 2, 3), (6, 7, 4, 5))[half][n])
-                nc.tensor.matmul_mx(
-                    out=y_banks[half, n][:],
-                    lhsT=w2_q[b, n][0].bitcast(FP8X4),
-                    lhsT_scale=w2_q[b, n][1],
-                    rhs=z_q[0][:].bitcast(FP8X4),
-                    rhs_scale=z_q[1][:],
-                    start=(b == 1),
-                    stop=(b == 0),
-                )
-                if b == 0:
-                    result = tile([P, HALF], F32, "result%d_%d" % (half, n))
-                    nc.scalar.activation(result[:], y_banks[half, n][:], ACT.Silu)
-                    nc.sync.dma_start(out[P * n : P * (n + 1), halves[half]], result[:])
+        def second_product(half, b, n, z_q):
+            if b == TURNED:
+                y_banks[half, n] = bank([P, HALF], "y%d_%d" % (half, n), y_places[half][n])
+            nc.tensor.matmul_mx(
+                out=y_banks[half, n][:],
+                lhsT=w2_q[b, n][0].bitcast(FP8X4),
+                lhsT_scale=w2_q[b, n][1],
+                rhs=z_q[0][:].bitcast(FP8X4),
+                rhs_scale=z_q[1][:],
+                start=(b == TURNED),
+                stop=(b == DEALT),
+            )
+            if b == DEALT:
+                result = tile([P, HALF], F32, "result%d_%d" % (half, n))
+                nc.scalar.activation(result[:], y_banks[half, n][:], ACT.Silu)
+                nc.sync.dma_start(out[P * n : P * (n + 1), halves[half]], result[:])
 
-        z1 = [copy_back(0)]
-        quantise_w2(1, 0, rounded1[0][:], "turned1")
-        z1_q = [quantise("z1_0", None, z1[0][:])]
-        second_product(0, 1, range(2), z1_q[0])
-        z1.append(copy_back(1))
-        quantise_w2(0, 0, rounded0[:, columns[0], :], "turned3")
-        z0_q = [quantise("z0_0", None, z0[0][:])]
-        second_product(0, 0, range(2), z0_q[0])
-        quantise_w2(1, 2, rounded1[1][:], "total0")
-        quantise_w2(0, 2, rounded0[:, columns[1], :], "turned0")
-        for n in (2, 3):
-            second_product(0, 1, [n], z1_q[0])
-            second_product(0, 0, [n], z0_q[0])
-        z1_q.append(quantise("z1_1", "total1", z1[1][:]))
-        z0_q.append(quantise("z0_1", None, z0[1][:]))
-        for n in range(4):
-            second_product(1, 1, [n], z1_q[1])
-            second_product(1, 0, [n], z0_q[1])
+        z_turned = [copy_back(0)]
+        quantise_w2(TURNED, 0, "roots1", rounded_turned[0][:])
+        first_turned = quantise("z_turned0", None, z_turned[0][:])
+        for n in range(2):
+            second_product(0, TURNED, n, first_turned)
+        z_turned.append(copy_back(1))
+        quantise_w2(DEALT, 0, "roots3", rounded_dealt[:, columns[0], :])
+        first_dealt = quantise("z_dealt0", None, z_dealt[0][:])
+        for n in range(2):
+            second_product(0, DEALT, n, first_dealt)
+        quantise_w2(TURNED, 1, "total0", rounded_turned[1][:])
+        quantise_w2(DEALT, 1, "roots0", rounded_dealt[:, columns[1], :])
+        for n in range(2, N // P):
+            second_product(0, TURNED, n, first_turned)
+            second_product(0, DEALT, n, first_dealt)
+        second_turned = quantise("z_turned1", "total1", z_turned[1][:])
+        second_dealt = quantise("z_dealt1", None, z_dealt[1][:])
+        for n in range(N // P):
+            second_product(1, TURNED, n, second_turned)
+            second_product(1, DEALT, n, second_dealt)

@@ -32,7 +32,6 @@ LINE = 4
 LISTS = 3
 DEALT, TURNED = 0, 1
 AHEAD = T // 4
-LOGGED = (6, 7)
 HANDED_OVER = (7, 0)
 WARM_PASSES = 4
 
@@ -140,8 +139,6 @@ def tile_list_choir_blend_features_kernel(
 
         eps_sb = tile([P, 2, PACK], F32, "eps_sb")
         nc.scalar.copy(eps_sb[:], eps_psum[:, :, 0 : 2 * QUADRANT : QUADRANT].rearrange("p t b -> p b t"))
-        eps_third = tile([P, len(LOGGED)], F32, "eps_third")
-        nc.scalar.mul(eps_third[:], eps_psum[:, LOGGED[0] - PACK : PACK, QUADRANT], 1.0 / LISTS)
 
         v_codes = {}
         for a in range(2):
@@ -158,15 +155,15 @@ def tile_list_choir_blend_features_kernel(
         )
         w4_codes = {DEALT: w4_dealt, TURNED: w4_turned}
 
-        logs = [tile([P, 2 * S], F32, "logs%d" % i) for i in range(len(LOGGED))]
+        eps_spread = tile([P, PACK, M], F32, "eps_spread")
         for pair in range(2):
             nc.scalar.copy(
-                logs[pair][:, S : 2 * S].rearrange("p (t m) -> p t m", m=M),
+                eps_spread[:, 2 * pair : 2 * pair + 2, :],
                 eps_sb[:, DEALT, 2 * pair : 2 * pair + 2].unsqueeze(2).to_broadcast([P, 2, M]),
             )
-        so_far = {j: logs[j // 2][:, S + M * (j % 2) : S + M * (j % 2 + 1)] for j in range(PACK)}
+        so_far = {j: eps_spread[:, j, :] for j in range(PACK)}
         warm = tile([P, 1], F32, "warm")
-        nc.scalar.activation(warm[:], eps_sb[:, DEALT, 0:1], ACT.Ln)
+        nc.scalar.activation(warm[:], eps_sb[:, DEALT, 0:1], ACT.Sqrt)
 
         def round_on_gpsimd(name, tag, rows):
             rounded = tile([P, rows.shape[2], PACK], BF16, name, tag)
@@ -211,67 +208,67 @@ def tile_list_choir_blend_features_kernel(
                 first_product(j, half, 0)
         for j, half in ((4, 0), (5, 0), HANDED_OVER, (4, 1), (5, 1), (6, 0), (6, 1), (7, 1)):
             first_product(j, half, 1)
-        for i, j in enumerate(LOGGED):
-            nc.scalar.activation(logs[i][:, 0:S], squares[j][:], ACT.Ln, bias=eps_third[:, i : i + 1])
 
-        terms = [tile([P, LISTS, M], F32, "terms%d" % t) for t in range(2)]
-        for i in range(LISTS):
-            for t in range(2):
-                nc.vector.tensor_copy(terms[t][:, i, :], squares[PACK + t][:].indirect(pos_sb[i][:]))
+        halves = [slice(0, HALF), slice(HALF, M)]
+        whole = slice(0, M)
+
+        def entries_of(i, beats):
+            return pos_sb[i][:, beats.start // PER_COLUMN : beats.stop // PER_COLUMN]
+
+        def pick(engine, j, i, beats):
+            term = tile([P, beats.stop - beats.start], F32, "term%d_%d_%d" % (j, i, beats.start))
+            window = squares[j][:].indirect(entries_of(i, beats))
+            if engine == "vector":
+                nc.vector.tensor_copy(term[:], window)
+            else:
+                nc.scalar.activation(term[:], window, ACT.Copy)
+            return (j, beats, term)
+
+        by_vector = [(4, 0, whole), (5, 0, whole), (4, 1, whole), (4, 2, whole), (5, 1, halves[0])]
+        by_scalar = [(6, 0, whole), (6, 1, whole), (6, 2, whole), (5, 2, whole)]
+        by_scalar_late = [(7, 0, whole), (7, 1, whole), (5, 1, halves[1]), (7, 2, halves[0]), (7, 2, halves[1])]
+        terms = [pick("vector", *item) for item in by_vector]
         rounded_turned.append(round_on_gpsimd("rounded_turned1", "h_copy", w2_turned[1][:]))
         rounded_dealt = round_on_gpsimd("rounded_dealt", None, w2_dealt[:])
         whole_tiles((0, 1))
-        picked = [tile([P, LISTS, M], F32, "picked%d" % i, ("eps_third", None)[i]) for i in range(len(LOGGED))]
-        by_scalar = [(i, k) for i in range(len(LOGGED)) for k in range(LISTS)]
-
-        def pick_on_scalar(i, k):
-            nc.scalar.activation(picked[i][:, k, :], logs[i][:].indirect(pos_sb[k][:]), ACT.Exp)
-
-        for i, k in by_scalar[:LISTS]:
-            pick_on_scalar(i, k)
+        terms.extend(pick("scalar", *item) for item in by_scalar)
         whole_tiles((2, 3))
-        for i, k in by_scalar[LISTS:]:
-            pick_on_scalar(i, k)
+        terms.extend(pick("scalar", *item) for item in by_scalar_late)
 
         sums = [bank([P, PASS], "sums%d" % c, PACK + c) for c in range(M // P)]
 
-        def add_turned(t, term, first=False, last=False):
-            for c in range(M // P):
+        def add_turned(t, beats, term, first=False, last=False):
+            for c in range(beats.start // P, beats.stop // P):
                 nc.tensor.matmul(
                     sums[c][:, P * t : P * (t + 1)],
-                    lhsT=term[:, P * c : P * (c + 1)],
+                    lhsT=term[:, P * c - beats.start : P * (c + 1) - beats.start],
                     rhs=identity[:],
                     is_transpose=True,
                     start=first,
                     stop=last,
                 )
 
-        for t in range(2):
-            add_turned(t, eps_sb[:, TURNED, t : t + 1].to_broadcast([P, M]), first=(t == 0))
-        for i in range(LISTS):
-            for t in range(2):
-                add_turned(t, terms[t][:, i, :])
-        for i, k in by_scalar:
-            add_turned(LOGGED[i] - PACK, picked[i][:, k, :], last=((i, k) == by_scalar[-1]))
+        for t in range(PACK):
+            add_turned(t, whole, eps_sb[:, TURNED, t : t + 1].to_broadcast([P, M]), first=(t == 0))
+        for index, (j, beats, term) in enumerate(terms):
+            add_turned(j - PACK, beats, term, last=(index >= len(terms) - 2))
 
-        halves = [slice(0, HALF), slice(HALF, M)]
         totals = [tile([P, PACK, HALF], F32, "total%d" % half) for half in range(2)]
 
         def pick_and_add(dst, j, i, beats, before):
-            entries = slice(beats.start // PER_COLUMN, beats.stop // PER_COLUMN)
-            nc.vector.tensor_tensor(dst, squares[j][:].indirect(pos_sb[i][:, entries]), before[:, beats], ADD)
+            nc.vector.tensor_tensor(dst, squares[j][:].indirect(entries_of(i, beats)), before[:, beats], ADD)
 
-        part_tags = [("squares%d" % (PACK + t), "second_sum%d" % t) for t in range(2)]
+        part_tags = ("squares4", "second_sums")
         root_steps = [[halves[0]], [slice(HALF, M - HALF // 2), slice(M - HALF // 2, M)]]
 
         def within(half, beats):
             return slice(beats.start - HALF * half, beats.stop - HALF * half)
 
         def whole_list(pair, i):
+            parts = tile([P, 2, M], F32, "parts%d_%d" % (pair[0], i), part_tags[i])
             for j in pair:
-                part = tile([P, M], F32, "part%d_%d" % (j, i), part_tags[j % 2][i])
-                pick_and_add(part[:], j, i, slice(0, M), so_far[j])
-                so_far[j] = part[:]
+                pick_and_add(parts[:, j % 2, :], j, i, whole, so_far[j])
+                so_far[j] = parts[:, j % 2, :]
 
         def last_list(pair, half, beats, before):
             for j in pair:
@@ -282,7 +279,8 @@ def tile_list_choir_blend_features_kernel(
         for half in range(2):
             last_list((0, 1), half, halves[half], so_far)
         whole_list((2, 3), 0)
-        second = {j: tile([P, M], F32, "part%d_1" % j, part_tags[j % 2][1])[:] for j in (2, 3)}
+        seconds = tile([P, 2, M], F32, "parts2_1", part_tags[1])
+        second = {j: seconds[:, j % 2, :] for j in (2, 3)}
         for half in range(2):
             for j in (2, 3):
                 pick_and_add(second[j][:, halves[half]], j, 1, halves[half], so_far[j])

@@ -31,8 +31,7 @@ BLOCKS = PASS // 32
 LINE = 4
 LISTS = 3
 DEALT, TURNED = 0, 1
-AHEAD = T // 4
-HANDED_OVER = (7, 0)
+AHEAD = T // 2
 WARM_PASSES = 4
 
 
@@ -140,13 +139,12 @@ def tile_list_choir_blend_features_kernel(
         eps_sb = tile([P, 2, PACK], F32, "eps_sb")
         nc.scalar.copy(eps_sb[:], eps_psum[:, :, 0 : 2 * QUADRANT : QUADRANT].rearrange("p t b -> p b t"))
 
-        v_codes = {}
+        cuts = [slice(0, S // 4), slice(S // 4, S - S // 4), slice(S - S // 4, S)]
+        v_codes = [tile([P, S], U32, "v_codes%d" % a) for a in range(2)]
         for a in range(2):
-            for half in range(2):
-                codes = tile([P, BANK], U32, "v_codes%d_%d" % (a, half))
-                entries = slice(BANK * half // PER_COLUMN, BANK * (half + 1) // PER_COLUMN)
-                nc.vector.tensor_copy(codes[:], words[a][:].bitcast(U32).indirect(offs_sb[:, entries]))
-                v_codes[a, half] = codes[:]
+            for frames in cuts:
+                entries = slice(frames.start // PER_COLUMN, frames.stop // PER_COLUMN)
+                nc.vector.tensor_copy(v_codes[a][:, frames], words[a][:].bitcast(U32).indirect(offs_sb[:, entries]))
 
         w4_dealt = tile([P, 2, 2 * PASS], U8, "w4_dealt")
         nc.vector.tensor_copy(
@@ -170,44 +168,43 @@ def tile_list_choir_blend_features_kernel(
             nc.gpsimd.tensor_scalar(rounded[:], rows.rearrange("p t n -> p n t"), 1.0, 0.0, MULT, ADD)
             return rounded
 
-        squares = [tile([P, S], F32, "squares%d" % j) for j in range(2 * PACK - 1)]
+        squares = [tile([P, S], F32, "squares%d" % j) for j in range(2 * PACK)]
         rounded_turned = [round_on_gpsimd("rounded_turned0", "w4_raw%d" % DEALT, w2_turned[0][:])]
-        squares.append(tile([P, S], F32, "squares7", "w2_turned0"))
         h_banks = {}
 
-        def first_product(j, half, a):
+        def first_product(j, frames, a, place=None):
             b, t = divmod(j, PACK)
             if a == 0:
-                h_banks[j, half] = bank([P, BANK], "h%d_%d" % (j, half), 2 * (t if b == TURNED else t % 2) + half)
+                width = frames.stop - frames.start
+                h_banks[j, frames.start] = bank([P, width], "h%d_%d" % (j, frames.start), place)
             nc.tensor.matmul_mx(
-                out=h_banks[j, half][:],
+                out=h_banks[j, frames.start][:],
                 lhsT=w4_codes[b][:, a, 2 * P * t : 2 * P * (t + 1)].bitcast(FP4X4),
                 lhsT_scale=w4_planes[:, a, P * j : P * (j + 1)],
-                rhs=v_codes[a, half].bitcast(FP8X4),
-                rhs_scale=v_planes[a][:, BANK * half : BANK * (half + 1)],
+                rhs=v_codes[a][:, frames].bitcast(FP8X4),
+                rhs_scale=v_planes[a][:, frames],
                 start=(a == 0),
                 stop=(a == 1),
             )
             if a == 1:
-                frames = slice(BANK * half, BANK * (half + 1))
-                if (j, half) == HANDED_OVER:
-                    h_copy = tile([P, BANK], F32, "h_copy")
-                    nc.vector.tensor_copy(h_copy[:], h_banks[j, half][:])
-                    nc.gpsimd.tensor_tensor(squares[j][:, frames], h_copy[:], h_copy[:], MULT)
-                else:
-                    nc.scalar.activation(squares[j][:, frames], h_banks[j, half][:], ACT.Square)
+                nc.scalar.activation(squares[j][:, frames], h_banks[j, frames.start][:], ACT.Square)
+
+        def both_passes(j, frames, place):
+            first_product(j, frames, 0, place)
+            first_product(j, frames, 1)
 
         def whole_tiles(pair):
-            for j in pair:
-                for half in range(2):
-                    for a in range(2):
-                        first_product(j, half, a)
+            for half in range(2):
+                for j in pair:
+                    both_passes(j, slice(BANK * half, BANK * (half + 1)), j % 2 + 2 * half)
 
-        for half in range(2):
-            for j in range(PACK, 2 * PACK):
-                first_product(j, half, 0)
-        for j, half in ((4, 0), (5, 0), HANDED_OVER, (4, 1), (5, 1), (6, 0), (6, 1), (7, 1)):
-            first_product(j, half, 1)
+        early = [(j, cuts[cut]) for j, cut in ((4, 0), (5, 0), (6, 0), (7, 0), (4, 1), (4, 2), (5, 1), (5, 2))]
+        for place, (j, frames) in enumerate(early):
+            first_product(j, frames, 0, (place + PACK) % (2 * PACK))
+        for j, frames in early:
+            first_product(j, frames, 1)
+        for place, (j, frames) in enumerate((j, cut) for j in (6, 7) for cut in cuts[1:]):
+            both_passes(j, frames, PACK + place)
 
         halves = [slice(0, HALF), slice(HALF, M)]
         whole = slice(0, M)
@@ -224,11 +221,11 @@ def tile_list_choir_blend_features_kernel(
                 nc.scalar.activation(term[:], window, ACT.Copy)
             return (j, beats, term)
 
-        by_vector = [(4, 0, whole), (5, 0, whole), (4, 1, whole), (4, 2, whole), (5, 1, halves[0])]
+        by_vector = [(4, 0, whole), (4, 1, whole), (4, 2, whole), (5, 0, whole)]
         by_scalar = [(6, 0, whole), (6, 1, whole), (6, 2, whole), (5, 2, whole)]
-        by_scalar_late = [(7, 0, whole), (7, 1, whole), (5, 1, halves[1]), (7, 2, halves[0]), (7, 2, halves[1])]
+        by_scalar_late = [(7, 0, whole), (7, 1, whole), (7, 2, whole), (5, 1, halves[0]), (5, 1, halves[1])]
         terms = [pick("vector", *item) for item in by_vector]
-        rounded_turned.append(round_on_gpsimd("rounded_turned1", "h_copy", w2_turned[1][:]))
+        rounded_turned.append(round_on_gpsimd("rounded_turned1", "w2_turned0", w2_turned[1][:]))
         rounded_dealt = round_on_gpsimd("rounded_dealt", None, w2_dealt[:])
         whole_tiles((0, 1))
         terms.extend(pick("scalar", *item) for item in by_scalar)
@@ -237,7 +234,7 @@ def tile_list_choir_blend_features_kernel(
 
         sums = [bank([P, PASS], "sums%d" % c, PACK + c) for c in range(M // P)]
 
-        def add_turned(t, beats, term, first=False, last=False):
+        def add_turned(t, beats, term, first=False, closes=()):
             for c in range(beats.start // P, beats.stop // P):
                 nc.tensor.matmul(
                     sums[c][:, P * t : P * (t + 1)],
@@ -245,51 +242,48 @@ def tile_list_choir_blend_features_kernel(
                     rhs=identity[:],
                     is_transpose=True,
                     start=first,
-                    stop=last,
+                    stop=(c in closes),
                 )
 
         for t in range(PACK):
             add_turned(t, whole, eps_sb[:, TURNED, t : t + 1].to_broadcast([P, M]), first=(t == 0))
-        for index, (j, beats, term) in enumerate(terms):
-            add_turned(j - PACK, beats, term, last=(index >= len(terms) - 2))
+        for j, beats, term in terms[:-2]:
+            add_turned(j - PACK, beats, term)
+        for j, beats, term in terms[-2:]:
+            add_turned(j - PACK, beats, term, closes=range(M // P))
 
-        totals = [tile([P, PACK, HALF], F32, "total%d" % half) for half in range(2)]
+        totals = tile([P, PACK, M], F32, "totals")
 
         def pick_and_add(dst, j, i, beats, before):
             nc.vector.tensor_tensor(dst, squares[j][:].indirect(entries_of(i, beats)), before[:, beats], ADD)
 
-        part_tags = ("squares4", "second_sums")
-        root_steps = [[halves[0]], [slice(HALF, M - HALF // 2), slice(M - HALF // 2, M)]]
+        part_tags = (("squares4", "first_sum"), ("second_sums", "second_sum"))
+        root_steps = [halves[0], slice(HALF, M - HALF // 2), slice(M - HALF // 2, M)]
 
-        def within(half, beats):
-            return slice(beats.start - HALF * half, beats.stop - HALF * half)
-
-        def whole_list(pair, i):
-            parts = tile([P, 2, M], F32, "parts%d_%d" % (pair[0], i), part_tags[i])
-            for j in pair:
-                pick_and_add(parts[:, j % 2, :], j, i, whole, so_far[j])
-                so_far[j] = parts[:, j % 2, :]
-
-        def last_list(pair, half, beats, before):
-            for j in pair:
-                pick_and_add(totals[half][:, j, within(half, beats)], j, LISTS - 1, beats, before[j])
-
-        for i in range(LISTS - 1):
-            whole_list((0, 1), i)
-        for half in range(2):
-            last_list((0, 1), half, halves[half], so_far)
-        whole_list((2, 3), 0)
-        seconds = tile([P, 2, M], F32, "parts2_1", part_tags[1])
-        second = {j: seconds[:, j % 2, :] for j in (2, 3)}
-        for half in range(2):
-            for j in (2, 3):
-                pick_and_add(second[j][:, halves[half]], j, 1, halves[half], so_far[j])
-            for beats in root_steps[half]:
-                last_list((2, 3), half, beats, second)
+        for pair, steps in (((0, 1), [whole]), ((2, 3), root_steps)):
+            for i in range(LISTS - 1):
+                for j in pair:
+                    part = tile([P, M], F32, "part%d_%d" % (j, i), part_tags[i][j % 2])
+                    pick_and_add(part[:], j, i, whole, so_far[j])
+                    so_far[j] = part[:]
+            for beats in steps:
+                for j in pair:
+                    pick_and_add(totals[:, j, beats], j, LISTS - 1, beats, so_far[j])
 
         backs = [bank([P, 2, HALF], "back%d" % half, half) for half in range(2)]
+
+        def copy_back(half, tag, copy):
+            z = tile([P, HALF, PACK], BF16, "z_turned%d" % half, tag)
+            copy(
+                z[:].rearrange("p m t -> p (m t)").bitcast(F32).rearrange("p (m u) -> p m u", u=2),
+                backs[half][:].rearrange("p u m -> p m u"),
+            )
+            return z
+
         for c in range(M // P):
             half, part = divmod(c, 2)
+            if c == M // P - 1:
+                z_turned = copy_back(0, None, nc.scalar.copy)
             roots = tile([P, PASS], BF16, "roots%d" % c)
             nc.scalar.activation(
                 roots[:].rearrange("m (u p e) -> m u p e", u=2, e=2),
@@ -308,42 +302,32 @@ def tile_list_choir_blend_features_kernel(
                 out=unread[:],
                 lhsT=w4_dealt[:, 0, 2 * P * t : 2 * P * (t + 1)].bitcast(FP4X4),
                 lhsT_scale=w4_planes[:, 0, P * t : P * (t + 1)],
-                rhs=v_codes[0, 0].bitcast(FP8X4),
+                rhs=v_codes[0][:, 0:BANK].bitcast(FP8X4),
                 rhs_scale=v_planes[0][:, 0:BANK],
                 start=True,
                 stop=True,
             )
-        z_dealt = []
-        for half in range(2):
-            z_dealt.append(tile([P, HALF, PACK], BF16, "z_dealt%d" % half, "roots%d" % (2 * half)))
-            for beats in root_steps[half]:
-                nc.scalar.activation(
-                    z_dealt[half][:, within(half, beats), :].rearrange("p (c i) t -> p c t i", i=LINE),
-                    totals[half][:, :, within(half, beats)].rearrange("p t (c i) -> p c t i", i=LINE),
-                    ACT.Sqrt,
-                )
-
-        def copy_back(half):
-            z = tile([P, HALF, PACK], BF16, "z_turned%d" % half)
-            nc.vector.tensor_copy(
-                z[:].rearrange("p m t -> p (m t)").bitcast(F32).rearrange("p (m u) -> p m u", u=2),
-                backs[half][:].rearrange("p u m -> p m u"),
+        z_dealt = [tile([P, HALF, PACK], BF16, "z_dealt%d" % half, "roots%d" % (2 * half)) for half in range(2)]
+        for beats in root_steps:
+            half, first = divmod(beats.start, HALF)
+            nc.scalar.activation(
+                z_dealt[half][:, first : beats.stop - HALF * half, :].rearrange("p (c i) t -> p c t i", i=LINE),
+                totals[:, :, beats].rearrange("p t (c i) -> p c t i", i=LINE),
+                ACT.Sqrt,
             )
-            return z
 
-        def quantise(name, tag, rounded):
-            width = rounded.shape[1]
-            codes = tile([P, width], U32, name + "_codes", tag)
-            plane = tile([P, width], U8, name + "_plane")
-            nc.vector.quantize_mx(
-                out=codes[:].bitcast(FP8X4), scales=plane[:], in_=rounded.rearrange("p m t -> p (m t)")
-            )
-            return codes, plane
+        def quantise(name, codes, rounded):
+            plane = tile([P, HALF], U8, name + "_plane")
+            nc.vector.quantize_mx(out=codes.bitcast(FP8X4), scales=plane[:], in_=rounded.rearrange("p m t -> p (m t)"))
+            return codes, plane[:]
+
+        def own_codes(name, tag=None, width=HALF):
+            return tile([P, width], U32, name + "_codes", tag)[:]
 
         w2_q = {}
 
-        def quantise_w2(b, g, tag, rounded):
-            codes, plane = quantise("w2_%d_%d" % (b, g), tag, rounded)
+        def quantise_w2(b, g, codes, rounded):
+            codes, plane = quantise("w2_%d_%d" % (b, g), codes, rounded)
             for n in range(2):
                 w2_q[b, 2 * g + n] = (codes[:, P * n : P * (n + 1)], plane[:, P * n : P * (n + 1)])
 
@@ -351,39 +335,40 @@ def tile_list_choir_blend_features_kernel(
         y_banks = {}
 
         def second_product(half, b, n, z_q):
-            if b == TURNED:
+            opens = b == (TURNED, DEALT)[half]
+            if opens:
                 y_banks[half, n] = bank([P, HALF], "y%d_%d" % (half, n), y_places[half][n])
             nc.tensor.matmul_mx(
                 out=y_banks[half, n][:],
                 lhsT=w2_q[b, n][0].bitcast(FP8X4),
                 lhsT_scale=w2_q[b, n][1],
-                rhs=z_q[0][:].bitcast(FP8X4),
-                rhs_scale=z_q[1][:],
-                start=(b == TURNED),
-                stop=(b == DEALT),
+                rhs=z_q[0].bitcast(FP8X4),
+                rhs_scale=z_q[1],
+                start=opens,
+                stop=not opens,
             )
-            if b == DEALT:
+            if not opens:
                 result = tile([P, HALF], F32, "result%d_%d" % (half, n))
                 nc.scalar.activation(result[:], y_banks[half, n][:], ACT.Silu)
                 nc.sync.dma_start(out[P * n : P * (n + 1), halves[half]], result[:])
 
-        z_turned = [copy_back(0)]
-        quantise_w2(TURNED, 0, "roots1", rounded_turned[0][:])
-        first_turned = quantise("z_turned0", None, z_turned[0][:])
+        quantise_w2(TURNED, 0, own_codes("w2_first", "roots1"), rounded_turned[0][:])
+        first_turned = quantise("z_turned0", own_codes("z_turned0"), z_turned[:])
         for n in range(2):
             second_product(0, TURNED, n, first_turned)
-        z_turned.append(copy_back(1))
-        quantise_w2(DEALT, 0, "roots3", rounded_dealt[:, columns[0], :])
-        first_dealt = quantise("z_dealt0", None, z_dealt[0][:])
+        quantise_w2(DEALT, 0, own_codes("w2_second", "roots3"), rounded_dealt[:, columns[0], :])
+        first_dealt = quantise("z_dealt0", own_codes("z_dealt0"), z_dealt[0][:])
         for n in range(2):
             second_product(0, DEALT, n, first_dealt)
-        quantise_w2(TURNED, 1, "total0", rounded_turned[1][:])
-        quantise_w2(DEALT, 1, "roots0", rounded_dealt[:, columns[1], :])
+        later = own_codes("w2_later", "roots0", 2 * HALF)
+        quantise_w2(TURNED, 1, later[:, 0:HALF], rounded_turned[1][:])
+        quantise_w2(DEALT, 1, later[:, HALF : 2 * HALF], rounded_dealt[:, columns[1], :])
         for n in range(2, N // P):
             second_product(0, TURNED, n, first_turned)
             second_product(0, DEALT, n, first_dealt)
-        second_turned = quantise("z_turned1", "total1", z_turned[1][:])
-        second_dealt = quantise("z_dealt1", None, z_dealt[1][:])
-        for n in range(N // P):
-            second_product(1, TURNED, n, second_turned)
-            second_product(1, DEALT, n, second_dealt)
+        z_turned = copy_back(1, "w2_turned0", nc.vector.tensor_copy)
+        second_q = {DEALT: quantise("z_dealt1", own_codes("z_dealt1"), z_dealt[1][:])}
+        second_q[TURNED] = quantise("z_turned1", own_codes("z_turned1"), z_turned[:])
+        for b in (DEALT, TURNED):
+            for n in range(N // P):
+                second_product(1, b, n, second_q[b])

@@ -125,11 +125,9 @@ def tile_list_choir_blend_features_kernel(
         w4_raw = load_w4_words(DEALT)
         nc.sync.dma_start(pos_sb[0][:], pos1)
         columns = [slice(0, N // 2), slice(N // 2, N)]
-        w2_turned = [tile([P, PACK, N // 2], F32, "w2_turned%d" % g) for g in range(2)]
-        turned_rows = w2[PASS:H, :].rearrange("(p i) n -> p i n", i=PACK)
-        nc.sync.dma_start(w2_turned[0][:], turned_rows[:, :, columns[0]])
+        w2_turned = tile([P, PACK, N], F32, "w2_turned")
+        nc.sync.dma_start(w2_turned[:], w2[PASS:H, :].rearrange("(p i) n -> p i n", i=PACK))
         nc.sync.dma_start(pos_sb[1][:], pos2)
-        nc.sync.dma_start(w2_turned[1][:], turned_rows[:, :, columns[1]])
         nc.sync.dma_start(pos_sb[2][:], pos3)
         w2_dealt = tile([P, PACK, N], F32, "w2_dealt")
         dealt_rows = w2[0:PASS, :].rearrange("(g t u) n -> t g u n", t=PACK, u=RUN)
@@ -169,42 +167,66 @@ def tile_list_choir_blend_features_kernel(
             return rounded
 
         squares = [tile([P, S], F32, "squares%d" % j) for j in range(2 * PACK)]
-        rounded_turned = [round_on_gpsimd("rounded_turned0", "w4_raw%d" % DEALT, w2_turned[0][:])]
+        rounded_turned = round_on_gpsimd("rounded_turned", "w4_raw%d" % DEALT, w2_turned[:])
         h_banks = {}
 
-        def first_product(j, frames, a, place=None):
-            b, t = divmod(j, PACK)
+        def first_product(pieces, a, place=None):
             if a == 0:
-                width = frames.stop - frames.start
-                h_banks[j, frames.start] = bank([P, width], "h%d_%d" % (j, frames.start), place)
+                widths = [frames.stop - frames.start for j, frames in pieces]
+                held = bank([P, sum(widths)], "h%d_%d" % (pieces[0][0], pieces[0][1].start), place)
+                for index, (j, frames) in enumerate(pieces):
+                    h_banks[j, frames.start] = held[:, sum(widths[:index]) : sum(widths[: index + 1])]
+            for index, (j, frames) in enumerate(pieces):
+                one_pass(j, frames, a, a == 0 and index == 0, a == 1 and index == len(pieces) - 1)
+            if a == 1:
+                for j, frames in pieces:
+                    square(j, frames)
+
+        def square(j, frames):
+            h = h_banks[j, frames.start]
+            if (j, frames) == on_vector:
+                factor = tile([P, frames.stop - frames.start], F32, "factor")
+                nc.vector.tensor_copy(factor[:], h)
+                nc.vector.tensor_tensor(squares[j][:, frames], h, factor[:], MULT)
+            else:
+                nc.scalar.activation(squares[j][:, frames], h, ACT.Square)
+
+        def one_pass(j, frames, a, start, stop):
+            b, t = divmod(j, PACK)
             nc.tensor.matmul_mx(
-                out=h_banks[j, frames.start][:],
+                out=h_banks[j, frames.start],
                 lhsT=w4_codes[b][:, a, 2 * P * t : 2 * P * (t + 1)].bitcast(FP4X4),
                 lhsT_scale=w4_planes[:, a, P * j : P * (j + 1)],
                 rhs=v_codes[a][:, frames].bitcast(FP8X4),
                 rhs_scale=v_planes[a][:, frames],
-                start=(a == 0),
-                stop=(a == 1),
+                start=start,
+                stop=stop,
             )
-            if a == 1:
-                nc.scalar.activation(squares[j][:, frames], h_banks[j, frames.start][:], ACT.Square)
 
-        def both_passes(j, frames, place):
-            first_product(j, frames, 0, place)
-            first_product(j, frames, 1)
+        def both_passes(pieces, place):
+            first_product(pieces, 0, place)
+            first_product(pieces, 1)
 
         def whole_tiles(pair):
             for half in range(2):
                 for j in pair:
-                    both_passes(j, slice(BANK * half, BANK * (half + 1)), j % 2 + 2 * half)
+                    both_passes([(j, slice(BANK * half, BANK * (half + 1)))], j % 2 + 2 * half)
 
-        early = [(j, cuts[cut]) for j, cut in ((4, 0), (5, 0), (6, 0), (7, 0), (4, 1), (4, 2), (5, 1), (5, 2))]
-        for place, (j, frames) in enumerate(early):
-            first_product(j, frames, 0, (place + PACK) % (2 * PACK))
-        for j, frames in early:
-            first_product(j, frames, 1)
-        for place, (j, frames) in enumerate((j, cut) for j in (6, 7) for cut in cuts[1:]):
-            both_passes(j, frames, PACK + place)
+        quarters = [slice(S // PACK * q, S // PACK * (q + 1)) for q in range(PACK)]
+        early = [[(j, cuts[0])] for j in range(PACK, 2 * PACK)]
+        early.extend([(4, frames)] for frames in quarters[1:])
+        early.append([(5, cuts[1])])
+        on_vector = (7, cuts[0])
+        rest = [[(5, cuts[2]), (6, cuts[2])], [(6, cuts[1])], [(7, cuts[1])], [(7, cuts[2])]]
+        for place, pieces in enumerate(early):
+            first_product(pieces, 0, (place + PACK) % (2 * PACK))
+        for pieces in early[0:6]:
+            first_product(pieces, 1)
+        first_product(rest[0], 0, PACK)
+        for pieces in early[6:8] + rest[0:1]:
+            first_product(pieces, 1)
+        for place in range(1, len(rest)):
+            both_passes(rest[place], PACK + place)
 
         halves = [slice(0, HALF), slice(HALF, M)]
         whole = slice(0, M)
@@ -221,12 +243,11 @@ def tile_list_choir_blend_features_kernel(
                 nc.scalar.activation(term[:], window, ACT.Copy)
             return (j, beats, term)
 
-        by_vector = [(4, 0, whole), (4, 1, whole), (4, 2, whole), (5, 0, whole)]
+        by_vector = [(4, 0, whole), (4, 1, whole), (4, 2, whole), (5, 0, whole), (5, 1, slice(0, P))]
         by_scalar = [(6, 0, whole), (6, 1, whole), (6, 2, whole), (5, 2, whole)]
-        by_scalar_late = [(7, 0, whole), (7, 1, whole), (7, 2, whole), (5, 1, halves[0]), (5, 1, halves[1])]
+        by_scalar_late = [(7, 0, whole), (7, 1, whole), (7, 2, whole), (5, 1, slice(P, M))]
         terms = [pick("vector", *item) for item in by_vector]
-        rounded_turned.append(round_on_gpsimd("rounded_turned1", "w2_turned0", w2_turned[1][:]))
-        rounded_dealt = round_on_gpsimd("rounded_dealt", None, w2_dealt[:])
+        rounded_dealt = round_on_gpsimd("rounded_dealt", "w2_turned", w2_dealt[:])
         whole_tiles((0, 1))
         terms.extend(pick("scalar", *item) for item in by_scalar)
         whole_tiles((2, 3))
@@ -249,8 +270,8 @@ def tile_list_choir_blend_features_kernel(
             add_turned(t, whole, eps_sb[:, TURNED, t : t + 1].to_broadcast([P, M]), first=(t == 0))
         for j, beats, term in terms[:-2]:
             add_turned(j - PACK, beats, term)
-        for j, beats, term in terms[-2:]:
-            add_turned(j - PACK, beats, term, closes=range(M // P))
+        for (j, beats, term), closes in zip(terms[-2:], ((0,), range(1, M // P))):
+            add_turned(j - PACK, beats, term, closes=closes)
 
         totals = tile([P, PACK, M], F32, "totals")
 
@@ -352,7 +373,7 @@ def tile_list_choir_blend_features_kernel(
                 nc.scalar.activation(result[:], y_banks[half, n][:], ACT.Silu)
                 nc.sync.dma_start(out[P * n : P * (n + 1), halves[half]], result[:])
 
-        quantise_w2(TURNED, 0, own_codes("w2_first", "roots1"), rounded_turned[0][:])
+        quantise_w2(TURNED, 0, own_codes("w2_first", "roots1"), rounded_turned[:, columns[0], :])
         first_turned = quantise("z_turned0", own_codes("z_turned0"), z_turned[:])
         for n in range(2):
             second_product(0, TURNED, n, first_turned)
@@ -361,12 +382,12 @@ def tile_list_choir_blend_features_kernel(
         for n in range(2):
             second_product(0, DEALT, n, first_dealt)
         later = own_codes("w2_later", "roots0", 2 * HALF)
-        quantise_w2(TURNED, 1, later[:, 0:HALF], rounded_turned[1][:])
+        quantise_w2(TURNED, 1, later[:, 0:HALF], rounded_turned[:, columns[1], :])
         quantise_w2(DEALT, 1, later[:, HALF : 2 * HALF], rounded_dealt[:, columns[1], :])
         for n in range(2, N // P):
             second_product(0, TURNED, n, first_turned)
             second_product(0, DEALT, n, first_dealt)
-        z_turned = copy_back(1, "w2_turned0", nc.vector.tensor_copy)
+        z_turned = copy_back(1, "w4_raw%d" % DEALT, nc.vector.tensor_copy)
         second_q = {DEALT: quantise("z_dealt1", own_codes("z_dealt1"), z_dealt[1][:])}
         second_q[TURNED] = quantise("z_turned1", own_codes("z_turned1"), z_turned[:])
         for b in (DEALT, TURNED):

from contextlib import ExitStack

import concourse.mybir as mybir
from concourse.masks import make_identity

K, T, S, M, H, N = 1024, 4096, 1024, 512, 1024, 512
FLOPS = 2 * K * H * S + 2 * H * N * M

F32 = mybir.dt.float32
BF16 = mybir.dt.bfloat16
I32 = mybir.dt.int32
U32 = mybir.dt.uint32
U16 = mybir.dt.uint16
U8 = mybir.dt.uint8
FP8X4 = mybir.dt.float8_e4m3fn_x4
FP4X4 = mybir.dt.float4_e2m1fn_x4
ACT = mybir.ActivationFunctionType
ADD = mybir.AluOpType.add
MULT = mybir.AluOpType.mult

P = 128
PACK = 4
PASS = P * PACK
RUN = 8
BANK = 512
HALF = M // 2
PER_COLUMN = 16
QUADRANT = 32
LIVE = 4
BLOCKS = PASS // 32
LINE = 4
LISTS = 3
DEALT, TURNED = 0, 1
AHEAD = T // 2
WARM_PASSES = 4


def tile_list_choir_blend_features_kernel(
    tc, tab_words, tab_scales, offs, w4_words, w4_scales, pos1, pos2, pos3, eps, w2, out
):
    nc = tc.nc
    with ExitStack() as ctx:
        lists = ctx.enter_context(tc.tile_pool(name="lists", bufs=1))
        keep = ctx.enter_context(tc.tile_pool(name="keep", bufs=1))
        psum = ctx.enter_context(tc.psum_pool(name="psum", bufs=1))

        def tile(shape, dtype, name, tag=None):
            return keep.tile(shape, dtype, name=name, tag=tag or name, align_bytes=64)

        def bank(shape, name, index):
            return psum.tile(shape, F32, name=name, tag="bank%d" % index)

        offs_sb = lists.tile([P, S // PER_COLUMN], U16, name="offs_sb")
        pos_sb = [lists.tile([P, M // PER_COLUMN], U16, name="pos%d_sb" % i) for i in range(LISTS)]

        tab = [tab_words[a].rearrange("p t i -> p (t i)").bitcast(I32) for a in range(2)]

        def load_w4_words(b):
            raw = tile([P, 2, 2 * PASS], U8, "w4_raw%d" % b)
            src = w4_words[:, :, 2 * PASS * b : 2 * PASS * (b + 1)].rearrange("a p c -> p a c")
            nc.sync.dma_start(raw[:].bitcast(I32), src.bitcast(I32))
            return raw

        nc.sync.dma_start(offs_sb[:], offs)
        scale_rows = tile([P, T], U8, "scale_rows")
        nc.sync.dma_start(
            scale_rows[0:QUADRANT, :].bitcast(I32), tab_scales.rearrange("a q t -> (a q) t").bitcast(I32)
        )
        eps_rows = tile([2 * QUADRANT, PASS], F32, "eps_rows")
        nc.sync.dma_start(eps_rows[0 : 2 * QUADRANT : QUADRANT, :], eps.rearrange("(b r) -> b r", b=2))
        w4_rows = tile([P, 2, H], U8, "w4_rows")
        for row in range(LIVE):
            nc.sync.dma_start(
                w4_rows[row:P:QUADRANT, :, :].bitcast(I32),
                w4_scales[:, row:BLOCKS:LIVE, :].rearrange("a q c -> q a c").bitcast(I32),
            )
        words = [tile([P, T], I32, "words%d" % a) for a in range(2)]
        nc.sync.dma_start(words[0][:], tab[0])
        w4_turned = load_w4_words(TURNED)
        nc.vector.memset(scale_rows[QUADRANT : 2 * QUADRANT, :].bitcast(I32), 0)
        nc.vector.memset(scale_rows[2 * QUADRANT : P, :].bitcast(I32), 0)
        v_planes = [tile([P, S], U8, "v_plane%d" % a) for a in range(2)]
        for a in range(2):
            nc.vector.memset(v_planes[a][:].bitcast(I32), 0)

        eps_ordered = tile([P, PACK, P], F32, "eps_ordered")
        nc.gpsimd.memset(eps_ordered[:], 0.0)
        identity = tile([P, P], F32, "identity")
        make_identity(nc, identity[:])
        nc.scalar.copy(
            eps_ordered[0:1, :, :].rearrange("b t (g u) -> b t g u", u=RUN),
            eps_rows[0:1, :].rearrange("b (g t u) -> b t g u", t=PACK, u=RUN),
        )
        nc.scalar.copy(
            eps_ordered[QUADRANT : QUADRANT + 1, :, :].rearrange("b t p -> b (t p)"),
            eps_rows[QUADRANT : QUADRANT + 1, :],
        )
        eps_psum = bank([P, PACK, P], "eps_psum", 7)
        for t in range(PACK):
            nc.tensor.transpose(eps_psum[:, t, :], eps_ordered[:, t, :], identity[:])

        picked_scales = tile([P, S], U8, "picked_scales")
        nc.vector.tensor_copy(picked_scales[:], scale_rows[:].indirect(offs_sb[:]))
        w4_planes = tile([P, 2, H], U8, "w4_planes", "scale_rows")
        nc.vector.memset(w4_planes[:].bitcast(I32), 0)
        for quad in range(P // QUADRANT):
            live = slice(QUADRANT * quad, QUADRANT * quad + LIVE)
            nc.vector.tensor_copy(
                w4_planes[live, :, 0:PASS].bitcast(I32).rearrange("p a (t g v) -> p a t g v", t=PACK, v=2),
                w4_rows[live, :, 0:PASS].bitcast(I32).rearrange("p a (g t v) -> p a t g v", t=PACK, v=2),
            )
            nc.vector.tensor_copy(w4_planes[live, :, PASS:H].bitcast(I32), w4_rows[live, :, PASS:H].bitcast(I32))

        def move_scale_rows(a):
            for row in range(LIVE):
                nc.sync.dma_start(
                    v_planes[a][row:P:QUADRANT, :].bitcast(I32),
                    picked_scales[BLOCKS * a + row : BLOCKS * (a + 1) : LIVE, :].bitcast(I32),
                )

        nc.sync.dma_start(words[1][:, 0:AHEAD], tab[1][:, 0:AHEAD])
        move_scale_rows(0)
        nc.sync.dma_start(words[1][:, AHEAD:T], tab[1][:, AHEAD:T])
        move_scale_rows(1)
        w4_raw = load_w4_words(DEALT)
        nc.sync.dma_start(pos_sb[0][:], pos1)
        columns = [slice(0, N // 2), slice(N // 2, N)]
        w2_turned = tile([P, PACK, N], F32, "w2_turned")
        nc.sync.dma_start(w2_turned[:], w2[PASS:H, :].rearrange("(p i) n -> p i n", i=PACK))
        nc.sync.dma_start(pos_sb[1][:], pos2)
        nc.sync.dma_start(pos_sb[2][:], pos3)
        w2_dealt = tile([P, PACK, N], F32, "w2_dealt")
        dealt_rows = w2[0:PASS, :].rearrange("(g t u) n -> t g u n", t=PACK, u=RUN)
        for t in range(PACK):
            nc.sync.dma_start(w2_dealt[:, t, :], dealt_rows[t])

        eps_sb = tile([P, 2, PACK], F32, "eps_sb")
        nc.scalar.copy(eps_sb[:], eps_psum[:, :, 0 : 2 * QUADRANT : QUADRANT].rearrange("p t b -> p b t"))

        cuts = [slice(0, S // 4), slice(S // 4, S - S // 4), slice(S - S // 4, S)]
        v_codes = [tile([P, S], U32, "v_codes%d" % a) for a in range(2)]
        for a in range(2):
            for frames in cuts:
                entries = slice(frames.start // PER_COLUMN, frames.stop // PER_COLUMN)
                nc.vector.tensor_copy(v_codes[a][:, frames], words[a][:].bitcast(U32).indirect(offs_sb[:, entries]))

        w4_dealt = tile([P, 2, 2 * PASS], U8, "w4_dealt")
        nc.vector.tensor_copy(
            w4_dealt[:].bitcast(I32).rearrange("p a (t g v) -> p a t g v", t=PACK, v=4),
            w4_raw[:].bitcast(I32).rearrange("p a (g t v) -> p a t g v", t=PACK, v=4),
        )
        w4_codes = {DEALT: w4_dealt, TURNED: w4_turned}

        eps_spread = tile([P, PACK, M], F32, "eps_spread")
        for pair in range(2):
            nc.scalar.copy(
                eps_spread[:, 2 * pair : 2 * pair + 2, :],
                eps_sb[:, DEALT, 2 * pair : 2 * pair + 2].unsqueeze(2).to_broadcast([P, 2, M]),
            )
        so_far = {j: eps_spread[:, j, :] for j in range(PACK)}
        warm = tile([P, 1], F32, "warm")
        nc.scalar.activation(warm[:], eps_sb[:, DEALT, 0:1], ACT.Sqrt)

        def round_on_gpsimd(name, tag, rows):
            rounded = tile([P, rows.shape[2], PACK], BF16, name, tag)
            nc.gpsimd.tensor_scalar(rounded[:], rows.rearrange("p t n -> p n t"), 1.0, 0.0, MULT, ADD)
            return rounded

        squares = [tile([P, S], F32, "squares%d" % j) for j in range(2 * PACK)]
        rounded_turned = round_on_gpsimd("rounded_turned", "w4_raw%d" % DEALT, w2_turned[:])
        h_banks = {}

        def first_product(pieces, a, place=None):
            if a == 0:
                widths = [frames.stop - frames.start for j, frames in pieces]
                held = bank([P, sum(widths)], "h%d_%d" % (pieces[0][0], pieces[0][1].start), place)
                for index, (j, frames) in enumerate(pieces):
                    h_banks[j, frames.start] = held[:, sum(widths[:index]) : sum(widths[: index + 1])]
            for index, (j, frames) in enumerate(pieces):
                one_pass(j, frames, a, a == 0 and index == 0, a == 1 and index == len(pieces) - 1)
            if a == 1:
                for j, frames in pieces:
                    square(j, frames)

        def square(j, frames):
            h = h_banks[j, frames.start]
            if (j, frames) == on_vector:
                factor = tile([P, frames.stop - frames.start], F32, "factor")
                nc.vector.tensor_copy(factor[:], h)
                nc.vector.tensor_tensor(squares[j][:, frames], h, factor[:], MULT)
            else:
                nc.scalar.activation(squares[j][:, frames], h, ACT.Square)

        def one_pass(j, frames, a, start, stop):
            b, t = divmod(j, PACK)
            nc.tensor.matmul_mx(
                out=h_banks[j, frames.start],
                lhsT=w4_codes[b][:, a, 2 * P * t : 2 * P * (t + 1)].bitcast(FP4X4),
                lhsT_scale=w4_planes[:, a, P * j : P * (j + 1)],
                rhs=v_codes[a][:, frames].bitcast(FP8X4),
                rhs_scale=v_planes[a][:, frames],
                start=start,
                stop=stop,
            )

        def both_passes(pieces, place):
            first_product(pieces, 0, place)
            first_product(pieces, 1)

        def whole_tiles(pair):
            for half in range(2):
                for j in pair:
                    both_passes([(j, slice(BANK * half, BANK * (half + 1)))], j % 2 + 2 * half)

        quarters = [slice(S // PACK * q, S // PACK * (q + 1)) for q in range(PACK)]
        early = [[(j, cuts[0])] for j in range(PACK, 2 * PACK)]
        early.extend([(4, frames)] for frames in quarters[1:])
        early.append([(5, cuts[1])])
        on_vector = (7, cuts[0])
        rest = [[(5, cuts[2]), (6, cuts[2])], [(6, cuts[1])], [(7, cuts[1])], [(7, cuts[2])]]
        for place, pieces in enumerate(early):
            first_product(pieces, 0, (place + PACK) % (2 * PACK))
        for pieces in early[0:6]:
            first_product(pieces, 1)
        first_product(rest[0], 0, PACK)
        for pieces in early[6:8] + rest[0:1]:
            first_product(pieces, 1)
        for place in range(1, len(rest)):
            both_passes(rest[place], PACK + place)

        halves = [slice(0, HALF), slice(HALF, M)]
        whole = slice(0, M)

        def entries_of(i, beats):
            return pos_sb[i][:, beats.start // PER_COLUMN : beats.stop // PER_COLUMN]

        def pick(engine, j, i, beats):
            term = tile([P, beats.stop - beats.start], F32, "term%d_%d_%d" % (j, i, beats.start))
            window = squares[j][:].indirect(entries_of(i, beats))
            if engine == "vector":
                nc.vector.tensor_copy(term[:], window)
            else:
                nc.scalar.activation(term[:], window, ACT.Copy)
            return (j, beats, term)

        by_vector = [(4, 0, whole), (4, 1, whole), (4, 2, whole), (5, 0, whole), (5, 1, slice(0, P))]
        by_scalar = [(6, 0, whole), (6, 1, whole), (6, 2, whole), (5, 2, whole)]
        by_scalar_late = [(7, 0, whole), (7, 1, whole), (7, 2, whole), (5, 1, slice(P, M))]
        terms = [pick("vector", *item) for item in by_vector]
        rounded_dealt = round_on_gpsimd("rounded_dealt", "w2_turned", w2_dealt[:])
        whole_tiles((0, 1))
        terms.extend(pick("scalar", *item) for item in by_scalar)
        whole_tiles((2, 3))
        terms.extend(pick("scalar", *item) for item in by_scalar_late)

        sums = [bank([P, PASS], "sums%d" % c, PACK + c) for c in range(M // P)]

        def add_turned(t, beats, term, first=False, closes=()):
            for c in range(beats.start // P, beats.stop // P):
                nc.tensor.matmul(
                    sums[c][:, P * t : P * (t + 1)],
                    lhsT=term[:, P * c - beats.start : P * (c + 1) - beats.start],
                    rhs=identity[:],
                    is_transpose=True,
                    start=first,
                    stop=(c in closes),
                )

        for t in range(PACK):
            add_turned(t, whole, eps_sb[:, TURNED, t : t + 1].to_broadcast([P, M]), first=(t == 0))
        for j, beats, term in terms[:-2]:
            add_turned(j - PACK, beats, term)
        for (j, beats, term), closes in zip(terms[-2:], ((0,), range(1, M // P))):
            add_turned(j - PACK, beats, term, closes=closes)

        totals = tile([P, PACK, M], F32, "totals")

        def pick_and_add(dst, j, i, beats, before):
            nc.vector.tensor_tensor(dst, squares[j][:].indirect(entries_of(i, beats)), before[:, beats], ADD)

        part_tags = (("squares4", "first_sum"), ("second_sums", "second_sum"))
        root_steps = [halves[0], slice(HALF, M - HALF // 2), slice(M - HALF // 2, M)]

        for pair, steps in (((0, 1), [whole]), ((2, 3), root_steps)):
            for i in range(LISTS - 1):
                for j in pair:
                    part = tile([P, M], F32, "part%d_%d" % (j, i), part_tags[i][j % 2])
                    pick_and_add(part[:], j, i, whole, so_far[j])
                    so_far[j] = part[:]
            for beats in steps:
                for j in pair:
                    pick_and_add(totals[:, j, beats], j, LISTS - 1, beats, so_far[j])

        backs = [bank([P, 2, HALF], "back%d" % half, half) for half in range(2)]

        def copy_back(half, tag, copy):
            z = tile([P, HALF, PACK], BF16, "z_turned%d" % half, tag)
            copy(
                z[:].rearrange("p m t -> p (m t)").bitcast(F32).rearrange("p (m u) -> p m u", u=2),
                backs[half][:].rearrange("p u m -> p m u"),
            )
            return z

        for c in range(M // P):
            half, part = divmod(c, 2)
            if c == M // P - 1:
                z_turned = copy_back(0, None, nc.scalar.copy)
            roots = tile([P, PASS], BF16, "roots%d" % c)
            nc.scalar.activation(
                roots[:].rearrange("m (u p e) -> m u p e", u=2, e=2),
                sums[c][:].rearrange("m (p u e) -> m u p e", u=2, e=2),
                ACT.Sqrt,
            )
            for u in range(2):
                nc.tensor.transpose(
                    backs[half][:, u, P * part : P * (part + 1)],
                    roots[:].bitcast(F32)[:, P * u : P * (u + 1)],
                    identity[:],
                )
        unread = bank([P, BANK], "unread", 2 * PACK - 1)
        for t in range(WARM_PASSES):
            nc.tensor.matmul_mx(
                out=unread[:],
                lhsT=w4_dealt[:, 0, 2 * P * t : 2 * P * (t + 1)].bitcast(FP4X4),
                lhsT_scale=w4_planes[:, 0, P * t : P * (t + 1)],
                rhs=v_codes[0][:, 0:BANK].bitcast(FP8X4),
                rhs_scale=v_planes[0][:, 0:BANK],
                start=True,
                stop=True,
            )
        z_dealt = [tile([P, HALF, PACK], BF16, "z_dealt%d" % half, "roots%d" % (2 * half)) for half in range(2)]
        for beats in root_steps:
            half, first = divmod(beats.start, HALF)
            nc.scalar.activation(
                z_dealt[half][:, first : beats.stop - HALF * half, :].rearrange("p (c i) t -> p c t i", i=LINE),
                totals[:, :, beats].rearrange("p t (c i) -> p c t i", i=LINE),
                ACT.Sqrt,
            )

        def quantise(name, codes, rounded):
            plane = tile([P, HALF], U8, name + "_plane")
            nc.vector.quantize_mx(out=codes.bitcast(FP8X4), scales=plane[:], in_=rounded.rearrange("p m t -> p (m t)"))
            return codes, plane[:]

        def own_codes(name, tag=None, width=HALF):
            return tile([P, width], U32, name + "_codes", tag)[:]

        w2_q = {}

        def quantise_w2(b, g, codes, rounded):
            codes, plane = quantise("w2_%d_%d" % (b, g), codes, rounded)
            for n in range(2):
                w2_q[b, 2 * g + n] = (codes[:, P * n : P * (n + 1)], plane[:, P * n : P * (n + 1)])

        y_places = ((4, 5, 6, 7), (2, 3, 0, 1))
        y_banks = {}

        def second_product(half, b, n, z_q):
            opens = b == (TURNED, DEALT)[half]
            if opens:
                y_banks[half, n] = bank([P, HALF], "y%d_%d" % (half, n), y_places[half][n])
            nc.tensor.matmul_mx(
                out=y_banks[half, n][:],
                lhsT=w2_q[b, n][0].bitcast(FP8X4),
                lhsT_scale=w2_q[b, n][1],
                rhs=z_q[0].bitcast(FP8X4),
                rhs_scale=z_q[1],
                start=opens,
                stop=not opens,
            )
            if not opens:
                result = tile([P, HALF], F32, "result%d_%d" % (half, n))
                nc.scalar.activation(result[:], y_banks[half, n][:], ACT.Silu)
                nc.sync.dma_start(out[P * n : P * (n + 1), halves[half]], result[:])

        quantise_w2(TURNED, 0, own_codes("w2_first", "roots1"), rounded_turned[:, columns[0], :])
        first_turned = quantise("z_turned0", own_codes("z_turned0"), z_turned[:])
        for n in range(2):
            second_product(0, TURNED, n, first_turned)
        quantise_w2(DEALT, 0, own_codes("w2_second", "roots3"), rounded_dealt[:, columns[0], :])
        first_dealt = quantise("z_dealt0", own_codes("z_dealt0"), z_dealt[0][:])
        for n in range(2):
            second_product(0, DEALT, n, first_dealt)
        later = own_codes("w2_later", "roots0", 2 * HALF)
        quantise_w2(TURNED, 1, later[:, 0:HALF], rounded_turned[:, columns[1], :])
        quantise_w2(DEALT, 1, later[:, HALF : 2 * HALF], rounded_dealt[:, columns[1], :])
        for n in range(2, N // P):
            second_product(0, TURNED, n, first_turned)
            second_product(0, DEALT, n, first_dealt)
        z_turned = copy_back(1, "w4_raw%d" % DEALT, nc.vector.tensor_copy)
        second_q = {DEALT: quantise("z_dealt1", own_codes("z_dealt1"), z_dealt[1][:])}
        second_q[TURNED] = quantise("z_turned1", own_codes("z_turned1"), z_turned[:])
        for b in (DEALT, TURNED):
            for n in range(N // P):
                second_product(1, b, n, second_q[b])
